import numpy as np
import ml_dtypes


def mxq(x, axis, fmt="e4m3"):
    dtype, down = {"e4m3": (ml_dtypes.float8_e4m3fn, 7), "e5m2": (ml_dtypes.float8_e5m2, 14)}[fmt]
    v = np.moveaxis(np.asarray(x, np.float32).astype(ml_dtypes.bfloat16).astype(np.float64), axis, -1)
    blocks = v.reshape(v.shape[:-1] + (-1, 32))
    amax = np.abs(blocks).max(-1, keepdims=True)
    byte = np.maximum(np.where(amax > 0, np.frexp(amax)[1] - 1 + 127, 0) - down, 1)
    scale = np.exp2(byte - 127.0)
    codes = (blocks / scale).astype(np.float32).astype(dtype).astype(np.float64)
    return np.moveaxis((codes * scale).reshape(v.shape), -1, axis)


WIDE = False


def mx_kscale(k):
    if not WIDE:
        return np.ones(k)
    levels = np.array([10, -10, 5, -5, 0])
    if k % 512:
        return np.exp2(np.random.permutation(np.resize(levels, k // 32))).repeat(32)
    a = np.empty((k // 512, 16))
    for p in range(k // 512):
        a[p, :8] = np.random.permutation(np.resize(levels, 8))
        for g in range(8):
            far = levels[np.abs(levels - a[p, g]) >= 10]
            a[p, g + 8] = far[np.random.randint(len(far))]
    return np.exp2(a.ravel()).repeat(32)


def f64(x):
    return np.asarray(x).astype(np.float64)


def striped(idx):
    return np.tile(idx.reshape(-1, 16).T, (8, 1)).astype(np.uint16)


def unstriped(offs):
    return offs[:16].T.reshape(-1).astype(np.int64)


def striped8(idx):
    return np.concatenate([x.reshape(-1, 16).T for x in idx]).astype(np.uint16)


def runs(offs, k):
    lists = np.stack([offs[16 * r : 16 * r + 16].T.reshape(-1) for r in range(8)]).astype(np.int64)
    return lists[np.arange(k) % 512 // 64]


def pack_weight(w):
    k, n = w.shape
    w = f64(np.asarray(w, np.float32).astype(ml_dtypes.bfloat16)).reshape(k // 32, 32, n)
    amax = np.abs(w).max(1)
    byte = np.clip(np.where(amax > 0, np.frexp(amax)[1] - 1 + 127 - 7, 1), 1, 254)
    scaled = (w * np.exp2(127.0 - byte)[:, None, :]).reshape(k, n).astype(np.float32)
    words = np.ascontiguousarray(scaled.reshape(k // 512, 128, 4, n).transpose(0, 1, 3, 2)).astype(ml_dtypes.float8_e4m3fn).view(np.uint8)
    return words, np.ascontiguousarray(byte.astype(np.uint8).reshape(k // 512, 16, n))


def unpack_weight(words, scales):
    g, p, n, _ = words.shape
    vals = np.ascontiguousarray(words).view(ml_dtypes.float8_e4m3fn).astype(np.float64) * np.repeat(np.exp2(scales.astype(np.float64) - 127.0), 8, axis=1)[..., None]
    return vals.transpose(0, 1, 3, 2).reshape(g * 512, n)


E2M1 = np.array([0.0, 0.5, 1.0, 1.5, 2.0, 3.0, 4.0, 6.0, -0.0, -0.5, -1.0, -1.5, -2.0, -3.0, -4.0, -6.0])


def pack_fp4(w):
    k, n = w.shape
    w = f64(np.asarray(w, np.float32).astype(ml_dtypes.bfloat16)).reshape(k // 32, 32, n)
    amax = np.abs(w).max(1)
    mant, ex = np.frexp(amax / 6.0)
    byte = np.clip(np.where(amax > 0, np.where(mant > 0.5, ex, ex - 1) + 127, 1), 1, 254)
    scaled = (w * np.exp2(127.0 - byte)[:, None, :]).reshape(k, n).astype(np.float32)
    c = np.ascontiguousarray(scaled.reshape(k // 512, 128, 4, n).transpose(0, 1, 3, 2)).astype(ml_dtypes.float4_e2m1fn).view(np.uint8) & 0xF
    words = (c[..., 0::2] | (c[..., 1::2] << 4)).reshape(k // 512, 128, 2 * n)
    return np.ascontiguousarray(words), np.ascontiguousarray(byte.astype(np.uint8).reshape(k // 512, 16, n))


def unpack_fp4(words, scales):
    g, _, n = scales.shape
    words = np.ascontiguousarray(words).reshape(g, 128, n, 2)
    nib = np.empty((g, 128, n, 4), np.uint8)
    nib[..., 0::2] = words & 0xF
    nib[..., 1::2] = words >> 4
    vals = E2M1[nib] * np.repeat(np.exp2(scales.astype(np.float64) - 127.0), 8, axis=1)[..., None]
    return vals.transpose(0, 1, 3, 2).reshape(g * 512, n)


def gelu(v):
    return 0.5 * v * (1.0 + np.tanh(np.sqrt(2.0 / np.pi) * (v + 0.044715 * v**3)))

def planes(y):
    n, m = y.shape
    v = y.astype(np.float32).astype(ml_dtypes.bfloat16).astype(np.float64).reshape(n // 32, 32, m)
    top = np.abs(v).max(1)
    byte = np.clip(np.where(top > 0, np.frexp(top)[1] - 1 + 127 - 7, 1), 1, 254)
    codes = (v * np.exp2(127.0 - byte)[:, None, :]).reshape(n, m).astype(np.float32).astype(ml_dtypes.float8_e4m3fn).view(np.uint8)
    words = codes.reshape(n // 512, 128, 4, m).transpose(0, 1, 3, 2)
    return np.ascontiguousarray(words), np.ascontiguousarray(byte.astype(np.uint8).reshape(n // 512, 16, m))


K, T, S, V, N, H = 512, 2048, 512, 512, 512, 512


def setup_inputs():
    n = np.random.standard_normal
    s = mx_kscale(K)[:, None]
    u = mx_kscale(H)
    packed_xT = pack_weight(n((K, T)) * s)
    packed_w3 = pack_fp4(n((H, N)) / np.sqrt(H) / u[:, None])
    return {
        "x_words": packed_xT[0],
        "x_scales": packed_xT[1],
        "w1": (n((K, H)) / np.sqrt(K) / s * u).astype(np.float32),
        "a1": np.repeat(np.random.uniform(0.1, 0.5, (8, V)), 64, axis=0).astype(np.float32),
        "a2": np.repeat(np.random.uniform(0.1, 0.5, (8, V)), 64, axis=0).astype(np.float32),
        "a3": np.repeat(np.random.uniform(0.1, 0.5, (8, V)), 64, axis=0).astype(np.float32),
        "a4": np.repeat(np.random.uniform(0.1, 0.5, (8, V)), 64, axis=0).astype(np.float32),
        "w2": (n((H, H)) / np.sqrt(H) / u[:, None] * u).astype(np.float32),
        "res": (2 * n((N, V))).astype(np.float32),
        "w3_words": packed_w3[0],
        "w3_scales": packed_w3[1],
        "offs": striped(np.random.permutation(T)[:S]),
        "c1": striped8(np.random.randint(0, S, (8, V))),
        "c2": striped8(np.random.randint(0, S, (8, V))),
        "c3": striped8(np.random.randint(0, S, (8, V))),
        "c4": striped8(np.random.randint(0, S, (8, V))),
    }


def reference(x_words, x_scales, w1, a1, a2, a3, a4, w2, res, w3_words, w3_scales, offs, c1, c2, c3, c4):
    xq = unpack_weight(x_words, x_scales)[:, unstriped(offs)]
    y = mxq(f64(w1), 0, "e4m3").T @ xq
    z = (y[np.arange(H)[:, None], runs(c1, H)]) * f64(a1) + (y[np.arange(H)[:, None], runs(c2, H)]) * f64(a2) + (y[np.arange(H)[:, None], runs(c3, H)]) * f64(a3) + (y[np.arange(H)[:, None], runs(c4, H)]) * f64(a4)
    h = gelu(mxq(f64(w2), 0, "e4m3").T @ mxq(z, 0, "e4m3"))
    out_0 = f64(res) + (unpack_fp4(w3_words, w3_scales).T @ mxq(h, 0, "e4m3"))
    return (out_0,) + planes(out_0)

@@ -1,0 +1,259 @@
+from contextlib import ExitStack
+
+import concourse.mybir as mybir
+from concourse.masks import make_identity
+
+F32 = mybir.dt.float32
+BF16 = mybir.dt.bfloat16
+I32 = mybir.dt.int32
+U32 = mybir.dt.uint32
+U16 = mybir.dt.uint16
+U8 = mybir.dt.uint8
+FP8X4 = mybir.dt.float8_e4m3fn_x4
+FP4X4 = mybir.dt.float4_e2m1fn_x4
+MULT = mybir.AluOpType.mult
+ADD = mybir.AluOpType.add
+GELU = mybir.ActivationFunctionType.Gelu_apprx_tanh
+
+P = 128
+PACK = 4
+D = 512
+TABLE = 2048
+BLOCK = 128
+CHUNKS = ((0, 1), (2,), (3,))
+
+FLOPS = 3 * 2 * D * D * D
+BYTES = (
+    P * TABLE * 4 + 16 * TABLE + 3 * D * D * 4 + 4 * 8 * D * 4 + P * 2 * D + 16 * D + 5 * P * 32 * 2
+    + D * D * 4 + P * D * 4 + 16 * D
+)
+
+
+def tile_picked_hgrid_gelu_po_kernel(
+    tc, x_words, x_scales, w1, a1, a2, a3, a4, w2, res, w3_words, w3_scales, offs, c1, c2, c3, c4,
+    out_0, out_1, out_2,
+):
+    nc = tc.nc
+    with ExitStack() as ctx:
+        keep = ctx.enter_context(tc.tile_pool(name="keep", bufs=1))
+        ps_sum = ctx.enter_context(tc.psum_pool(name="ps_sum", bufs=2))
+        ps_turn = ctx.enter_context(tc.psum_pool(name="ps_turn", bufs=1))
+        ps_mm = ctx.enter_context(tc.psum_pool(name="ps_mm", bufs=5))
+
+        def sb(name, shape, dtype):
+            return keep.tile(shape, dtype, name=name, align_bytes=64)
+
+        def load_scale_rows(queue, plane, rows):
+            for q in range(4):
+                queue.dma_start(
+                    out=plane[32 * q : 32 * q + 4, :].bitcast(I32),
+                    in_=rows[0, 4 * q : 4 * q + 4, :].bitcast(I32),
+                )
+
+        xs_table = sb("xs_table", [P, TABLE], U8)
+        nc.vector.memset(xs_table[:].bitcast(I32), 0)
+        load_scale_rows(nc.scalar, xs_table, x_scales)
+        w3_raw = sb("w3_raw", [P, 2 * D], U8)
+        nc.gpsimd.dma_start(out=w3_raw[:].bitcast(I32), in_=w3_words[0].bitcast(I32))
+        w3s_raw = sb("w3s_raw", [P, D], U8)
+        nc.vector.memset(w3s_raw[:].bitcast(I32), 0)
+        load_scale_rows(nc.gpsimd, w3s_raw, w3_scales)
+        picked = sb("picked", [P, D // 16], U16)
+        nc.sync.dma_start(out=picked[:], in_=offs)
+
+        w1_rows = w1.rearrange("(p j) c -> p j c", j=PACK)
+        w1_raw = []
+        for half in range(2):
+            raw = sb("w1_raw%d" % half, [P, PACK, D // 2], F32)
+            nc.sync.dma_start(out=raw[:], in_=w1_rows[:, :, half * 256 : (half + 1) * 256])
+            w1_raw.append(raw)
+        xw_table = sb("xw_table", [P, TABLE], U32)
+        nc.sync.dma_start(
+            out=xw_table[:].bitcast(I32), in_=x_words[0].rearrange("p n r -> p (n r)").bitcast(I32)
+        )
+        corners = []
+        for c, lists in enumerate((c1, c2, c3, c4)):
+            corner = sb("corner%d" % c, [P, D // 16], U16)
+            nc.sync.dma_start(out=corner[:], in_=lists)
+            corners.append(corner)
+        weights = []
+        for c, a in enumerate((a1, a2, a3, a4)):
+            weight = sb("weight%d" % c, [P, D], F32)
+            nc.sync.dma_start(out=weight[:], in_=a.rearrange("(p j) v -> p j v", j=PACK)[:, 0, :])
+            weights.append(weight)
+        w2_raw = sb("w2_raw", [P, PACK, D], F32)
+        nc.sync.dma_start(out=w2_raw[:], in_=w2.rearrange("(p j) c -> p j c", j=PACK))
+        res_sb = sb("res_sb", [P, PACK, D], F32)
+        nc.sync.dma_start(out=res_sb[:], in_=res.rearrange("(p t) v -> p t v", t=PACK))
+
+        ident = sb("ident", [P, P], F32)
+        make_identity(nc, ident[:])
+        warm_in = sb("warm_in", [P, 1], F32)
+        warm_out = sb("warm_out", [P, 1], F32)
+        nc.vector.memset(warm_in[:], 0.0)
+        nc.scalar.activation(out=warm_out[:], in_=warm_in[:], func=GELU)
+
+        w1_bf = sb("w1_bf", [P, PACK, P, PACK], BF16)
+        for half, copy in enumerate((nc.scalar.copy, nc.vector.tensor_copy)):
+            copy(
+                out=w1_bf[:, :, 64 * half : 64 * (half + 1), :].rearrange("p t m j -> p m j t"),
+                in_=w1_raw[half][:].rearrange("p j (m t) -> p m j t", t=PACK),
+            )
+        xs = sb("xs", [P, D], U8)
+        nc.vector.tensor_copy(out=xs[:], in_=xs_table[:].indirect(picked[:]))
+        w1_codes = sb("w1_codes", [P, D], U32)
+        w1_scales = sb("w1_scales", [P, D], U8)
+        nc.vector.quantize_mx(
+            out=w1_codes[:].bitcast(FP8X4), scales=w1_scales[:],
+            in_=w1_bf[:].rearrange("p t m j -> p (t m j)"),
+        )
+        xw = []
+        for half in range(2):
+            part = sb("xw%d" % half, [P, D // 2], U32)
+            nc.vector.tensor_copy(
+                out=part[:], in_=xw_table[:].indirect(picked[:, 16 * half : 16 * (half + 1)])
+            )
+            xw.append(part)
+        y = []
+        for t in range(PACK):
+            bank = ps_mm.tile([P, D], F32, name="mm")
+            for half in range(2):
+                cols = slice(256 * half, 256 * (half + 1))
+                nc.tensor.matmul_mx(
+                    out=bank[:, cols],
+                    lhsT=w1_codes[:, P * t : P * (t + 1)].bitcast(FP8X4),
+                    lhsT_scale=w1_scales[:, P * t : P * (t + 1)],
+                    rhs=xw[half][:].bitcast(FP8X4), rhs_scale=xs[:, cols],
+                    start=True, stop=True,
+                )
+            plane = sb("y%d" % t, [P, D], F32)
+            nc.scalar.copy(out=plane[:], in_=bank[:])
+            y.append(plane)
+
+        w3_codes = sb("w3_codes", [P, PACK, P, 2], U8)
+        nc.vector.tensor_copy(
+            out=w3_codes[:].rearrange("p t m b -> p m t b"),
+            in_=w3_raw[:].rearrange("p (m t b) -> p m t b", t=PACK, b=2),
+        )
+        w3_sc = sb("w3_sc", [P, PACK, P], U8)
+        nc.vector.tensor_copy(
+            out=w3_sc[:].rearrange("p t m -> p m t"),
+            in_=w3s_raw[:].rearrange("p (m t) -> p m t", t=PACK),
+        )
+        w2_bf = sb("w2_bf", [P, PACK, P, PACK], BF16)
+        nc.scalar.copy(
+            out=w2_bf[:].rearrange("p t m j -> p m j t"),
+            in_=w2_raw[:].rearrange("p j (m t) -> p m j t", t=PACK),
+        )
+        w2_codes = sb("w2_codes", [P, D], U32)
+        w2_scales = sb("w2_scales", [P, D], U8)
+        nc.vector.quantize_mx(
+            out=w2_codes[:].bitcast(FP8X4), scales=w2_scales[:],
+            in_=w2_bf[:].rearrange("p t m j -> p (t m j)"),
+        )
+
+        def quantize_block(name, grouped):
+            codes = sb(name + "_codes", [P, BLOCK], U32)
+            scales = sb(name + "_scales", [P, BLOCK], U8)
+            nc.vector.quantize_mx(
+                out=codes[:].bitcast(FP8X4), scales=scales[:],
+                in_=grouped[:].rearrange("p v t -> p (v t)"),
+            )
+            return codes, scales
+
+        products = {}
+        for chunk in CHUNKS:
+            v0, width = chunk[0] * BLOCK, len(chunk) * BLOCK
+            last = chunk == CHUNKS[-1]
+            z_turned = {b: sb("z_turned%d" % b, [P, 2, P, 2], BF16) for b in chunk}
+            sums = {}
+            for t in range(PACK):
+                for b in chunk:
+                    if t == 0 or (last and t == 2):
+                        sums[b] = ps_sum.tile([P, 2, 2, P], F32, name="sums")
+                for c in range(4):
+                    g = sb("g%d_%d_%d" % (v0, t, c), [P, width], F32)
+                    nc.vector.tensor_tensor(
+                        out=g[:],
+                        in0=y[t][:].indirect(corners[c][:, v0 // 16 : (v0 + width) // 16]),
+                        in1=weights[c][:, v0 : v0 + width], op=MULT,
+                    )
+                    for i, b in enumerate(chunk):
+                        nc.tensor.matmul(
+                            out=sums[b][:, t // 2, t % 2, :], lhsT=g[:, i * BLOCK : (i + 1) * BLOCK],
+                            rhs=ident[:], start=(c == 0), stop=(c == 3), is_transpose=True,
+                        )
+                if last and t % 2 == 1:
+                    for b in chunk:
+                        nc.scalar.copy(
+                            out=z_turned[b][:, t // 2, :, :],
+                            in_=sums[b][:, t // 2, :, :].rearrange("v e p -> v p e"),
+                        )
+            for b in chunk:
+                if not last:
+                    nc.scalar.copy(out=z_turned[b][:], in_=sums[b][:].rearrange("v u e p -> v u p e"))
+                words = z_turned[b][:].rearrange("v u p e -> v (u p e)").bitcast(F32)
+                back = ps_turn.tile([P, 2, BLOCK], F32, name="back")
+                for u in range(2):
+                    nc.tensor.transpose(back[:, u, :], words[:, P * u : P * (u + 1)], ident[:])
+                z_bf = sb("z_bf%d" % b, [P, BLOCK, PACK], BF16)
+                nc.scalar.copy(
+                    out=z_bf[:].rearrange("p v t -> p (v t)").bitcast(F32).rearrange("p (v u) -> p v u", u=2),
+                    in_=back[:].rearrange("p u v -> p v u"),
+                )
+                z_codes, z_scales = quantize_block("z%d" % b, z_bf)
+                pre = ps_mm.tile([P, PACK, BLOCK], F32, name="mm")
+                for t in range(PACK):
+                    nc.tensor.matmul_mx(
+                        out=pre[:, t, :],
+                        lhsT=w2_codes[:, P * t : P * (t + 1)].bitcast(FP8X4),
+                        lhsT_scale=w2_scales[:, P * t : P * (t + 1)],
+                        rhs=z_codes[:].bitcast(FP8X4), rhs_scale=z_scales[:],
+                        start=True, stop=True,
+                    )
+                h_bf = sb("h_bf%d" % b, [P, BLOCK, PACK], BF16)
+                nc.scalar.activation(out=h_bf[:], in_=pre[:].rearrange("p t v -> p v t"), func=GELU)
+                h_codes, h_scales = quantize_block("h%d" % b, h_bf)
+                product = ps_mm.tile([P, PACK, BLOCK], F32, name="mm")
+                for t in range(PACK):
+                    nc.tensor.matmul_mx(
+                        out=product[:, t, :],
+                        lhsT=w3_codes[:, t, :, :].rearrange("p m b -> p (m b)").bitcast(FP4X4),
+                        lhsT_scale=w3_sc[:, t, :],
+                        rhs=h_codes[:].bitcast(FP8X4), rhs_scale=h_scales[:],
+                        start=True, stop=True,
+                    )
+                products[b] = product
+
+        out_rows = out_0.rearrange("(p t) v -> p t v", t=PACK)
+        out_words = out_1[0].rearrange("p n r -> p (n r)").bitcast(I32)
+        o_codes = sb("o_codes", [P, D], U32)
+        o_scales = sb("o_scales", [P, D], U8)
+        for chunk in CHUNKS:
+            v0, width = chunk[0] * BLOCK, len(chunk) * BLOCK
+            last = chunk == CHUNKS[-1]
+            cols = slice(v0, v0 + width)
+            result = sb("result%d" % v0, [P, PACK, width], F32)
+            for i, b in enumerate(chunk):
+                nc.vector.tensor_tensor(
+                    out=result[:, :, i * BLOCK : (i + 1) * BLOCK], in0=products[b][:],
+                    in1=res_sb[:, :, b * BLOCK : (b + 1) * BLOCK], op=ADD,
+                )
+            nc.sync.dma_start(out=out_rows[:, :, cols], in_=result[:])
+            o_bf = sb("o_bf%d" % v0, [P, width, PACK], BF16)
+            copy = nc.vector.tensor_copy if last else nc.scalar.copy
+            copy(
+                out=o_bf[:].rearrange("p (c i) t -> p c t i", i=4),
+                in_=result[:].rearrange("p t (c i) -> p c t i", i=4),
+            )
+            nc.vector.quantize_mx(
+                out=o_codes[:, cols].bitcast(FP8X4), scales=o_scales[:, cols],
+                in_=o_bf[:].rearrange("p v t -> p (v t)"),
+            )
+            nc.sync.dma_start(out=out_words[:, cols], in_=o_codes[:, cols].bitcast(I32))
+        for q in range(4):
+            queue = nc.scalar if q % 2 else nc.sync
+            queue.dma_start(
+                out=out_2[0, 4 * q : 4 * q + 4, :].bitcast(I32),
+                in_=o_scales[32 * q : 32 * q + 4, :].bitcast(I32),
+            )

@@ -36,12 +36,13 @@ def tile_picked_hgrid_gelu_po_kernel(
     nc = tc.nc
     with ExitStack() as ctx:
         keep = ctx.enter_context(tc.tile_pool(name="keep", bufs=1))
+        ring = ctx.enter_context(tc.tile_pool(name="ring", bufs=6))
         ps_sum = ctx.enter_context(tc.psum_pool(name="ps_sum", bufs=2))
         ps_turn = ctx.enter_context(tc.psum_pool(name="ps_turn", bufs=1))
         ps_mm = ctx.enter_context(tc.psum_pool(name="ps_mm", bufs=5))
 
-        def sb(name, shape, dtype):
-            return keep.tile(shape, dtype, name=name, align_bytes=64)
+        def sb(name, shape, dtype, tag=None):
+            return keep.tile(shape, dtype, name=name, tag=tag or name, align_bytes=64)
 
         def load_scale_rows(queue, plane, rows):
             for q in range(4):
@@ -53,104 +54,89 @@ def tile_picked_hgrid_gelu_po_kernel(
         xs_table = sb("xs_table", [P, TABLE], U8)
         nc.vector.memset(xs_table[:].bitcast(I32), 0)
         load_scale_rows(nc.scalar, xs_table, x_scales)
-        w3_raw = sb("w3_raw", [P, 2 * D], U8)
-        nc.gpsimd.dma_start(out=w3_raw[:].bitcast(I32), in_=w3_words[0].bitcast(I32))
-        w3s_raw = sb("w3s_raw", [P, D], U8)
-        nc.vector.memset(w3s_raw[:].bitcast(I32), 0)
-        load_scale_rows(nc.gpsimd, w3s_raw, w3_scales)
         picked = sb("picked", [P, D // 16], U16)
         nc.sync.dma_start(out=picked[:], in_=offs)
-
-        w1_rows = w1.rearrange("(p j) c -> p j c", j=PACK)
-        w1_raw = []
-        for half in range(2):
-            raw = sb("w1_raw%d" % half, [P, PACK, D // 2], F32)
-            nc.sync.dma_start(out=raw[:], in_=w1_rows[:, :, half * 256 : (half + 1) * 256])
-            w1_raw.append(raw)
         xw_table = sb("xw_table", [P, TABLE], U32)
         nc.sync.dma_start(
             out=xw_table[:].bitcast(I32), in_=x_words[0].rearrange("p n r -> p (n r)").bitcast(I32)
         )
-        corners = []
-        for c, lists in enumerate((c1, c2, c3, c4)):
+        w1_rows = w1.rearrange("(p j) c -> p j c", j=PACK)
+        w1_raw = [sb("w1_raw%d" % half, [P, PACK, D // 2], F32) for half in range(2)]
+        nc.sync.dma_start(out=w1_raw[0][:], in_=w1_rows[:, :, : D // 2])
+        corners, weights = [], []
+        for c, (lists, a) in enumerate(((c1, a1), (c2, a2), (c3, a3), (c4, a4))):
             corner = sb("corner%d" % c, [P, D // 16], U16)
             nc.sync.dma_start(out=corner[:], in_=lists)
             corners.append(corner)
-        weights = []
-        for c, a in enumerate((a1, a2, a3, a4)):
+            if c == 0:
+                nc.sync.dma_start(out=w1_raw[1][:], in_=w1_rows[:, :, D // 2 :])
             weight = sb("weight%d" % c, [P, D], F32)
             nc.sync.dma_start(out=weight[:], in_=a.rearrange("(p j) v -> p j v", j=PACK)[:, 0, :])
             weights.append(weight)
         w2_raw = sb("w2_raw", [P, PACK, D], F32)
         nc.sync.dma_start(out=w2_raw[:], in_=w2.rearrange("(p j) c -> p j c", j=PACK))
+        w3_raw = sb("w3_raw", [P, 2 * D], U8)
+        nc.sync.dma_start(out=w3_raw[:].bitcast(I32), in_=w3_words[0].bitcast(I32))
+        w3s_raw = sb("w3s_raw", [P, D], U8)
+        nc.gpsimd.memset(w3s_raw[:].bitcast(I32), 0)
+        load_scale_rows(nc.sync, w3s_raw, w3_scales)
         res_sb = sb("res_sb", [P, PACK, D], F32)
         nc.sync.dma_start(out=res_sb[:], in_=res.rearrange("(p t) v -> p t v", t=PACK))
 
         ident = sb("ident", [P, P], F32)
         make_identity(nc, ident[:])
-        warm_in = sb("warm_in", [P, 1], F32)
         warm_out = sb("warm_out", [P, 1], F32)
-        nc.vector.memset(warm_in[:], 0.0)
-        nc.scalar.activation(out=warm_out[:], in_=warm_in[:], func=GELU)
+        nc.scalar.activation(out=warm_out[:], in_=ident[:, 0:1], func=GELU)
 
+        xw = sb("xw", [P, D], U32)
+        nc.vector.tensor_copy(out=xw[:], in_=xw_table[:].indirect(picked[:]))
+        xs = sb("xs", [P, D], U8)
+        nc.vector.tensor_copy(out=xs[:], in_=xs_table[:].indirect(picked[:]))
         w1_bf = sb("w1_bf", [P, PACK, P, PACK], BF16)
         for half, copy in enumerate((nc.scalar.copy, nc.vector.tensor_copy)):
             copy(
-                out=w1_bf[:, :, 64 * half : 64 * (half + 1), :].rearrange("p t m j -> p m j t"),
-                in_=w1_raw[half][:].rearrange("p j (m t) -> p m j t", t=PACK),
+                out=w1_bf[:, :, 64 * half : 64 * (half + 1), :].rearrange("p t m j -> p m t j"),
+                in_=w1_raw[half][:].rearrange("p j (m t) -> p m t j", t=PACK),
             )
-        xs = sb("xs", [P, D], U8)
-        nc.vector.tensor_copy(out=xs[:], in_=xs_table[:].indirect(picked[:]))
         w1_codes = sb("w1_codes", [P, D], U32)
         w1_scales = sb("w1_scales", [P, D], U8)
-        nc.vector.quantize_mx(
-            out=w1_codes[:].bitcast(FP8X4), scales=w1_scales[:],
-            in_=w1_bf[:].rearrange("p t m j -> p (t m j)"),
-        )
-        xw = []
-        for half in range(2):
-            part = sb("xw%d" % half, [P, D // 2], U32)
-            nc.vector.tensor_copy(
-                out=part[:], in_=xw_table[:].indirect(picked[:, 16 * half : 16 * (half + 1)])
+        for t0, t1 in ((0, 1), (1, 2), (2, 4)):
+            nc.vector.quantize_mx(
+                out=w1_codes[:, P * t0 : P * t1].bitcast(FP8X4), scales=w1_scales[:, P * t0 : P * t1],
+                in_=w1_bf[:, t0:t1, :, :].rearrange("p t m j -> p (t m j)"),
             )
-            xw.append(part)
         y = []
         for t in range(PACK):
-            bank = ps_mm.tile([P, D], F32, name="mm")
-            for half in range(2):
-                cols = slice(256 * half, 256 * (half + 1))
+            plane = sb("y%d" % t, [P, D], F32)
+            step = D // 2 if t == 0 else D
+            for n0 in range(0, D, step):
+                cols = slice(n0, n0 + step)
+                bank = ps_mm.tile([P, step], F32, name="mm")
                 nc.tensor.matmul_mx(
-                    out=bank[:, cols],
+                    out=bank[:],
                     lhsT=w1_codes[:, P * t : P * (t + 1)].bitcast(FP8X4),
                     lhsT_scale=w1_scales[:, P * t : P * (t + 1)],
-                    rhs=xw[half][:].bitcast(FP8X4), rhs_scale=xs[:, cols],
+                    rhs=xw[:, cols].bitcast(FP8X4), rhs_scale=xs[:, cols],
                     start=True, stop=True,
                 )
-            plane = sb("y%d" % t, [P, D], F32)
-            nc.scalar.copy(out=plane[:], in_=bank[:])
+                nc.scalar.copy(out=plane[:, cols], in_=bank[:])
             y.append(plane)
 
-        w3_codes = sb("w3_codes", [P, PACK, P, 2], U8)
-        nc.vector.tensor_copy(
-            out=w3_codes[:].rearrange("p t m b -> p m t b"),
-            in_=w3_raw[:].rearrange("p (m t b) -> p m t b", t=PACK, b=2),
-        )
-        w3_sc = sb("w3_sc", [P, PACK, P], U8)
-        nc.vector.tensor_copy(
-            out=w3_sc[:].rearrange("p t m -> p m t"),
-            in_=w3s_raw[:].rearrange("p (m t) -> p m t", t=PACK),
-        )
-        w2_bf = sb("w2_bf", [P, PACK, P, PACK], BF16)
-        nc.scalar.copy(
-            out=w2_bf[:].rearrange("p t m j -> p m j t"),
-            in_=w2_raw[:].rearrange("p j (m t) -> p m j t", t=PACK),
-        )
+        w2_bf = sb("w2_bf", [P, PACK, P, PACK], BF16, tag="w1_codes")
         w2_codes = sb("w2_codes", [P, D], U32)
         w2_scales = sb("w2_scales", [P, D], U8)
+        nc.scalar.copy(
+            out=w2_bf[:].rearrange("p t m j -> p m t j"),
+            in_=w2_raw[:].rearrange("p j (m t) -> p m t j", t=PACK),
+        )
         nc.vector.quantize_mx(
             out=w2_codes[:].bitcast(FP8X4), scales=w2_scales[:],
             in_=w2_bf[:].rearrange("p t m j -> p (t m j)"),
         )
+        w3_codes = sb("w3_codes", [P, PACK, P, 2], U8, tag="w2_raw")
+        w3_sc = sb("w3_sc", [P, PACK, P], U8, tag="w1_codes")
+        nc.vector.tensor_copy(out=w3_codes[:], in_=w3_raw[:].rearrange("p (m t b) -> p t m b", t=PACK, b=2))
+        nc.vector.tensor_copy(out=w3_sc[:], in_=w3s_raw[:].rearrange("p (m t) -> p t m", t=PACK))
 
         def quantize_block(name, grouped):
             codes = sb(name + "_codes", [P, BLOCK], U32)
@@ -161,38 +147,55 @@ def tile_picked_hgrid_gelu_po_kernel(
             )
             return codes, scales
 
-        products = {}
-        for chunk in CHUNKS:
-            v0, width = chunk[0] * BLOCK, len(chunk) * BLOCK
-            last = chunk == CHUNKS[-1]
-            z_turned = {b: sb("z_turned%d" % b, [P, 2, P, 2], BF16) for b in chunk}
-            sums = {}
+        def gather(out, t, c, v0, width):
+            nc.vector.tensor_tensor(
+                out=out,
+                in0=y[t][:].indirect(corners[c][:, v0 // 16 : (v0 + width) // 16]),
+                in1=weights[c][:, v0 : v0 + width], op=MULT,
+            )
+
+        def add_turned(out, g, first, final):
+            nc.tensor.matmul(out=out, lhsT=g, rhs=ident[:], start=first, stop=final, is_transpose=True)
+
+        def network(b, z_bf):
+            z_codes, z_scales = quantize_block("z%d" % b, z_bf)
+            pre = ps_mm.tile([P, PACK, BLOCK], F32, name="mm")
             for t in range(PACK):
-                for b in chunk:
-                    if t == 0 or (last and t == 2):
-                        sums[b] = ps_sum.tile([P, 2, 2, P], F32, name="sums")
+                nc.tensor.matmul_mx(
+                    out=pre[:, t, :],
+                    lhsT=w2_codes[:, P * t : P * (t + 1)].bitcast(FP8X4),
+                    lhsT_scale=w2_scales[:, P * t : P * (t + 1)],
+                    rhs=z_codes[:].bitcast(FP8X4), rhs_scale=z_scales[:],
+                    start=True, stop=True,
+                )
+            h_bf = sb("h_bf%d" % b, [P, BLOCK, PACK], BF16)
+            nc.scalar.activation(out=h_bf[:], in_=pre[:].rearrange("p t v -> p v t"), func=GELU)
+            h_codes, h_scales = quantize_block("h%d" % b, h_bf)
+            product = ps_mm.tile([P, PACK, BLOCK], F32, name="mm")
+            for t in range(PACK):
+                nc.tensor.matmul_mx(
+                    out=product[:, t, :],
+                    lhsT=w3_codes[:, t, :, :].rearrange("p m b -> p (m b)").bitcast(FP4X4),
+                    lhsT_scale=w3_sc[:, t, :],
+                    rhs=h_codes[:].bitcast(FP8X4), rhs_scale=h_scales[:],
+                    start=True, stop=True,
+                )
+            return product
+
+        products = {}
+        for chunk in CHUNKS[:-1]:
+            v0, width = chunk[0] * BLOCK, len(chunk) * BLOCK
+            sums = {b: ps_sum.tile([P, 2, 2, P], F32, name="sums") for b in chunk}
+            for t in range(PACK):
                 for c in range(4):
-                    g = sb("g%d_%d_%d" % (v0, t, c), [P, width], F32)
-                    nc.vector.tensor_tensor(
-                        out=g[:],
-                        in0=y[t][:].indirect(corners[c][:, v0 // 16 : (v0 + width) // 16]),
-                        in1=weights[c][:, v0 : v0 + width], op=MULT,
-                    )
+                    g = ring.tile([P, width], F32, name="g")
+                    gather(g[:], t, c, v0, width)
                     for i, b in enumerate(chunk):
-                        nc.tensor.matmul(
-                            out=sums[b][:, t // 2, t % 2, :], lhsT=g[:, i * BLOCK : (i + 1) * BLOCK],
-                            rhs=ident[:], start=(c == 0), stop=(c == 3), is_transpose=True,
-                        )
-                if last and t % 2 == 1:
-                    for b in chunk:
-                        nc.scalar.copy(
-                            out=z_turned[b][:, t // 2, :, :],
-                            in_=sums[b][:, t // 2, :, :].rearrange("v e p -> v p e"),
-                        )
+                        add_turned(sums[b][:, t // 2, t % 2, :], g[:, i * BLOCK : (i + 1) * BLOCK], c == 0, c == 3)
             for b in chunk:
-                if not last:
-                    nc.scalar.copy(out=z_turned[b][:], in_=sums[b][:].rearrange("v u e p -> v u p e"))
-                words = z_turned[b][:].rearrange("v u p e -> v (u p e)").bitcast(F32)
+                z_turned = sb("z_turned%d" % b, [P, 2, P, 2], BF16)
+                nc.scalar.copy(out=z_turned[:], in_=sums[b][:].rearrange("v u e p -> v u p e"))
+                words = z_turned[:].rearrange("v u p e -> v (u p e)").bitcast(F32)
                 back = ps_turn.tile([P, 2, BLOCK], F32, name="back")
                 for u in range(2):
                     nc.tensor.transpose(back[:, u, :], words[:, P * u : P * (u + 1)], ident[:])
@@ -201,51 +204,56 @@ def tile_picked_hgrid_gelu_po_kernel(
                     out=z_bf[:].rearrange("p v t -> p (v t)").bitcast(F32).rearrange("p (v u) -> p v u", u=2),
                     in_=back[:].rearrange("p u v -> p v u"),
                 )
-                z_codes, z_scales = quantize_block("z%d" % b, z_bf)
-                pre = ps_mm.tile([P, PACK, BLOCK], F32, name="mm")
-                for t in range(PACK):
-                    nc.tensor.matmul_mx(
-                        out=pre[:, t, :],
-                        lhsT=w2_codes[:, P * t : P * (t + 1)].bitcast(FP8X4),
-                        lhsT_scale=w2_scales[:, P * t : P * (t + 1)],
-                        rhs=z_codes[:].bitcast(FP8X4), rhs_scale=z_scales[:],
-                        start=True, stop=True,
-                    )
-                h_bf = sb("h_bf%d" % b, [P, BLOCK, PACK], BF16)
-                nc.scalar.activation(out=h_bf[:], in_=pre[:].rearrange("p t v -> p v t"), func=GELU)
-                h_codes, h_scales = quantize_block("h%d" % b, h_bf)
-                product = ps_mm.tile([P, PACK, BLOCK], F32, name="mm")
-                for t in range(PACK):
-                    nc.tensor.matmul_mx(
-                        out=product[:, t, :],
-                        lhsT=w3_codes[:, t, :, :].rearrange("p m b -> p (m b)").bitcast(FP4X4),
-                        lhsT_scale=w3_sc[:, t, :],
-                        rhs=h_codes[:].bitcast(FP8X4), rhs_scale=h_scales[:],
-                        start=True, stop=True,
-                    )
-                products[b] = product
+                products[b] = network(b, z_bf)
+
+        (b,) = CHUNKS[-1]
+        v0 = b * BLOCK
+        back = ps_turn.tile([P, PACK, BLOCK], F32, name="back")
+        for t in range(PACK):
+            part = ps_sum.tile([P, P], F32, name="sums")
+            for c in range(3):
+                if (t, c) == (PACK - 1, 0):
+                    g = sb("late", [P, BLOCK], F32)
+                else:
+                    g = ring.tile([P, BLOCK], F32, name="g")
+                gather(g[:], t, c, v0, BLOCK)
+                add_turned(part[:], g[:], c == 0, c == 2)
+            part_sb = sb("part%d" % t, [P, P], F32)
+            nc.scalar.copy(out=part_sb[:], in_=part[:])
+            nc.tensor.transpose(back[:, t, :], part_sb[:], ident[:])
+        fourth = sb("fourth", [P, PACK, BLOCK], F32, tag="late")
+        for t in range(PACK):
+            gather(fourth[:, t, :], t, 3, v0, BLOCK)
+        z_bf = sb("z_bf%d" % b, [P, BLOCK, PACK], BF16)
+        nc.vector.tensor_tensor(
+            out=z_bf[:], in0=back[:].rearrange("p t v -> p v t"),
+            in1=fourth[:].rearrange("p t v -> p v t"), op=ADD,
+        )
+        products[b] = network(b, z_bf)
 
         out_rows = out_0.rearrange("(p t) v -> p t v", t=PACK)
         out_words = out_1[0].rearrange("p n r -> p (n r)").bitcast(I32)
         o_codes = sb("o_codes", [P, D], U32)
         o_scales = sb("o_scales", [P, D], U8)
-        for chunk in CHUNKS:
+        for n, chunk in enumerate(CHUNKS):
             v0, width = chunk[0] * BLOCK, len(chunk) * BLOCK
             last = chunk == CHUNKS[-1]
             cols = slice(v0, v0 + width)
-            result = sb("result%d" % v0, [P, PACK, width], F32)
-            for i, b in enumerate(chunk):
+            result = sb("result%d" % v0, [P, PACK, width], F32, tag=("late", "z_bf3", None)[n])
+            o_bf = sb("o_bf%d" % v0, [P, width, PACK], BF16)
+            step = BLOCK // 2 if last else BLOCK
+            for n0 in range(0, width, step):
+                piece = slice(n0, n0 + step)
+                inside = slice(n0 % BLOCK, n0 % BLOCK + step)
                 nc.vector.tensor_tensor(
-                    out=result[:, :, i * BLOCK : (i + 1) * BLOCK], in0=products[b][:],
-                    in1=res_sb[:, :, b * BLOCK : (b + 1) * BLOCK], op=ADD,
+                    out=result[:, :, piece], in0=products[(v0 + n0) // BLOCK][:, :, inside],
+                    in1=res_sb[:, :, v0 + n0 : v0 + n0 + step], op=ADD,
+                )
+                nc.scalar.copy(
+                    out=o_bf[:, piece, :].rearrange("p (c i) t -> p c t i", i=4),
+                    in_=result[:, :, piece].rearrange("p t (c i) -> p c t i", i=4),
                 )
             nc.sync.dma_start(out=out_rows[:, :, cols], in_=result[:])
-            o_bf = sb("o_bf%d" % v0, [P, width, PACK], BF16)
-            copy = nc.vector.tensor_copy if last else nc.scalar.copy
-            copy(
-                out=o_bf[:].rearrange("p (c i) t -> p c t i", i=4),
-                in_=result[:].rearrange("p t (c i) -> p c t i", i=4),
-            )
             nc.vector.quantize_mx(
                 out=o_codes[:, cols].bitcast(FP8X4), scales=o_scales[:, cols],
                 in_=o_bf[:].rearrange("p v t -> p (v t)"),

@@ -36,7 +36,6 @@ def tile_picked_hgrid_gelu_po_kernel(
     nc = tc.nc
     with ExitStack() as ctx:
         keep = ctx.enter_context(tc.tile_pool(name="keep", bufs=1))
-        ring = ctx.enter_context(tc.tile_pool(name="ring", bufs=6))
         ps_sum = ctx.enter_context(tc.psum_pool(name="ps_sum", bufs=2))
         ps_turn = ctx.enter_context(tc.psum_pool(name="ps_turn", bufs=1))
         ps_mm = ctx.enter_context(tc.psum_pool(name="ps_mm", bufs=5))
@@ -182,16 +181,17 @@ def tile_picked_hgrid_gelu_po_kernel(
                 )
             return product
 
+        after = {(2, 2): "z_bf0", (2, 3): "z_bf1", (3, 0): "h_bf0", (3, 1): "h_bf1", (3, 2): "z_bf2"}
         products = {}
         for chunk in CHUNKS[:-1]:
             v0, width = chunk[0] * BLOCK, len(chunk) * BLOCK
             sums = {b: ps_sum.tile([P, 2, 2, P], F32, name="sums") for b in chunk}
             for t in range(PACK):
+                g = sb("g%d_%d" % (v0, t), [P, 4, width], F32, tag=after.get((chunk[0], t)))
                 for c in range(4):
-                    g = ring.tile([P, width], F32, name="g")
-                    gather(g[:], t, c, v0, width)
+                    gather(g[:, c, :], t, c, v0, width)
                     for i, b in enumerate(chunk):
-                        add_turned(sums[b][:, t // 2, t % 2, :], g[:, i * BLOCK : (i + 1) * BLOCK], c == 0, c == 3)
+                        add_turned(sums[b][:, t // 2, t % 2, :], g[:, c, i * BLOCK : (i + 1) * BLOCK], c == 0, c == 3)
             for b in chunk:
                 z_turned = sb("z_turned%d" % b, [P, 2, P, 2], BF16)
                 nc.scalar.copy(out=z_turned[:], in_=sums[b][:].rearrange("v u e p -> v u p e"))
@@ -211,17 +211,15 @@ def tile_picked_hgrid_gelu_po_kernel(
         back = ps_turn.tile([P, PACK, BLOCK], F32, name="back")
         for t in range(PACK):
             part = ps_sum.tile([P, P], F32, name="sums")
+            if t < 3:
+                g = sb("g%d_%d" % (v0, t), [P, 2, 3, BLOCK], F32, tag=after[b, t])
             for c in range(3):
-                if (t, c) == (PACK - 1, 0):
-                    g = sb("late", [P, BLOCK], F32)
-                else:
-                    g = ring.tile([P, BLOCK], F32, name="g")
-                gather(g[:], t, c, v0, BLOCK)
-                add_turned(part[:], g[:], c == 0, c == 2)
+                gather(g[:, t // 3, c, :], t, c, v0, BLOCK)
+                add_turned(part[:], g[:, t // 3, c, :], c == 0, c == 2)
             part_sb = sb("part%d" % t, [P, P], F32)
             nc.scalar.copy(out=part_sb[:], in_=part[:])
             nc.tensor.transpose(back[:, t, :], part_sb[:], ident[:])
-        fourth = sb("fourth", [P, PACK, BLOCK], F32, tag="late")
+        fourth = sb("fourth", [P, PACK, BLOCK], F32, tag="h_bf2")
         for t in range(PACK):
             gather(fourth[:, t, :], t, 3, v0, BLOCK)
         z_bf = sb("z_bf%d" % b, [P, BLOCK, PACK], BF16)
@@ -239,7 +237,7 @@ def tile_picked_hgrid_gelu_po_kernel(
             v0, width = chunk[0] * BLOCK, len(chunk) * BLOCK
             last = chunk == CHUNKS[-1]
             cols = slice(v0, v0 + width)
-            result = sb("result%d" % v0, [P, PACK, width], F32, tag=("late", "z_bf3", None)[n])
+            result = sb("result%d" % v0, [P, PACK, width], F32, tag=("h_bf2", "z_bf3", None)[n])
             o_bf = sb("o_bf%d" % v0, [P, width, PACK], BF16)
             step = BLOCK // 2 if last else BLOCK
             for n0 in range(0, width, step):

@@ -18,14 +18,23 @@ GELU = mybir.ActivationFunctionType.Gelu_apprx_tanh
 P = 128
 PACK = 4
 D = 512
+HALF = D // 2
 TABLE = 2048
+GROUP = 16
+CORNERS = 4
+LEVELS = 8
 BLOCK = 128
-CHUNKS = ((0, 1), (2,), (3,))
+EARLY_CHUNKS = ((0, 1), (2,))
+LAST_BLOCK = 3
 
 FLOPS = 3 * 2 * D * D * D
 BYTES = (
-    P * TABLE * 4 + 16 * TABLE + 3 * D * D * 4 + 4 * 8 * D * 4 + P * 2 * D + 16 * D + 5 * P * 32 * 2
-    + D * D * 4 + P * D * 4 + 16 * D
+    P * TABLE * PACK + 16 * TABLE
+    + 3 * D * D * 4
+    + CORNERS * LEVELS * D * 4
+    + P * 2 * D + 16 * D
+    + 5 * P * (D // GROUP) * 2
+    + D * D * 4 + P * D * PACK + 16 * D
 )
 
 
@@ -37,11 +46,11 @@ def tile_picked_hgrid_gelu_po_kernel(
     with ExitStack() as ctx:
         keep = ctx.enter_context(tc.tile_pool(name="keep", bufs=1))
         ps_sum = ctx.enter_context(tc.psum_pool(name="ps_sum", bufs=2))
-        ps_turn = ctx.enter_context(tc.psum_pool(name="ps_turn", bufs=1))
+        ps_back = ctx.enter_context(tc.psum_pool(name="ps_back", bufs=1))
         ps_mm = ctx.enter_context(tc.psum_pool(name="ps_mm", bufs=5))
 
-        def sb(name, shape, dtype, tag=None):
-            return keep.tile(shape, dtype, name=name, tag=tag or name, align_bytes=64)
+        def sb(name, shape, dtype, reuses=None):
+            return keep.tile(shape, dtype, name=name, tag=reuses or name, align_bytes=64)
 
         def load_scale_rows(queue, plane, rows):
             for q in range(4):
@@ -50,32 +59,47 @@ def tile_picked_hgrid_gelu_po_kernel(
                     in_=rows[0, 4 * q : 4 * q + 4, :].bitcast(I32),
                 )
 
+        def round_and_deal(copy, grouped, raw):
+            copy(
+                out=grouped.rearrange("p t m j -> p m t j"),
+                in_=raw.rearrange("p j (m t) -> p m t j", t=PACK),
+            )
+
+        def product_planes(bank, codes, scales, rhs_codes, rhs_scales):
+            for t in range(PACK):
+                nc.tensor.matmul_mx(
+                    out=bank[:, t, :], lhsT=codes(t), lhsT_scale=scales(t),
+                    rhs=rhs_codes[:].bitcast(FP8X4), rhs_scale=rhs_scales[:], start=True, stop=True,
+                )
+
         xs_table = sb("xs_table", [P, TABLE], U8)
         nc.vector.memset(xs_table[:].bitcast(I32), 0)
         load_scale_rows(nc.scalar, xs_table, x_scales)
-        picked = sb("picked", [P, D // 16], U16)
+        picked = sb("picked", [P, D // GROUP], U16)
         nc.sync.dma_start(out=picked[:], in_=offs)
         xw_table = sb("xw_table", [P, TABLE], U32)
         nc.sync.dma_start(
             out=xw_table[:].bitcast(I32), in_=x_words[0].rearrange("p n r -> p (n r)").bitcast(I32)
         )
         w1_rows = w1.rearrange("(p j) c -> p j c", j=PACK)
-        w1_raw = [sb("w1_raw%d" % half, [P, PACK, D // 2], F32) for half in range(2)]
-        nc.sync.dma_start(out=w1_raw[0][:], in_=w1_rows[:, :, : D // 2])
-        corners, weights = [], []
-        for c, (lists, a) in enumerate(((c1, a1), (c2, a2), (c3, a3), (c4, a4))):
-            corner = sb("corner%d" % c, [P, D // 16], U16)
-            nc.sync.dma_start(out=corner[:], in_=lists)
-            corners.append(corner)
-            if c == 0:
-                nc.sync.dma_start(out=w1_raw[1][:], in_=w1_rows[:, :, D // 2 :])
-            weight = sb("weight%d" % c, [P, D], F32)
-            nc.sync.dma_start(out=weight[:], in_=a.rearrange("(p j) v -> p j v", j=PACK)[:, 0, :])
-            weights.append(weight)
+        w1_raw = [sb("w1_raw%d" % half, [P, PACK, HALF], F32) for half in range(2)]
+        w3_raw = sb("w3_raw", [P, 2 * D], U8)
+        lists = [sb("list%d" % c, [P, D // GROUP], U16) for c in range(CORNERS)]
+        weights = [sb("weight%d" % c, [P, D], F32) for c in range(CORNERS)]
+
+        def load_weight(c, a):
+            nc.sync.dma_start(out=weights[c][:], in_=a.rearrange("(p j) v -> p j v", j=PACK)[:, 0, :])
+
+        nc.sync.dma_start(out=w1_raw[0][:], in_=w1_rows[:, :, :HALF])
+        nc.sync.dma_start(out=lists[0][:], in_=c1)
+        nc.sync.dma_start(out=w1_raw[1][:], in_=w1_rows[:, :, HALF:])
+        nc.sync.dma_start(out=w3_raw[:].bitcast(I32), in_=w3_words[0].bitcast(I32))
+        load_weight(0, a1)
+        for c, (entries, a) in enumerate(((c2, a2), (c3, a3), (c4, a4)), 1):
+            nc.sync.dma_start(out=lists[c][:], in_=entries)
+            load_weight(c, a)
         w2_raw = sb("w2_raw", [P, PACK, D], F32)
         nc.sync.dma_start(out=w2_raw[:], in_=w2.rearrange("(p j) c -> p j c", j=PACK))
-        w3_raw = sb("w3_raw", [P, 2 * D], U8)
-        nc.sync.dma_start(out=w3_raw[:].bitcast(I32), in_=w3_words[0].bitcast(I32))
         w3s_raw = sb("w3s_raw", [P, D], U8)
         nc.gpsimd.memset(w3s_raw[:].bitcast(I32), 0)
         load_scale_rows(nc.sync, w3s_raw, w3_scales)
@@ -93,13 +117,10 @@ def tile_picked_hgrid_gelu_po_kernel(
         nc.vector.tensor_copy(out=xs[:], in_=xs_table[:].indirect(picked[:]))
         w1_bf = sb("w1_bf", [P, PACK, P, PACK], BF16)
         for half, copy in enumerate((nc.scalar.copy, nc.vector.tensor_copy)):
-            copy(
-                out=w1_bf[:, :, 64 * half : 64 * (half + 1), :].rearrange("p t m j -> p m t j"),
-                in_=w1_raw[half][:].rearrange("p j (m t) -> p m t j", t=PACK),
-            )
+            round_and_deal(copy, w1_bf[:, :, P // 2 * half : P // 2 * (half + 1), :], w1_raw[half][:])
         w1_codes = sb("w1_codes", [P, D], U32)
         w1_scales = sb("w1_scales", [P, D], U8)
-        for t0, t1 in ((0, 1), (1, 2), (2, 4)):
+        for t0, t1 in ((0, 1), (1, 2), (2, PACK)):
             nc.vector.quantize_mx(
                 out=w1_codes[:, P * t0 : P * t1].bitcast(FP8X4), scales=w1_scales[:, P * t0 : P * t1],
                 in_=w1_bf[:, t0:t1, :, :].rearrange("p t m j -> p (t m j)"),
@@ -107,7 +128,7 @@ def tile_picked_hgrid_gelu_po_kernel(
         y = []
         for t in range(PACK):
             plane = sb("y%d" % t, [P, D], F32)
-            step = D // 2 if t == 0 else D
+            step = HALF if t == 0 else D
             for n0 in range(0, D, step):
                 cols = slice(n0, n0 + step)
                 bank = ps_mm.tile([P, step], F32, name="mm")
@@ -121,21 +142,48 @@ def tile_picked_hgrid_gelu_po_kernel(
                 nc.scalar.copy(out=plane[:, cols], in_=bank[:])
             y.append(plane)
 
-        w2_bf = sb("w2_bf", [P, PACK, P, PACK], BF16, tag="w1_codes")
-        w2_codes = sb("w2_codes", [P, D], U32)
-        w2_scales = sb("w2_scales", [P, D], U8)
-        nc.scalar.copy(
-            out=w2_bf[:].rearrange("p t m j -> p m t j"),
-            in_=w2_raw[:].rearrange("p j (m t) -> p m t j", t=PACK),
-        )
-        nc.vector.quantize_mx(
-            out=w2_codes[:].bitcast(FP8X4), scales=w2_scales[:],
-            in_=w2_bf[:].rearrange("p t m j -> p (t m j)"),
-        )
-        w3_codes = sb("w3_codes", [P, PACK, P, 2], U8, tag="w2_raw")
-        w3_sc = sb("w3_sc", [P, PACK, P], U8, tag="w1_codes")
+        w3_codes = sb("w3_codes", [P, PACK, P, 2], U8, reuses="w1_bf")
         nc.vector.tensor_copy(out=w3_codes[:], in_=w3_raw[:].rearrange("p (m t b) -> p t m b", t=PACK, b=2))
-        nc.vector.tensor_copy(out=w3_sc[:], in_=w3s_raw[:].rearrange("p (m t) -> p t m", t=PACK))
+        w2_bf = sb("w2_bf", [P, PACK, P, PACK], BF16, reuses="w1_codes")
+        round_and_deal(nc.scalar.copy, w2_bf[:], w2_raw[:])
+
+        def gather(out, t, c, v0, width):
+            nc.vector.tensor_tensor(
+                out=out,
+                in0=y[t][:].indirect(lists[c][:, v0 // GROUP : (v0 + width) // GROUP]),
+                in1=weights[c][:, v0 : v0 + width], op=MULT,
+            )
+
+        def add_turned(out, values, first, final):
+            nc.tensor.matmul(out=out, lhsT=values, rhs=ident[:], start=first, stop=final, is_transpose=True)
+
+        def gather_chunk(chunk, reuses):
+            v0, width = chunk[0] * BLOCK, len(chunk) * BLOCK
+            sums = [ps_sum.tile([P, 2, 2, P], F32, name="sums") for b in chunk]
+            for t in range(PACK):
+                terms = sb("terms%d_%d" % (chunk[0], t), [P, CORNERS, width], F32, reuses=reuses[t])
+                for c in range(CORNERS):
+                    gather(terms[:, c, :], t, c, v0, width)
+                    for i, bank in enumerate(sums):
+                        add_turned(
+                            bank[:, t // 2, t % 2, :], terms[:, c, i * BLOCK : (i + 1) * BLOCK],
+                            c == 0, c == CORNERS - 1,
+                        )
+            return sums
+
+        def turn_back(b, bank):
+            z_turned = sb("z_turned%d" % b, [P, 2, P, 2], BF16)
+            nc.scalar.copy(out=z_turned[:], in_=bank[:].rearrange("v u e p -> v u p e"))
+            pairs = z_turned[:].rearrange("v u p e -> v (u p e)").bitcast(F32)
+            back = ps_back.tile([P, 2, BLOCK], F32, name="back")
+            for u in range(2):
+                nc.tensor.transpose(back[:, u, :], pairs[:, P * u : P * (u + 1)], ident[:])
+            z_bf = sb("z_bf%d" % b, [P, BLOCK, PACK], BF16)
+            nc.scalar.copy(
+                out=z_bf[:].rearrange("p v t -> p (v t)").bitcast(F32).rearrange("p (v u) -> p v u", u=2),
+                in_=back[:].rearrange("p u v -> p v u"),
+            )
+            return z_bf
 
         def quantize_block(name, grouped):
             codes = sb(name + "_codes", [P, BLOCK], U32)
@@ -146,105 +194,78 @@ def tile_picked_hgrid_gelu_po_kernel(
             )
             return codes, scales
 
-        def gather(out, t, c, v0, width):
-            nc.vector.tensor_tensor(
-                out=out,
-                in0=y[t][:].indirect(corners[c][:, v0 // 16 : (v0 + width) // 16]),
-                in1=weights[c][:, v0 : v0 + width], op=MULT,
-            )
-
-        def add_turned(out, g, first, final):
-            nc.tensor.matmul(out=out, lhsT=g, rhs=ident[:], start=first, stop=final, is_transpose=True)
-
         def network(b, z_bf):
             z_codes, z_scales = quantize_block("z%d" % b, z_bf)
             pre = ps_mm.tile([P, PACK, BLOCK], F32, name="mm")
-            for t in range(PACK):
-                nc.tensor.matmul_mx(
-                    out=pre[:, t, :],
-                    lhsT=w2_codes[:, P * t : P * (t + 1)].bitcast(FP8X4),
-                    lhsT_scale=w2_scales[:, P * t : P * (t + 1)],
-                    rhs=z_codes[:].bitcast(FP8X4), rhs_scale=z_scales[:],
-                    start=True, stop=True,
-                )
+            product_planes(
+                pre, lambda t: w2_codes[:, P * t : P * (t + 1)].bitcast(FP8X4),
+                lambda t: w2_scales[:, P * t : P * (t + 1)], z_codes, z_scales,
+            )
             h_bf = sb("h_bf%d" % b, [P, BLOCK, PACK], BF16)
             nc.scalar.activation(out=h_bf[:], in_=pre[:].rearrange("p t v -> p v t"), func=GELU)
             h_codes, h_scales = quantize_block("h%d" % b, h_bf)
             product = ps_mm.tile([P, PACK, BLOCK], F32, name="mm")
-            for t in range(PACK):
-                nc.tensor.matmul_mx(
-                    out=product[:, t, :],
-                    lhsT=w3_codes[:, t, :, :].rearrange("p m b -> p (m b)").bitcast(FP4X4),
-                    lhsT_scale=w3_sc[:, t, :],
-                    rhs=h_codes[:].bitcast(FP8X4), rhs_scale=h_scales[:],
-                    start=True, stop=True,
-                )
+            product_planes(
+                product, lambda t: w3_codes[:, t, :, :].rearrange("p m b -> p (m b)").bitcast(FP4X4),
+                lambda t: w3_sc[:, t, :], h_codes, h_scales,
+            )
             return product
 
-        after = {(2, 2): "z_bf0", (2, 3): "z_bf1", (3, 0): "h_bf0", (3, 1): "h_bf1", (3, 2): "z_bf2"}
-        products = {}
-        for chunk in CHUNKS[:-1]:
-            v0, width = chunk[0] * BLOCK, len(chunk) * BLOCK
-            sums = {b: ps_sum.tile([P, 2, 2, P], F32, name="sums") for b in chunk}
-            for t in range(PACK):
-                g = sb("g%d_%d" % (v0, t), [P, 4, width], F32, tag=after.get((chunk[0], t)))
-                for c in range(4):
-                    gather(g[:, c, :], t, c, v0, width)
-                    for i, b in enumerate(chunk):
-                        add_turned(sums[b][:, t // 2, t % 2, :], g[:, c, i * BLOCK : (i + 1) * BLOCK], c == 0, c == 3)
-            for b in chunk:
-                z_turned = sb("z_turned%d" % b, [P, 2, P, 2], BF16)
-                nc.scalar.copy(out=z_turned[:], in_=sums[b][:].rearrange("v u e p -> v u p e"))
-                words = z_turned[:].rearrange("v u p e -> v (u p e)").bitcast(F32)
-                back = ps_turn.tile([P, 2, BLOCK], F32, name="back")
-                for u in range(2):
-                    nc.tensor.transpose(back[:, u, :], words[:, P * u : P * (u + 1)], ident[:])
-                z_bf = sb("z_bf%d" % b, [P, BLOCK, PACK], BF16)
-                nc.scalar.copy(
-                    out=z_bf[:].rearrange("p v t -> p (v t)").bitcast(F32).rearrange("p (v u) -> p v u", u=2),
-                    in_=back[:].rearrange("p u v -> p v u"),
-                )
-                products[b] = network(b, z_bf)
+        first_sums = gather_chunk(EARLY_CHUNKS[0], (None,) * PACK)
+        w2_codes = sb("w2_codes", [P, D], U32, reuses="terms0_2")
+        w2_scales = sb("w2_scales", [P, D], U8)
+        nc.vector.quantize_mx(
+            out=w2_codes[:].bitcast(FP8X4), scales=w2_scales[:],
+            in_=w2_bf[:].rearrange("p t m j -> p (t m j)"),
+        )
+        w3_sc = sb("w3_sc", [P, PACK, P], U8, reuses="w1_codes")
+        nc.vector.tensor_copy(out=w3_sc[:], in_=w3s_raw[:].rearrange("p (m t) -> p t m", t=PACK))
+        products = [network(b, turn_back(b, bank)) for b, bank in zip(EARLY_CHUNKS[0], first_sums)]
 
-        (b,) = CHUNKS[-1]
-        v0 = b * BLOCK
-        back = ps_turn.tile([P, PACK, BLOCK], F32, name="back")
+        (bank,) = gather_chunk(EARLY_CHUNKS[1], (None, None, "z_bf0", "z_bf1"))
+        products.append(network(2, turn_back(2, bank)))
+
+        v0 = LAST_BLOCK * BLOCK
+        three = CORNERS - 1
+        back = ps_back.tile([P, PACK, BLOCK], F32, name="back")
+        plane0_terms = sb("plane0_terms", [P, three, BLOCK], F32, reuses="h_bf0")
+        plane1_terms = sb("plane1_terms", [P, three, BLOCK], F32, reuses="h_bf1")
+        plane23_terms = sb("plane23_terms", [P, 2 * three, BLOCK], F32, reuses="z_bf2")
+        last_terms = (plane0_terms[:], plane1_terms[:], plane23_terms[:, :three, :], plane23_terms[:, three:, :])
         for t in range(PACK):
             part = ps_sum.tile([P, P], F32, name="sums")
-            if t < 3:
-                g = sb("g%d_%d" % (v0, t), [P, 2, 3, BLOCK], F32, tag=after[b, t])
-            for c in range(3):
-                gather(g[:, t // 3, c, :], t, c, v0, BLOCK)
-                add_turned(part[:], g[:, t // 3, c, :], c == 0, c == 2)
+            for c in range(three):
+                gather(last_terms[t][:, c, :], t, c, v0, BLOCK)
+                add_turned(part[:], last_terms[t][:, c, :], c == 0, c == three - 1)
             part_sb = sb("part%d" % t, [P, P], F32)
             nc.scalar.copy(out=part_sb[:], in_=part[:])
             nc.tensor.transpose(back[:, t, :], part_sb[:], ident[:])
-        fourth = sb("fourth", [P, PACK, BLOCK], F32, tag="h_bf2")
+        fourth = sb("fourth", [P, PACK, BLOCK], F32, reuses="h_bf2")
         for t in range(PACK):
-            gather(fourth[:, t, :], t, 3, v0, BLOCK)
-        z_bf = sb("z_bf%d" % b, [P, BLOCK, PACK], BF16)
+            gather(fourth[:, t, :], t, three, v0, BLOCK)
+        z_last = sb("z_bf3", [P, BLOCK, PACK], BF16)
         nc.vector.tensor_tensor(
-            out=z_bf[:], in0=back[:].rearrange("p t v -> p v t"),
+            out=z_last[:], in0=back[:].rearrange("p t v -> p v t"),
             in1=fourth[:].rearrange("p t v -> p v t"), op=ADD,
         )
-        products[b] = network(b, z_bf)
+        products.append(network(LAST_BLOCK, z_last))
 
         out_rows = out_0.rearrange("(p t) v -> p t v", t=PACK)
         out_words = out_1[0].rearrange("p n r -> p (n r)").bitcast(I32)
         o_codes = sb("o_codes", [P, D], U32)
         o_scales = sb("o_scales", [P, D], U8)
-        for n, chunk in enumerate(CHUNKS):
+        for chunk, reuses, step in (
+            (EARLY_CHUNKS[0], "h_bf2", BLOCK), (EARLY_CHUNKS[1], "z_bf3", BLOCK), ((LAST_BLOCK,), None, BLOCK // 2)
+        ):
             v0, width = chunk[0] * BLOCK, len(chunk) * BLOCK
-            last = chunk == CHUNKS[-1]
             cols = slice(v0, v0 + width)
-            result = sb("result%d" % v0, [P, PACK, width], F32, tag=("h_bf2", "z_bf3", None)[n])
-            o_bf = sb("o_bf%d" % v0, [P, width, PACK], BF16)
-            step = BLOCK // 2 if last else BLOCK
+            result = sb("result%d" % chunk[0], [P, PACK, width], F32, reuses=reuses)
+            o_bf = sb("o_bf%d" % chunk[0], [P, width, PACK], BF16)
             for n0 in range(0, width, step):
                 piece = slice(n0, n0 + step)
-                inside = slice(n0 % BLOCK, n0 % BLOCK + step)
+                in_bank = slice(n0 % BLOCK, n0 % BLOCK + step)
                 nc.vector.tensor_tensor(
-                    out=result[:, :, piece], in0=products[(v0 + n0) // BLOCK][:, :, inside],
+                    out=result[:, :, piece], in0=products[(v0 + n0) // BLOCK][:, :, in_bank],
                     in1=res_sb[:, :, v0 + n0 : v0 + n0 + step], op=ADD,
                 )
                 nc.scalar.copy(

@@ -24,7 +24,7 @@ GROUP = 16
 CORNERS = 4
 LEVELS = 8
 BLOCK = 128
-EARLY_CHUNKS = ((0, 1), (2,))
+EARLY_BLOCKS = (0, 1, 2)
 LAST_BLOCK = 3
 
 FLOPS = 3 * 2 * D * D * D
@@ -45,9 +45,9 @@ def tile_picked_hgrid_gelu_po_kernel(
     nc = tc.nc
     with ExitStack() as ctx:
         keep = ctx.enter_context(tc.tile_pool(name="keep", bufs=1))
-        ps_sum = ctx.enter_context(tc.psum_pool(name="ps_sum", bufs=2))
+        ps_sum = ctx.enter_context(tc.psum_pool(name="ps_sum", bufs=3))
         ps_back = ctx.enter_context(tc.psum_pool(name="ps_back", bufs=1))
-        ps_mm = ctx.enter_context(tc.psum_pool(name="ps_mm", bufs=5))
+        ps_mm = ctx.enter_context(tc.psum_pool(name="ps_mm", bufs=4))
 
         def sb(name, shape, dtype, reuses=None):
             return keep.tile(shape, dtype, name=name, tag=reuses or name, align_bytes=64)
@@ -157,20 +157,6 @@ def tile_picked_hgrid_gelu_po_kernel(
         def add_turned(out, values, first, final):
             nc.tensor.matmul(out=out, lhsT=values, rhs=ident[:], start=first, stop=final, is_transpose=True)
 
-        def gather_chunk(chunk, reuses):
-            v0, width = chunk[0] * BLOCK, len(chunk) * BLOCK
-            sums = [ps_sum.tile([P, 2, 2, P], F32, name="sums") for b in chunk]
-            for t in range(PACK):
-                terms = sb("terms%d_%d" % (chunk[0], t), [P, CORNERS, width], F32, reuses=reuses[t])
-                for c in range(CORNERS):
-                    gather(terms[:, c, :], t, c, v0, width)
-                    for i, bank in enumerate(sums):
-                        add_turned(
-                            bank[:, t // 2, t % 2, :], terms[:, c, i * BLOCK : (i + 1) * BLOCK],
-                            c == 0, c == CORNERS - 1,
-                        )
-            return sums
-
         def turn_back(b, bank):
             z_turned = sb("z_turned%d" % b, [P, 2, P, 2], BF16)
             nc.scalar.copy(out=z_turned[:], in_=bank[:].rearrange("v u e p -> v u p e"))
@@ -211,8 +197,17 @@ def tile_picked_hgrid_gelu_po_kernel(
             )
             return product
 
-        first_sums = gather_chunk(EARLY_CHUNKS[0], (None,) * PACK)
-        w2_codes = sb("w2_codes", [P, D], U32, reuses="terms0_2")
+        sums = [ps_sum.tile([P, 2, 2, P], F32, name="sums") for b in EARLY_BLOCKS]
+        for t in range(PACK):
+            terms = sb("terms%d" % t, [P, CORNERS, LAST_BLOCK * BLOCK], F32)
+            for c in range(CORNERS):
+                gather(terms[:, c, :], t, c, 0, LAST_BLOCK * BLOCK)
+                for b in EARLY_BLOCKS:
+                    add_turned(
+                        sums[b][:, t // 2, t % 2, :], terms[:, c, b * BLOCK : (b + 1) * BLOCK],
+                        c == 0, c == CORNERS - 1,
+                    )
+        w2_codes = sb("w2_codes", [P, D], U32, reuses="terms2")
         w2_scales = sb("w2_scales", [P, D], U8)
         nc.vector.quantize_mx(
             out=w2_codes[:].bitcast(FP8X4), scales=w2_scales[:],
@@ -220,18 +215,15 @@ def tile_picked_hgrid_gelu_po_kernel(
         )
         w3_sc = sb("w3_sc", [P, PACK, P], U8, reuses="w1_codes")
         nc.vector.tensor_copy(out=w3_sc[:], in_=w3s_raw[:].rearrange("p (m t) -> p t m", t=PACK))
-        products = [network(b, turn_back(b, bank)) for b, bank in zip(EARLY_CHUNKS[0], first_sums)]
-
-        (bank,) = gather_chunk(EARLY_CHUNKS[1], (None, None, "z_bf0", "z_bf1"))
-        products.append(network(2, turn_back(2, bank)))
+        products = [network(b, turn_back(b, sums[b])) for b in EARLY_BLOCKS]
 
         v0 = LAST_BLOCK * BLOCK
         three = CORNERS - 1
         back = ps_back.tile([P, PACK, BLOCK], F32, name="back")
-        plane0_terms = sb("plane0_terms", [P, three, BLOCK], F32, reuses="h_bf0")
-        plane1_terms = sb("plane1_terms", [P, three, BLOCK], F32, reuses="h_bf1")
-        plane23_terms = sb("plane23_terms", [P, 2 * three, BLOCK], F32, reuses="z_bf2")
-        last_terms = (plane0_terms[:], plane1_terms[:], plane23_terms[:, :three, :], plane23_terms[:, three:, :])
+        last_terms = [
+            sb("last_terms%d" % t, [P, three, BLOCK], F32, reuses=reuses)
+            for t, reuses in enumerate((None, None, "z_bf0", "z_bf1"))
+        ]
         for t in range(PACK):
             part = ps_sum.tile([P, P], F32, name="sums")
             for c in range(three):
@@ -240,7 +232,7 @@ def tile_picked_hgrid_gelu_po_kernel(
             part_sb = sb("part%d" % t, [P, P], F32)
             nc.scalar.copy(out=part_sb[:], in_=part[:])
             nc.tensor.transpose(back[:, t, :], part_sb[:], ident[:])
-        fourth = sb("fourth", [P, PACK, BLOCK], F32, reuses="h_bf2")
+        fourth = sb("fourth", [P, PACK, BLOCK], F32, reuses="z_bf2")
         for t in range(PACK):
             gather(fourth[:, t, :], t, three, v0, BLOCK)
         z_last = sb("z_bf3", [P, BLOCK, PACK], BF16)
@@ -255,7 +247,7 @@ def tile_picked_hgrid_gelu_po_kernel(
         o_codes = sb("o_codes", [P, D], U32)
         o_scales = sb("o_scales", [P, D], U8)
         for chunk, reuses, step in (
-            (EARLY_CHUNKS[0], "h_bf2", BLOCK), (EARLY_CHUNKS[1], "z_bf3", BLOCK), ((LAST_BLOCK,), None, BLOCK // 2)
+            ((0, 1), "z_bf2", BLOCK), ((2,), "z_bf3", BLOCK), ((LAST_BLOCK,), None, BLOCK // 2)
         ):
             v0, width = chunk[0] * BLOCK, len(chunk) * BLOCK
             cols = slice(v0, v0 + width)

@@ -24,8 +24,9 @@ GROUP = 16
 CORNERS = 4
 LEVELS = 8
 BLOCK = 128
-EARLY_BLOCKS = (0, 1, 2)
-LAST_BLOCK = 3
+BLOCKS = D // BLOCK
+LAST_BLOCK = BLOCKS - 1
+W1_SPLIT = 48
 
 FLOPS = 3 * 2 * D * D * D
 BYTES = (
@@ -45,9 +46,10 @@ def tile_picked_hgrid_gelu_po_kernel(
     nc = tc.nc
     with ExitStack() as ctx:
         keep = ctx.enter_context(tc.tile_pool(name="keep", bufs=1))
-        ps_sum = ctx.enter_context(tc.psum_pool(name="ps_sum", bufs=3))
-        ps_back = ctx.enter_context(tc.psum_pool(name="ps_back", bufs=1))
-        ps_mm = ctx.enter_context(tc.psum_pool(name="ps_mm", bufs=4))
+        psum = ctx.enter_context(tc.psum_pool(name="psum", bufs=1))
+
+        def bank_tile(number, shape):
+            return psum.tile(shape, F32, name="bank%d" % number)
 
         def sb(name, shape, dtype, reuses=None):
             return keep.tile(shape, dtype, name=name, tag=reuses or name, align_bytes=64)
@@ -73,103 +75,89 @@ def tile_picked_hgrid_gelu_po_kernel(
                 )
 
         xs_table = sb("xs_table", [P, TABLE], U8)
-        nc.vector.memset(xs_table[:].bitcast(I32), 0)
-        load_scale_rows(nc.scalar, xs_table, x_scales)
+        nc.gpsimd.memset(xs_table[:].bitcast(I32), 0)
+        warm_in = sb("warm_in", [P, 1], F32)
+        nc.gpsimd.memset(warm_in[:], 0.0)
+        w3s_raw = sb("w3s_raw", [P, D], U8)
+        nc.gpsimd.memset(w3s_raw[:].bitcast(I32), 0)
         picked = sb("picked", [P, D // GROUP], U16)
         nc.sync.dma_start(out=picked[:], in_=offs)
+        w1_raw = sb("w1_raw", [P, PACK, D], F32)
+        nc.sync.dma_start(out=w1_raw[:], in_=w1.rearrange("(p j) c -> p j c", j=PACK))
+        load_scale_rows(nc.sync, xs_table, x_scales)
         xw_table = sb("xw_table", [P, TABLE], U32)
         nc.sync.dma_start(
             out=xw_table[:].bitcast(I32), in_=x_words[0].rearrange("p n r -> p (n r)").bitcast(I32)
         )
-        w1_rows = w1.rearrange("(p j) c -> p j c", j=PACK)
-        w1_raw = [sb("w1_raw%d" % half, [P, PACK, HALF], F32) for half in range(2)]
         w3_raw = sb("w3_raw", [P, 2 * D], U8)
         lists = [sb("list%d" % c, [P, D // GROUP], U16) for c in range(CORNERS)]
         weights = [sb("weight%d" % c, [P, D], F32) for c in range(CORNERS)]
 
-        def load_weight(c, a):
+        def load_corner(c, entries, a):
+            nc.sync.dma_start(out=lists[c][:], in_=entries)
             nc.sync.dma_start(out=weights[c][:], in_=a.rearrange("(p j) v -> p j v", j=PACK)[:, 0, :])
 
-        nc.sync.dma_start(out=w1_raw[0][:], in_=w1_rows[:, :, :HALF])
-        nc.sync.dma_start(out=lists[0][:], in_=c1)
-        nc.sync.dma_start(out=w1_raw[1][:], in_=w1_rows[:, :, HALF:])
         nc.sync.dma_start(out=w3_raw[:].bitcast(I32), in_=w3_words[0].bitcast(I32))
-        load_weight(0, a1)
+        load_corner(0, c1, a1)
+        load_scale_rows(nc.sync, w3s_raw, w3_scales)
         for c, (entries, a) in enumerate(((c2, a2), (c3, a3), (c4, a4)), 1):
-            nc.sync.dma_start(out=lists[c][:], in_=entries)
-            load_weight(c, a)
+            load_corner(c, entries, a)
         w2_raw = sb("w2_raw", [P, PACK, D], F32)
         nc.sync.dma_start(out=w2_raw[:], in_=w2.rearrange("(p j) c -> p j c", j=PACK))
-        w3s_raw = sb("w3s_raw", [P, D], U8)
-        nc.gpsimd.memset(w3s_raw[:].bitcast(I32), 0)
-        load_scale_rows(nc.sync, w3s_raw, w3_scales)
         res_sb = sb("res_sb", [P, PACK, D], F32)
         nc.sync.dma_start(out=res_sb[:], in_=res.rearrange("(p t) v -> p t v", t=PACK))
+
+        y = [sb("y%d" % t, [P, 2 * D], F32) for t in range(PACK)]
+        for plane in y:
+            nc.vector.memset(plane[:, D:], 0.0)
 
         ident = sb("ident", [P, P], F32)
         make_identity(nc, ident[:])
         warm_out = sb("warm_out", [P, 1], F32)
-        nc.scalar.activation(out=warm_out[:], in_=ident[:, 0:1], func=GELU)
+        nc.scalar.activation(out=warm_out[:], in_=warm_in[:], func=GELU)
 
-        xw = sb("xw", [P, D], U32)
-        nc.vector.tensor_copy(out=xw[:], in_=xw_table[:].indirect(picked[:]))
         xs = sb("xs", [P, D], U8)
         nc.vector.tensor_copy(out=xs[:], in_=xs_table[:].indirect(picked[:]))
         w1_bf = sb("w1_bf", [P, PACK, P, PACK], BF16)
-        for half, copy in enumerate((nc.scalar.copy, nc.vector.tensor_copy)):
-            round_and_deal(copy, w1_bf[:, :, P // 2 * half : P // 2 * (half + 1), :], w1_raw[half][:])
-        w1_codes = sb("w1_codes", [P, D], U32)
+        for m0, m1, copy in ((0, W1_SPLIT, nc.scalar.copy), (W1_SPLIT, P, nc.vector.tensor_copy)):
+            round_and_deal(copy, w1_bf[:, :, m0:m1, :], w1_raw[:, :, PACK * m0 : PACK * m1])
+        w1_codes = sb("w1_codes", [P, D], U32, reuses="xs_table")
         w1_scales = sb("w1_scales", [P, D], U8)
-        for t0, t1 in ((0, 1), (1, 2), (2, PACK)):
-            nc.vector.quantize_mx(
-                out=w1_codes[:, P * t0 : P * t1].bitcast(FP8X4), scales=w1_scales[:, P * t0 : P * t1],
-                in_=w1_bf[:, t0:t1, :, :].rearrange("p t m j -> p (t m j)"),
+        nc.vector.quantize_mx(
+            out=w1_codes[:].bitcast(FP8X4), scales=w1_scales[:],
+            in_=w1_bf[:].rearrange("p t m j -> p (t m j)"),
+        )
+        xw = sb("xw", [P, D], U32, reuses="w1_bf")
+        for n0 in range(0, D, HALF):
+            nc.vector.tensor_copy(
+                out=xw[:, n0 : n0 + HALF],
+                in_=xw_table[:].indirect(picked[:, n0 // GROUP : (n0 + HALF) // GROUP]),
             )
-        y = []
-        for t in range(PACK):
-            plane = sb("y%d" % t, [P, D], F32)
-            step = HALF if t == 0 else D
-            for n0 in range(0, D, step):
-                cols = slice(n0, n0 + step)
-                bank = ps_mm.tile([P, step], F32, name="mm")
-                nc.tensor.matmul_mx(
-                    out=bank[:],
-                    lhsT=w1_codes[:, P * t : P * (t + 1)].bitcast(FP8X4),
-                    lhsT_scale=w1_scales[:, P * t : P * (t + 1)],
-                    rhs=xw[:, cols].bitcast(FP8X4), rhs_scale=xs[:, cols],
-                    start=True, stop=True,
-                )
-                nc.scalar.copy(out=plane[:, cols], in_=bank[:])
-            y.append(plane)
+        pieces = [(0, 0, HALF), (0, HALF, HALF)] + [(t, 0, D) for t in range(1, PACK)]
+        for number, (t, n0, step) in enumerate(pieces):
+            cols = slice(n0, n0 + step)
+            bank = bank_tile(number, [P, step])
+            nc.tensor.matmul_mx(
+                out=bank[:],
+                lhsT=w1_codes[:, P * t : P * (t + 1)].bitcast(FP8X4),
+                lhsT_scale=w1_scales[:, P * t : P * (t + 1)],
+                rhs=xw[:, cols].bitcast(FP8X4), rhs_scale=xs[:, cols],
+                start=True, stop=True,
+            )
+            nc.scalar.copy(out=y[t][:, cols], in_=bank[:])
 
-        w3_codes = sb("w3_codes", [P, PACK, P, 2], U8, reuses="w1_bf")
+        w3_codes = sb("w3_codes", [P, PACK, P, 2], U8, reuses="xw_table")
         nc.vector.tensor_copy(out=w3_codes[:], in_=w3_raw[:].rearrange("p (m t b) -> p t m b", t=PACK, b=2))
-        w2_bf = sb("w2_bf", [P, PACK, P, PACK], BF16, reuses="w1_codes")
+        w3_sc = sb("w3_sc", [P, PACK, P], U8, reuses="w3_raw")
+        nc.vector.tensor_copy(out=w3_sc[:], in_=w3s_raw[:].rearrange("p (m t) -> p t m", t=PACK))
+        w2_bf = sb("w2_bf", [P, PACK, P, PACK], BF16, reuses="xs_table")
         round_and_deal(nc.scalar.copy, w2_bf[:], w2_raw[:])
 
-        def gather(out, t, c, v0, width):
-            nc.vector.tensor_tensor(
-                out=out,
-                in0=y[t][:].indirect(lists[c][:, v0 // GROUP : (v0 + width) // GROUP]),
-                in1=weights[c][:, v0 : v0 + width], op=MULT,
-            )
+        def gather(out, t, c):
+            nc.vector.tensor_tensor(out=out, in0=y[t][:].indirect(lists[c][:]), in1=weights[c][:], op=MULT)
 
         def add_turned(out, values, first, final):
             nc.tensor.matmul(out=out, lhsT=values, rhs=ident[:], start=first, stop=final, is_transpose=True)
-
-        def turn_back(b, bank):
-            z_turned = sb("z_turned%d" % b, [P, 2, P, 2], BF16)
-            nc.scalar.copy(out=z_turned[:], in_=bank[:].rearrange("v u e p -> v u p e"))
-            pairs = z_turned[:].rearrange("v u p e -> v (u p e)").bitcast(F32)
-            back = ps_back.tile([P, 2, BLOCK], F32, name="back")
-            for u in range(2):
-                nc.tensor.transpose(back[:, u, :], pairs[:, P * u : P * (u + 1)], ident[:])
-            z_bf = sb("z_bf%d" % b, [P, BLOCK, PACK], BF16)
-            nc.scalar.copy(
-                out=z_bf[:].rearrange("p v t -> p (v t)").bitcast(F32).rearrange("p (v u) -> p v u", u=2),
-                in_=back[:].rearrange("p u v -> p v u"),
-            )
-            return z_bf
 
         def quantize_block(name, grouped):
             codes = sb(name + "_codes", [P, BLOCK], U32)
@@ -180,74 +168,62 @@ def tile_picked_hgrid_gelu_po_kernel(
             )
             return codes, scales
 
-        def network(b, z_bf):
+        three = CORNERS - 1
+        backs = [bank_tile(BLOCKS + b, [P, PACK, BLOCK]) for b in range(BLOCKS)]
+        for t in range(PACK):
+            terms = sb("terms%d" % t, [P, three, D], F32)
+            for c in range(three):
+                gather(terms[:, c, :], t, c)
+            sums = bank_tile(t, [P, BLOCKS, P])
+            for b in range(BLOCKS):
+                for c in range(three):
+                    add_turned(sums[:, b, :], terms[:, c, b * BLOCK : (b + 1) * BLOCK], c == 0, c == three - 1)
+            sums_sb = sb("sums%d" % t, [P, BLOCKS, P], F32)
+            nc.scalar.copy(out=sums_sb[:], in_=sums[:])
+            for b in range(BLOCKS):
+                nc.tensor.transpose(backs[b][:, t, :], sums_sb[:, b, :], ident[:])
+        w2_codes = sb("w2_codes", [P, D], U32)
+        w2_scales = sb("w2_scales", [P, D], U8)
+        nc.vector.quantize_mx(
+            out=w2_codes[:].bitcast(FP8X4), scales=w2_scales[:],
+            in_=w2_bf[:].rearrange("p t m j -> p (t m j)"),
+        )
+        fourth = sb("fourth", [P, PACK, D], F32)
+        for t in range(PACK):
+            gather(fourth[:, t, :], t, three)
+        hidden = []
+        for b in range(BLOCKS):
+            z_bf = sb("z_bf%d" % b, [P, BLOCK, PACK], BF16)
+            nc.vector.tensor_tensor(
+                out=z_bf[:].rearrange("p (c i) t -> p c t i", i=2),
+                in0=backs[b][:].rearrange("p t (c i) -> p c t i", i=2),
+                in1=fourth[:, :, b * BLOCK : (b + 1) * BLOCK].rearrange("p t (c i) -> p c t i", i=2), op=ADD,
+            )
             z_codes, z_scales = quantize_block("z%d" % b, z_bf)
-            pre = ps_mm.tile([P, PACK, BLOCK], F32, name="mm")
+            pre = bank_tile(b, [P, PACK, BLOCK])
             product_planes(
                 pre, lambda t: w2_codes[:, P * t : P * (t + 1)].bitcast(FP8X4),
                 lambda t: w2_scales[:, P * t : P * (t + 1)], z_codes, z_scales,
             )
             h_bf = sb("h_bf%d" % b, [P, BLOCK, PACK], BF16)
             nc.scalar.activation(out=h_bf[:], in_=pre[:].rearrange("p t v -> p v t"), func=GELU)
-            h_codes, h_scales = quantize_block("h%d" % b, h_bf)
-            product = ps_mm.tile([P, PACK, BLOCK], F32, name="mm")
+            hidden.append(h_bf)
+        products = []
+        for b in range(BLOCKS):
+            h_codes, h_scales = quantize_block("h%d" % b, hidden[b])
+            product = bank_tile(BLOCKS + b, [P, PACK, BLOCK])
             product_planes(
                 product, lambda t: w3_codes[:, t, :, :].rearrange("p m b -> p (m b)").bitcast(FP4X4),
                 lambda t: w3_sc[:, t, :], h_codes, h_scales,
             )
-            return product
-
-        sums = [ps_sum.tile([P, 2, 2, P], F32, name="sums") for b in EARLY_BLOCKS]
-        for t in range(PACK):
-            terms = sb("terms%d" % t, [P, CORNERS, LAST_BLOCK * BLOCK], F32)
-            for c in range(CORNERS):
-                gather(terms[:, c, :], t, c, 0, LAST_BLOCK * BLOCK)
-                for b in EARLY_BLOCKS:
-                    add_turned(
-                        sums[b][:, t // 2, t % 2, :], terms[:, c, b * BLOCK : (b + 1) * BLOCK],
-                        c == 0, c == CORNERS - 1,
-                    )
-        w2_codes = sb("w2_codes", [P, D], U32, reuses="terms2")
-        w2_scales = sb("w2_scales", [P, D], U8)
-        nc.vector.quantize_mx(
-            out=w2_codes[:].bitcast(FP8X4), scales=w2_scales[:],
-            in_=w2_bf[:].rearrange("p t m j -> p (t m j)"),
-        )
-        w3_sc = sb("w3_sc", [P, PACK, P], U8, reuses="w1_codes")
-        nc.vector.tensor_copy(out=w3_sc[:], in_=w3s_raw[:].rearrange("p (m t) -> p t m", t=PACK))
-        products = [network(b, turn_back(b, sums[b])) for b in EARLY_BLOCKS]
-
-        v0 = LAST_BLOCK * BLOCK
-        three = CORNERS - 1
-        back = ps_back.tile([P, PACK, BLOCK], F32, name="back")
-        last_terms = [
-            sb("last_terms%d" % t, [P, three, BLOCK], F32, reuses=reuses)
-            for t, reuses in enumerate((None, None, "z_bf0", "z_bf1"))
-        ]
-        for t in range(PACK):
-            part = ps_sum.tile([P, P], F32, name="sums")
-            for c in range(three):
-                gather(last_terms[t][:, c, :], t, c, v0, BLOCK)
-                add_turned(part[:], last_terms[t][:, c, :], c == 0, c == three - 1)
-            part_sb = sb("part%d" % t, [P, P], F32)
-            nc.scalar.copy(out=part_sb[:], in_=part[:])
-            nc.tensor.transpose(back[:, t, :], part_sb[:], ident[:])
-        fourth = sb("fourth", [P, PACK, BLOCK], F32, reuses="z_bf2")
-        for t in range(PACK):
-            gather(fourth[:, t, :], t, three, v0, BLOCK)
-        z_last = sb("z_bf3", [P, BLOCK, PACK], BF16)
-        nc.vector.tensor_tensor(
-            out=z_last[:], in0=back[:].rearrange("p t v -> p v t"),
-            in1=fourth[:].rearrange("p t v -> p v t"), op=ADD,
-        )
-        products.append(network(LAST_BLOCK, z_last))
+            products.append(product)
 
         out_rows = out_0.rearrange("(p t) v -> p t v", t=PACK)
         out_words = out_1[0].rearrange("p n r -> p (n r)").bitcast(I32)
         o_codes = sb("o_codes", [P, D], U32)
         o_scales = sb("o_scales", [P, D], U8)
         for chunk, reuses, step in (
-            ((0, 1), "z_bf2", BLOCK), ((2,), "z_bf3", BLOCK), ((LAST_BLOCK,), None, BLOCK // 2)
+            ((0, 1), None, BLOCK), ((2,), None, BLOCK), ((LAST_BLOCK,), None, BLOCK // 2)
         ):
             v0, width = chunk[0] * BLOCK, len(chunk) * BLOCK
             cols = slice(v0, v0 + width)

@@ -26,6 +26,10 @@ LEVELS = 8
 BLOCK = 128
 BLOCKS = D // BLOCK
 LAST_BLOCK = BLOCKS - 1
+EARLY_BLOCKS = (0, 1)
+LATE_BLOCKS = (2, 3)
+RING = 3
+OUT_SPLIT = 48
 W1_SPLIT = 48
 
 FLOPS = 3 * 2 * D * D * D
@@ -67,10 +71,10 @@ def tile_picked_hgrid_gelu_po_kernel(
                 in_=raw.rearrange("p j (m t) -> p m t j", t=PACK),
             )
 
-        def product_planes(bank, codes, scales, rhs_codes, rhs_scales):
+        def product_planes(planes, codes, scales, rhs_codes, rhs_scales):
             for t in range(PACK):
                 nc.tensor.matmul_mx(
-                    out=bank[:, t, :], lhsT=codes(t), lhsT_scale=scales(t),
+                    out=planes[t], lhsT=codes(t), lhsT_scale=scales(t),
                     rhs=rhs_codes[:].bitcast(FP8X4), rhs_scale=rhs_scales[:], start=True, stop=True,
                 )
 
@@ -136,7 +140,7 @@ def tile_picked_hgrid_gelu_po_kernel(
         pieces = [(0, 0, HALF), (0, HALF, HALF)] + [(t, 0, D) for t in range(1, PACK)]
         for number, (t, n0, step) in enumerate(pieces):
             cols = slice(n0, n0 + step)
-            bank = bank_tile(number, [P, step])
+            bank = bank_tile(BLOCKS + number % BLOCKS, [P, step])
             nc.tensor.matmul_mx(
                 out=bank[:],
                 lhsT=w1_codes[:, P * t : P * (t + 1)].bitcast(FP8X4),
@@ -146,15 +150,21 @@ def tile_picked_hgrid_gelu_po_kernel(
             )
             nc.scalar.copy(out=y[t][:, cols], in_=bank[:])
 
-        w3_codes = sb("w3_codes", [P, PACK, P, 2], U8, reuses="xw_table")
-        nc.vector.tensor_copy(out=w3_codes[:], in_=w3_raw[:].rearrange("p (m t b) -> p t m b", t=PACK, b=2))
+        w3_codes = sb("w3_codes", [P, PACK, 2 * P], U8, reuses="xw_table")
+        nc.vector.tensor_copy(
+            out=w3_codes[:].bitcast(U16), in_=w3_raw[:].bitcast(U16).rearrange("p (m t) -> p t m", t=PACK)
+        )
         w3_sc = sb("w3_sc", [P, PACK, P], U8, reuses="w3_raw")
         nc.vector.tensor_copy(out=w3_sc[:], in_=w3s_raw[:].rearrange("p (m t) -> p t m", t=PACK))
         w2_bf = sb("w2_bf", [P, PACK, P, PACK], BF16, reuses="xs_table")
         round_and_deal(nc.scalar.copy, w2_bf[:], w2_raw[:])
 
-        def gather(out, t, c):
-            nc.vector.tensor_tensor(out=out, in0=y[t][:].indirect(lists[c][:]), in1=weights[c][:], op=MULT)
+        def gather(out, t, c, v0=0, width=D):
+            nc.vector.tensor_tensor(
+                out=out,
+                in0=y[t][:].indirect(lists[c][:, v0 // GROUP : (v0 + width) // GROUP]),
+                in1=weights[c][:, v0 : v0 + width], op=MULT,
+            )
 
         def add_turned(out, values, first, final):
             nc.tensor.matmul(out=out, lhsT=values, rhs=ident[:], start=first, stop=final, is_transpose=True)
@@ -164,87 +174,137 @@ def tile_picked_hgrid_gelu_po_kernel(
             scales = sb(name + "_scales", [P, BLOCK], U8)
             nc.vector.quantize_mx(
                 out=codes[:].bitcast(FP8X4), scales=scales[:],
-                in_=grouped[:].rearrange("p v t -> p (v t)"),
+                in_=grouped,
             )
             return codes, scales
 
         three = CORNERS - 1
-        backs = [bank_tile(BLOCKS + b, [P, PACK, BLOCK]) for b in range(BLOCKS)]
+        backs = [
+            bank_tile(BLOCKS + b, [P, 2 if b in EARLY_BLOCKS else PACK, BLOCK]) for b in range(BLOCKS)
+        ]
+        sums = {}
         for t in range(PACK):
-            terms = sb("terms%d" % t, [P, three, D], F32)
-            for c in range(three):
-                gather(terms[:, c, :], t, c)
-            sums = bank_tile(t, [P, BLOCKS, P])
+            u, e = divmod(t, 2)
             for b in range(BLOCKS):
-                for c in range(three):
-                    add_turned(sums[:, b, :], terms[:, c, b * BLOCK : (b + 1) * BLOCK], c == 0, c == three - 1)
-            sums_sb = sb("sums%d" % t, [P, BLOCKS, P], F32)
-            nc.scalar.copy(out=sums_sb[:], in_=sums[:])
-            for b in range(BLOCKS):
-                nc.tensor.transpose(backs[b][:, t, :], sums_sb[:, b, :], ident[:])
-        w2_codes = sb("w2_codes", [P, D], U32)
+                if b in LATE_BLOCKS:
+                    sums[b] = bank_tile(b, [P, P])
+                elif e == 0:
+                    sums[b] = bank_tile(b, [P, 2, P])
+            for c in range(CORNERS):
+                blocks = EARLY_BLOCKS if c == three else range(BLOCKS)
+                terms = sb(
+                    "terms%d_%d" % (t, c), [P, len(blocks) * BLOCK], F32,
+                    reuses="ring%d" % ((CORNERS * t + c) % RING),
+                )
+                gather(terms[:], t, c, 0, len(blocks) * BLOCK)
+                for b in blocks:
+                    early = b in EARLY_BLOCKS
+                    add_turned(
+                        sums[b][:, e, :] if early else sums[b][:], terms[:, b * BLOCK : (b + 1) * BLOCK],
+                        c == 0, c == (three if early else three - 1),
+                    )
+            for b in EARLY_BLOCKS if e == 1 else ():
+                pairs = sb("pairs%d_%d" % (b, u), [P, P, 2], BF16)
+                nc.scalar.copy(out=pairs[:], in_=sums[b][:].rearrange("v e p -> v p e"))
+                nc.tensor.transpose(
+                    backs[b][:, u, :], pairs[:].rearrange("v p e -> v (p e)").bitcast(F32), ident[:]
+                )
+            for b in LATE_BLOCKS:
+                part = sb("part%d_%d" % (b, t), [P, P], F32)
+                nc.scalar.copy(out=part[:], in_=sums[b][:])
+                nc.tensor.transpose(backs[b][:, t, :], part[:], ident[:])
+        w2_codes = sb("w2_codes", [P, D], U32, reuses="ring%d" % ((CORNERS * PACK - 1) % RING))
         w2_scales = sb("w2_scales", [P, D], U8)
         nc.vector.quantize_mx(
             out=w2_codes[:].bitcast(FP8X4), scales=w2_scales[:],
             in_=w2_bf[:].rearrange("p t m j -> p (t m j)"),
         )
-        fourth = sb("fourth", [P, PACK, D], F32)
-        for t in range(PACK):
-            gather(fourth[:, t, :], t, three)
-        hidden = []
-        for b in range(BLOCKS):
-            z_bf = sb("z_bf%d" % b, [P, BLOCK, PACK], BF16)
-            nc.vector.tensor_tensor(
-                out=z_bf[:].rearrange("p (c i) t -> p c t i", i=2),
-                in0=backs[b][:].rearrange("p t (c i) -> p c t i", i=2),
-                in1=fourth[:, :, b * BLOCK : (b + 1) * BLOCK].rearrange("p t (c i) -> p c t i", i=2), op=ADD,
-            )
+
+        def first_layer(b, z_bf):
             z_codes, z_scales = quantize_block("z%d" % b, z_bf)
             pre = bank_tile(b, [P, PACK, BLOCK])
             product_planes(
-                pre, lambda t: w2_codes[:, P * t : P * (t + 1)].bitcast(FP8X4),
+                [pre[:, t, :] for t in range(PACK)], lambda t: w2_codes[:, P * t : P * (t + 1)].bitcast(FP8X4),
                 lambda t: w2_scales[:, P * t : P * (t + 1)], z_codes, z_scales,
             )
             h_bf = sb("h_bf%d" % b, [P, BLOCK, PACK], BF16)
             nc.scalar.activation(out=h_bf[:], in_=pre[:].rearrange("p t v -> p v t"), func=GELU)
-            hidden.append(h_bf)
+            return h_bf
+
+        def interleave_pairs(words, b):
+            nc.scalar.copy(
+                out=words.rearrange("p (v u) -> p v u", u=2), in_=backs[b][:].rearrange("p u v -> p v u")
+            )
+
+        fourth = sb("fourth", [P, PACK * HALF], F32, reuses="ring%d" % ((CORNERS * PACK - 3) % RING))
+        last_plane = fourth[:, (PACK - 1) * HALF :]
+        for t in range(PACK - 1):
+            gather(fourth[:, t * HALF : (t + 1) * HALF], t, three, HALF, HALF)
+        interleave_pairs(last_plane, 0)
+        hidden = [first_layer(0, last_plane.bitcast(BF16))]
+        gather(last_plane, PACK - 1, three, HALF, HALF)
+        z_bf = sb("z_bf1", [P, BLOCK * PACK], BF16)
+        interleave_pairs(z_bf[:].bitcast(F32), 1)
+        hidden.append(first_layer(1, z_bf[:]))
+        for late, b in enumerate(LATE_BLOCKS):
+            z_bf = sb("z_bf%d" % b, [P, BLOCK * PACK], BF16, reuses=None if late else "z_bf1")
+            planes = fourth[:].rearrange("p (t v) -> p t v", t=PACK)[:, :, late * BLOCK : (late + 1) * BLOCK]
+            nc.vector.tensor_tensor(
+                out=z_bf[:].rearrange("p (c i t) -> p c t i", i=2, t=PACK),
+                in0=backs[b][:].rearrange("p t (c i) -> p c t i", i=2),
+                in1=planes.rearrange("p t (c i) -> p c t i", i=2), op=ADD,
+            )
+            hidden.append(first_layer(b, z_bf[:]))
         products = []
         for b in range(BLOCKS):
-            h_codes, h_scales = quantize_block("h%d" % b, hidden[b])
-            product = bank_tile(BLOCKS + b, [P, PACK, BLOCK])
+            h_codes, h_scales = quantize_block("h%d" % b, hidden[b][:].rearrange("p v t -> p (v t)"))
+            numbers = (0, BLOCKS + b) if b == LAST_BLOCK else (BLOCKS + b,)
+            share = PACK // len(numbers)
+            banks = [bank_tile(number, [P, share, BLOCK]) for number in numbers]
             product_planes(
-                product, lambda t: w3_codes[:, t, :, :].rearrange("p m b -> p (m b)").bitcast(FP4X4),
-                lambda t: w3_sc[:, t, :], h_codes, h_scales,
+                [banks[t // share][:, t % share, :] for t in range(PACK)],
+                lambda t: w3_codes[:, t, :].bitcast(FP4X4), lambda t: w3_sc[:, t, :], h_codes, h_scales,
             )
-            products.append(product)
+            products.append(banks)
 
         out_rows = out_0.rearrange("(p t) v -> p t v", t=PACK)
         out_words = out_1[0].rearrange("p n r -> p (n r)").bitcast(I32)
         o_codes = sb("o_codes", [P, D], U32)
         o_scales = sb("o_scales", [P, D], U8)
-        for chunk, reuses, step in (
-            ((0, 1), None, BLOCK), ((2,), None, BLOCK), ((LAST_BLOCK,), None, BLOCK // 2)
-        ):
+
+        def round_and_interleave(copy, o_bf, result, piece):
+            copy(
+                out=o_bf[:, piece, :].rearrange("p (c i) t -> p c t i", i=4),
+                in_=result[:, :, piece].rearrange("p t (c i) -> p c t i", i=4),
+            )
+
+        for chunk in (EARLY_BLOCKS, (2,), (LAST_BLOCK,)):
             v0, width = chunk[0] * BLOCK, len(chunk) * BLOCK
             cols = slice(v0, v0 + width)
-            result = sb("result%d" % chunk[0], [P, PACK, width], F32, reuses=reuses)
+            result = sb("result%d" % chunk[0], [P, PACK, width], F32)
             o_bf = sb("o_bf%d" % chunk[0], [P, width, PACK], BF16)
-            for n0 in range(0, width, step):
-                piece = slice(n0, n0 + step)
-                in_bank = slice(n0 % BLOCK, n0 % BLOCK + step)
-                nc.vector.tensor_tensor(
-                    out=result[:, :, piece], in0=products[(v0 + n0) // BLOCK][:, :, in_bank],
-                    in1=res_sb[:, :, v0 + n0 : v0 + n0 + step], op=ADD,
-                )
-                nc.scalar.copy(
-                    out=o_bf[:, piece, :].rearrange("p (c i) t -> p c t i", i=4),
-                    in_=result[:, :, piece].rearrange("p t (c i) -> p c t i", i=4),
-                )
+            if chunk[0] == LAST_BLOCK:
+                for u, bank in enumerate(products[LAST_BLOCK]):
+                    pair = slice(2 * u, 2 * u + 2)
+                    nc.vector.tensor_tensor(
+                        out=result[:, pair, :], in0=bank[:], in1=res_sb[:, pair, cols], op=ADD
+                    )
+                round_and_interleave(nc.scalar.copy, o_bf, result, slice(0, OUT_SPLIT))
+                round_and_interleave(nc.vector.tensor_copy, o_bf, result, slice(OUT_SPLIT, BLOCK))
+            else:
+                for n, b in enumerate(chunk):
+                    piece = slice(n * BLOCK, (n + 1) * BLOCK)
+                    nc.vector.tensor_tensor(
+                        out=result[:, :, piece], in0=products[b][0][:],
+                        in1=res_sb[:, :, b * BLOCK : (b + 1) * BLOCK], op=ADD,
+                    )
+                    round_and_interleave(nc.scalar.copy, o_bf, result, piece)
             nc.sync.dma_start(out=out_rows[:, :, cols], in_=result[:])
             nc.vector.quantize_mx(
                 out=o_codes[:, cols].bitcast(FP8X4), scales=o_scales[:, cols],
                 in_=o_bf[:].rearrange("p v t -> p (v t)"),
             )
+        for cols in (slice(0, LAST_BLOCK * BLOCK), slice(LAST_BLOCK * BLOCK, D)):
             nc.sync.dma_start(out=out_words[:, cols], in_=o_codes[:, cols].bitcast(I32))
         for q in range(4):
             queue = nc.scalar if q % 2 else nc.sync

@@ -30,7 +30,7 @@ EARLY_BLOCKS = (0, 1)
 LATE_BLOCKS = (2, 3)
 RING = 3
 OUT_SPLIT = 48
-W1_SPLIT = 48
+W1_SPLIT = 80
 
 FLOPS = 3 * 2 * D * D * D
 BYTES = (
@@ -93,7 +93,7 @@ def tile_picked_hgrid_gelu_po_kernel(
         nc.sync.dma_start(
             out=xw_table[:].bitcast(I32), in_=x_words[0].rearrange("p n r -> p (n r)").bitcast(I32)
         )
-        w3_raw = sb("w3_raw", [P, 2 * D], U8)
+        w3_raw = sb("w3_raw", [P, 2 * D], U8, reuses="ring0")
         lists = [sb("list%d" % c, [P, D // GROUP], U16) for c in range(CORNERS)]
         weights = [sb("weight%d" % c, [P, D], F32) for c in range(CORNERS)]
 
@@ -102,10 +102,9 @@ def tile_picked_hgrid_gelu_po_kernel(
             nc.sync.dma_start(out=weights[c][:], in_=a.rearrange("(p j) v -> p j v", j=PACK)[:, 0, :])
 
         nc.sync.dma_start(out=w3_raw[:].bitcast(I32), in_=w3_words[0].bitcast(I32))
-        load_corner(0, c1, a1)
-        load_scale_rows(nc.sync, w3s_raw, w3_scales)
-        for c, (entries, a) in enumerate(((c2, a2), (c3, a3), (c4, a4)), 1):
+        for c, (entries, a) in enumerate(((c1, a1), (c2, a2), (c3, a3), (c4, a4))):
             load_corner(c, entries, a)
+        load_scale_rows(nc.sync, w3s_raw, w3_scales)
         w2_raw = sb("w2_raw", [P, PACK, D], F32)
         nc.sync.dma_start(out=w2_raw[:], in_=w2.rearrange("(p j) c -> p j c", j=PACK))
         res_sb = sb("res_sb", [P, PACK, D], F32)
@@ -125,39 +124,41 @@ def tile_picked_hgrid_gelu_po_kernel(
         w1_bf = sb("w1_bf", [P, PACK, P, PACK], BF16)
         for m0, m1, copy in ((0, W1_SPLIT, nc.scalar.copy), (W1_SPLIT, P, nc.vector.tensor_copy)):
             round_and_deal(copy, w1_bf[:, :, m0:m1, :], w1_raw[:, :, PACK * m0 : PACK * m1])
-        w1_codes = sb("w1_codes", [P, D], U32, reuses="xs_table")
-        w1_scales = sb("w1_scales", [P, D], U8)
-        nc.vector.quantize_mx(
-            out=w1_codes[:].bitcast(FP8X4), scales=w1_scales[:],
-            in_=w1_bf[:].rearrange("p t m j -> p (t m j)"),
-        )
-        xw = sb("xw", [P, D], U32, reuses="w1_bf")
+
+        def quantize_w1(u, reuses):
+            codes = sb("w1_codes%d" % u, [P, HALF], U32, reuses=reuses)
+            scales = sb("w1_scales%d" % u, [P, HALF], U8)
+            nc.vector.quantize_mx(
+                out=codes[:].bitcast(FP8X4), scales=scales[:],
+                in_=w1_bf[:, 2 * u : 2 * u + 2, :, :].rearrange("p t m j -> p (t m j)"),
+            )
+            return codes, scales
+
+        w1_mx = [quantize_w1(0, "xs_table")]
+        xw = sb("xw", [P, D], U32)
         for n0 in range(0, D, HALF):
             nc.vector.tensor_copy(
                 out=xw[:, n0 : n0 + HALF],
                 in_=xw_table[:].indirect(picked[:, n0 // GROUP : (n0 + HALF) // GROUP]),
             )
+        w1_mx.append(quantize_w1(1, "xw_table"))
         pieces = [(0, 0, HALF), (0, HALF, HALF)] + [(t, 0, D) for t in range(1, PACK)]
         for number, (t, n0, step) in enumerate(pieces):
             cols = slice(n0, n0 + step)
             bank = bank_tile(BLOCKS + number % BLOCKS, [P, step])
             nc.tensor.matmul_mx(
                 out=bank[:],
-                lhsT=w1_codes[:, P * t : P * (t + 1)].bitcast(FP8X4),
-                lhsT_scale=w1_scales[:, P * t : P * (t + 1)],
+                lhsT=w1_mx[t // 2][0][:, P * (t % 2) : P * (t % 2 + 1)].bitcast(FP8X4),
+                lhsT_scale=w1_mx[t // 2][1][:, P * (t % 2) : P * (t % 2 + 1)],
                 rhs=xw[:, cols].bitcast(FP8X4), rhs_scale=xs[:, cols],
                 start=True, stop=True,
             )
             nc.scalar.copy(out=y[t][:, cols], in_=bank[:])
 
-        w3_codes = sb("w3_codes", [P, PACK, 2 * P], U8, reuses="xw_table")
+        w3_codes = sb("w3_codes", [P, PACK, 2 * P], U8)
         nc.vector.tensor_copy(
             out=w3_codes[:].bitcast(U16), in_=w3_raw[:].bitcast(U16).rearrange("p (m t) -> p t m", t=PACK)
         )
-        w3_sc = sb("w3_sc", [P, PACK, P], U8, reuses="w3_raw")
-        nc.vector.tensor_copy(out=w3_sc[:], in_=w3s_raw[:].rearrange("p (m t) -> p t m", t=PACK))
-        w2_bf = sb("w2_bf", [P, PACK, P, PACK], BF16, reuses="xs_table")
-        round_and_deal(nc.scalar.copy, w2_bf[:], w2_raw[:])
 
         def gather(out, t, c, v0=0, width=D):
             nc.vector.tensor_tensor(
@@ -213,6 +214,12 @@ def tile_picked_hgrid_gelu_po_kernel(
                 part = sb("part%d_%d" % (b, t), [P, P], F32)
                 nc.scalar.copy(out=part[:], in_=sums[b][:])
                 nc.tensor.transpose(backs[b][:, t, :], part[:], ident[:])
+        w2_bf = sb("w2_bf", [P, PACK, P, PACK], BF16, reuses="part%d_0" % LATE_BLOCKS[0])
+        for m0 in range(0, P, P // 4):
+            m1 = m0 + P // 4
+            round_and_deal(nc.scalar.copy, w2_bf[:, :, m0:m1, :], w2_raw[:, :, PACK * m0 : PACK * m1])
+        w3_sc = sb("w3_sc", [P, PACK, P], U8, reuses="part%d_1" % LAST_BLOCK)
+        nc.vector.tensor_copy(out=w3_sc[:], in_=w3s_raw[:].rearrange("p (m t) -> p t m", t=PACK))
         w2_codes = sb("w2_codes", [P, D], U32, reuses="ring%d" % ((CORNERS * PACK - 1) % RING))
         w2_scales = sb("w2_scales", [P, D], U8)
         nc.vector.quantize_mx(

@@ -26,8 +26,9 @@ LEVELS = 8
 BLOCK = 128
 BLOCKS = D // BLOCK
 LAST_BLOCK = BLOCKS - 1
-EARLY_BLOCKS = (0, 1)
-LATE_BLOCKS = (2, 3)
+EARLY_BLOCKS = (0, 1, 2)
+LATE_BLOCKS = (LAST_BLOCK,)
+FIRST_BLOCKS = (0, 1)
 RING = 3
 OUT_SPLIT = 48
 W1_SPLIT = 80
@@ -84,10 +85,10 @@ def tile_picked_hgrid_gelu_po_kernel(
         nc.gpsimd.memset(warm_in[:], 0.0)
         w3s_raw = sb("w3s_raw", [P, D], U8)
         nc.gpsimd.memset(w3s_raw[:].bitcast(I32), 0)
-        picked = sb("picked", [P, D // GROUP], U16)
-        nc.sync.dma_start(out=picked[:], in_=offs)
         w1_raw = sb("w1_raw", [P, PACK, D], F32)
         nc.sync.dma_start(out=w1_raw[:], in_=w1.rearrange("(p j) c -> p j c", j=PACK))
+        picked = sb("picked", [P, D // GROUP], U16)
+        nc.sync.dma_start(out=picked[:], in_=offs)
         load_scale_rows(nc.sync, xs_table, x_scales)
         xw_table = sb("xw_table", [P, TABLE], U32)
         nc.sync.dma_start(
@@ -183,7 +184,11 @@ def tile_picked_hgrid_gelu_po_kernel(
         backs = [
             bank_tile(BLOCKS + b, [P, 2 if b in EARLY_BLOCKS else PACK, BLOCK]) for b in range(BLOCKS)
         ]
+        fourth = sb("fourth", [P, PACK * BLOCK], F32)
+        z_third = sb("z_third", [P, HALF], F32)
+        z_words = [fourth[:, :HALF], fourth[:, HALF:], z_third[:]]
         sums = {}
+        gathers = 0
         for t in range(PACK):
             u, e = divmod(t, 2)
             for b in range(BLOCKS):
@@ -191,36 +196,51 @@ def tile_picked_hgrid_gelu_po_kernel(
                     sums[b] = bank_tile(b, [P, P])
                 elif e == 0:
                     sums[b] = bank_tile(b, [P, 2, P])
-            for c in range(CORNERS):
-                blocks = EARLY_BLOCKS if c == three else range(BLOCKS)
+            steps = [(c, range(BLOCKS)) for c in range(three)]
+            if t < PACK - 1:
+                steps = steps + [(three, EARLY_BLOCKS)]
+            else:
+                steps = [(c, FIRST_BLOCKS) for c in range(CORNERS)]
+                steps = steps + [(c, (2, LAST_BLOCK)) for c in range(three)] + [(three, (2,))]
+            for c, blocks in steps:
                 terms = sb(
-                    "terms%d_%d" % (t, c), [P, len(blocks) * BLOCK], F32,
-                    reuses="ring%d" % ((CORNERS * t + c) % RING),
+                    "terms%d" % gathers, [P, len(blocks) * BLOCK], F32, reuses="ring%d" % (gathers % RING)
                 )
-                gather(terms[:], t, c, 0, len(blocks) * BLOCK)
-                for b in blocks:
-                    early = b in EARLY_BLOCKS
+                gathers = gathers + 1
+                gather(terms[:], t, c, blocks[0] * BLOCK, len(blocks) * BLOCK)
+                closed = []
+                for n, b in enumerate(blocks):
+                    corners = [corner for corner, served in steps if b in served]
                     add_turned(
-                        sums[b][:, e, :] if early else sums[b][:], terms[:, b * BLOCK : (b + 1) * BLOCK],
-                        c == 0, c == (three if early else three - 1),
+                        sums[b][:, e, :] if b in EARLY_BLOCKS else sums[b][:],
+                        terms[:, n * BLOCK : (n + 1) * BLOCK], c == corners[0], c == corners[-1],
                     )
-            for b in EARLY_BLOCKS if e == 1 else ():
-                pairs = sb("pairs%d_%d" % (b, u), [P, P, 2], BF16)
-                nc.scalar.copy(out=pairs[:], in_=sums[b][:].rearrange("v e p -> v p e"))
-                nc.tensor.transpose(
-                    backs[b][:, u, :], pairs[:].rearrange("v p e -> v (p e)").bitcast(F32), ident[:]
-                )
-            for b in LATE_BLOCKS:
-                part = sb("part%d_%d" % (b, t), [P, P], F32)
-                nc.scalar.copy(out=part[:], in_=sums[b][:])
-                nc.tensor.transpose(backs[b][:, t, :], part[:], ident[:])
+                    if c == corners[-1]:
+                        closed.append(b)
+                for b in closed:
+                    if b == LAST_BLOCK:
+                        part = sb("part%d_%d" % (b, t), [P, P], F32)
+                        nc.scalar.copy(out=part[:], in_=sums[b][:])
+                        nc.tensor.transpose(backs[b][:, t, :], part[:], ident[:])
+                    elif e == 1:
+                        pairs = sb("pairs%d_%d" % (b, u), [P, P, 2], BF16)
+                        nc.scalar.copy(out=pairs[:], in_=sums[b][:].rearrange("v e p -> v p e"))
+                        nc.tensor.transpose(
+                            backs[b][:, u, :], pairs[:].rearrange("v p e -> v (p e)").bitcast(F32), ident[:]
+                        )
+                for b in closed:
+                    if b != LAST_BLOCK and t == PACK - 1:
+                        nc.scalar.copy(
+                            out=z_words[b].rearrange("p (v u) -> p v u", u=2),
+                            in_=backs[b][:].rearrange("p u v -> p v u"),
+                        )
         w2_bf = sb("w2_bf", [P, PACK, P, PACK], BF16, reuses="part%d_0" % LATE_BLOCKS[0])
         for m0 in range(0, P, P // 4):
             m1 = m0 + P // 4
             round_and_deal(nc.scalar.copy, w2_bf[:, :, m0:m1, :], w2_raw[:, :, PACK * m0 : PACK * m1])
-        w3_sc = sb("w3_sc", [P, PACK, P], U8, reuses="part%d_1" % LAST_BLOCK)
+        w3_sc = sb("w3_sc", [P, PACK, P], U8, reuses="ring%d" % ((gathers - 2) % RING))
         nc.vector.tensor_copy(out=w3_sc[:], in_=w3s_raw[:].rearrange("p (m t) -> p t m", t=PACK))
-        w2_codes = sb("w2_codes", [P, D], U32, reuses="ring%d" % ((CORNERS * PACK - 1) % RING))
+        w2_codes = sb("w2_codes", [P, D], U32, reuses="ring%d" % ((gathers - 3) % RING))
         w2_scales = sb("w2_scales", [P, D], U8)
         nc.vector.quantize_mx(
             out=w2_codes[:].bitcast(FP8X4), scales=w2_scales[:],
@@ -238,30 +258,17 @@ def tile_picked_hgrid_gelu_po_kernel(
             nc.scalar.activation(out=h_bf[:], in_=pre[:].rearrange("p t v -> p v t"), func=GELU)
             return h_bf
 
-        def interleave_pairs(words, b):
-            nc.scalar.copy(
-                out=words.rearrange("p (v u) -> p v u", u=2), in_=backs[b][:].rearrange("p u v -> p v u")
-            )
-
-        fourth = sb("fourth", [P, PACK * HALF], F32, reuses="ring%d" % ((CORNERS * PACK - 3) % RING))
-        last_plane = fourth[:, (PACK - 1) * HALF :]
-        for t in range(PACK - 1):
-            gather(fourth[:, t * HALF : (t + 1) * HALF], t, three, HALF, HALF)
-        interleave_pairs(last_plane, 0)
-        hidden = [first_layer(0, last_plane.bitcast(BF16))]
-        gather(last_plane, PACK - 1, three, HALF, HALF)
-        z_bf = sb("z_bf1", [P, BLOCK * PACK], BF16)
-        interleave_pairs(z_bf[:].bitcast(F32), 1)
-        hidden.append(first_layer(1, z_bf[:]))
-        for late, b in enumerate(LATE_BLOCKS):
-            z_bf = sb("z_bf%d" % b, [P, BLOCK * PACK], BF16, reuses=None if late else "z_bf1")
-            planes = fourth[:].rearrange("p (t v) -> p t v", t=PACK)[:, :, late * BLOCK : (late + 1) * BLOCK]
-            nc.vector.tensor_tensor(
-                out=z_bf[:].rearrange("p (c i t) -> p c t i", i=2, t=PACK),
-                in0=backs[b][:].rearrange("p t (c i) -> p c t i", i=2),
-                in1=planes.rearrange("p t (c i) -> p c t i", i=2), op=ADD,
-            )
-            hidden.append(first_layer(b, z_bf[:]))
+        hidden = [first_layer(b, z_words[b].bitcast(BF16)) for b in FIRST_BLOCKS]
+        for t in range(PACK):
+            gather(fourth[:, t * BLOCK : (t + 1) * BLOCK], t, three, LAST_BLOCK * BLOCK, BLOCK)
+        hidden.append(first_layer(2, z_words[2].bitcast(BF16)))
+        z_last = sb("z_last", [P, BLOCK * PACK], BF16)
+        nc.vector.tensor_tensor(
+            out=z_last[:].rearrange("p (c i t) -> p c t i", i=2, t=PACK),
+            in0=backs[LAST_BLOCK][:].rearrange("p t (c i) -> p c t i", i=2),
+            in1=fourth[:].rearrange("p (t c i) -> p c t i", t=PACK, i=2), op=ADD,
+        )
+        hidden.append(first_layer(LAST_BLOCK, z_last[:]))
         products = []
         for b in range(BLOCKS):
             h_codes, h_scales = quantize_block("h%d" % b, hidden[b][:].rearrange("p v t -> p (v t)"))
@@ -285,7 +292,7 @@ def tile_picked_hgrid_gelu_po_kernel(
                 in_=result[:, :, piece].rearrange("p t (c i) -> p c t i", i=4),
             )
 
-        for chunk in (EARLY_BLOCKS, (2,), (LAST_BLOCK,)):
+        for chunk in (FIRST_BLOCKS, (2,), (LAST_BLOCK,)):
             v0, width = chunk[0] * BLOCK, len(chunk) * BLOCK
             cols = slice(v0, v0 + width)
             result = sb("result%d" % chunk[0], [P, PACK, width], F32)

@@ -68,8 +68,8 @@ def tile_picked_hgrid_gelu_po_kernel(
 
         def round_and_deal(copy, grouped, raw):
             copy(
-                out=grouped.rearrange("p t m j -> p m t j"),
-                in_=raw.rearrange("p j (m t) -> p m t j", t=PACK),
+                out=grouped.rearrange("p t m j -> p m j t"),
+                in_=raw.rearrange("p j (m t) -> p m j t", t=PACK),
             )
 
         def product_planes(planes, codes, scales, rhs_codes, rhs_scales):

@@ -111,7 +111,7 @@ def tile_picked_hgrid_gelu_po_kernel(
         res_sb = sb("res_sb", [P, PACK, D], F32)
         nc.sync.dma_start(out=res_sb[:], in_=res.rearrange("(p t) v -> p t v", t=PACK))
 
-        y = [sb("y%d" % t, [P, 2 * D], F32) for t in range(PACK)]
+        y = [sb("y%d" % t, [P, 2 * D + 1], F32) for t in range(PACK)]
         for plane in y:
             nc.vector.memset(plane[:, D:], 0.0)
 

@@ -31,7 +31,7 @@ LATE_BLOCKS = (LAST_BLOCK,)
 FIRST_BLOCKS = (0, 1)
 RING = 3
 OUT_SPLIT = 48
-W1_SPLIT = 80
+W1_SPLITS = (88, 56)
 
 FLOPS = 3 * 2 * D * D * D
 BYTES = (
@@ -85,15 +85,15 @@ def tile_picked_hgrid_gelu_po_kernel(
         nc.gpsimd.memset(warm_in[:], 0.0)
         w3s_raw = sb("w3s_raw", [P, D], U8)
         nc.gpsimd.memset(w3s_raw[:].bitcast(I32), 0)
-        w1_raw = sb("w1_raw", [P, PACK, D], F32)
-        nc.sync.dma_start(out=w1_raw[:], in_=w1.rearrange("(p j) c -> p j c", j=PACK))
-        picked = sb("picked", [P, D // GROUP], U16)
-        nc.sync.dma_start(out=picked[:], in_=offs)
-        load_scale_rows(nc.sync, xs_table, x_scales)
         xw_table = sb("xw_table", [P, TABLE], U32)
         nc.sync.dma_start(
             out=xw_table[:].bitcast(I32), in_=x_words[0].rearrange("p n r -> p (n r)").bitcast(I32)
         )
+        picked = sb("picked", [P, D // GROUP], U16)
+        nc.sync.dma_start(out=picked[:], in_=offs)
+        load_scale_rows(nc.sync, xs_table, x_scales)
+        w1_raw = sb("w1_raw", [P, PACK, D], F32)
+        nc.sync.dma_start(out=w1_raw[:], in_=w1.rearrange("(p j) c -> p j c", j=PACK))
         w3_raw = sb("w3_raw", [P, 2 * D], U8, reuses="ring0")
         lists = [sb("list%d" % c, [P, D // GROUP], U16) for c in range(CORNERS)]
         weights = [sb("weight%d" % c, [P, D], F32) for c in range(CORNERS)]
@@ -120,37 +120,37 @@ def tile_picked_hgrid_gelu_po_kernel(
         warm_out = sb("warm_out", [P, 1], F32)
         nc.scalar.activation(out=warm_out[:], in_=warm_in[:], func=GELU)
 
+        xw = sb("xw", [P, D], U32)
+        nc.vector.tensor_copy(out=xw[:], in_=xw_table[:].indirect(picked[:]))
         xs = sb("xs", [P, D], U8)
         nc.vector.tensor_copy(out=xs[:], in_=xs_table[:].indirect(picked[:]))
-        w1_bf = sb("w1_bf", [P, PACK, P, PACK], BF16)
-        for m0, m1, copy in ((0, W1_SPLIT, nc.scalar.copy), (W1_SPLIT, P, nc.vector.tensor_copy)):
-            round_and_deal(copy, w1_bf[:, :, m0:m1, :], w1_raw[:, :, PACK * m0 : PACK * m1])
+        w1_bf = [sb("w1_bf%d" % u, [P, 2, P, PACK], BF16) for u in range(2)]
+        w1_columns = w1_raw[:].rearrange("p j (m t) -> p m j t", t=PACK)
+        for u, split in enumerate(W1_SPLITS):
+            for m0, m1, copy in ((0, split, nc.vector.tensor_copy), (split, P, nc.scalar.copy)):
+                copy(
+                    out=w1_bf[u][:, :, m0:m1, :].rearrange("p t m j -> p m j t"),
+                    in_=w1_columns[:, m0:m1, :, 2 * u : 2 * u + 2],
+                )
+        w1_codes = sb("w1_codes", [P, D], U32)
+        w1_scales = sb("w1_scales", [P, D], U8)
 
-        def quantize_w1(u, reuses):
-            codes = sb("w1_codes%d" % u, [P, HALF], U32, reuses=reuses)
-            scales = sb("w1_scales%d" % u, [P, HALF], U8)
+        def quantize_w1(t0, t1):
             nc.vector.quantize_mx(
-                out=codes[:].bitcast(FP8X4), scales=scales[:],
-                in_=w1_bf[:, 2 * u : 2 * u + 2, :, :].rearrange("p t m j -> p (t m j)"),
+                out=w1_codes[:, P * t0 : P * t1].bitcast(FP8X4), scales=w1_scales[:, P * t0 : P * t1],
+                in_=w1_bf[t0 // 2][:, t0 % 2 : t0 % 2 + t1 - t0, :, :].rearrange("p t m j -> p (t m j)"),
             )
-            return codes, scales
 
-        w1_mx = [quantize_w1(0, "xs_table")]
-        xw = sb("xw", [P, D], U32)
-        for n0 in range(0, D, HALF):
-            nc.vector.tensor_copy(
-                out=xw[:, n0 : n0 + HALF],
-                in_=xw_table[:].indirect(picked[:, n0 // GROUP : (n0 + HALF) // GROUP]),
-            )
-        w1_mx.append(quantize_w1(1, "xw_table"))
-        pieces = [(0, 0, HALF), (0, HALF, HALF)] + [(t, 0, D) for t in range(1, PACK)]
+        for t0, t1 in ((0, 1), (1, 2), (2, PACK)):
+            quantize_w1(t0, t1)
+        pieces = [(0, n0, BLOCK) for n0 in range(0, D, BLOCK)] + [(t, 0, D) for t in range(1, PACK)]
         for number, (t, n0, step) in enumerate(pieces):
             cols = slice(n0, n0 + step)
             bank = bank_tile(BLOCKS + number % BLOCKS, [P, step])
             nc.tensor.matmul_mx(
                 out=bank[:],
-                lhsT=w1_mx[t // 2][0][:, P * (t % 2) : P * (t % 2 + 1)].bitcast(FP8X4),
-                lhsT_scale=w1_mx[t // 2][1][:, P * (t % 2) : P * (t % 2 + 1)],
+                lhsT=w1_codes[:, P * t : P * (t + 1)].bitcast(FP8X4),
+                lhsT_scale=w1_scales[:, P * t : P * (t + 1)],
                 rhs=xw[:, cols].bitcast(FP8X4), rhs_scale=xs[:, cols],
                 start=True, stop=True,
             )
@@ -160,6 +160,7 @@ def tile_picked_hgrid_gelu_po_kernel(
         nc.vector.tensor_copy(
             out=w3_codes[:].bitcast(U16), in_=w3_raw[:].bitcast(U16).rearrange("p (m t) -> p t m", t=PACK)
         )
+
 
         def gather(out, t, c, v0=0, width=D):
             nc.vector.tensor_tensor(
@@ -313,7 +314,10 @@ def tile_picked_hgrid_gelu_po_kernel(
                         in1=res_sb[:, :, b * BLOCK : (b + 1) * BLOCK], op=ADD,
                     )
                     round_and_interleave(nc.scalar.copy, o_bf, result, piece)
-            nc.sync.dma_start(out=out_rows[:, :, cols], in_=result[:])
+            for n, b in enumerate(chunk):
+                nc.sync.dma_start(
+                    out=out_rows[:, :, b * BLOCK : (b + 1) * BLOCK], in_=result[:, :, n * BLOCK : (n + 1) * BLOCK]
+                )
             nc.vector.quantize_mx(
                 out=o_codes[:, cols].bitcast(FP8X4), scales=o_scales[:, cols],
                 in_=o_bf[:].rearrange("p v t -> p (v t)"),

@@ -293,10 +293,11 @@ def tile_picked_hgrid_gelu_po_kernel(
                 in_=result[:, :, piece].rearrange("p t (c i) -> p c t i", i=4),
             )
 
+        results = [sb("result%d" % h, [P, PACK, HALF], F32) for h in range(2)]
         for chunk in (FIRST_BLOCKS, (2,), (LAST_BLOCK,)):
             v0, width = chunk[0] * BLOCK, len(chunk) * BLOCK
             cols = slice(v0, v0 + width)
-            result = sb("result%d" % chunk[0], [P, PACK, width], F32)
+            result = results[v0 // HALF][:, :, v0 % HALF : v0 % HALF + width]
             o_bf = sb("o_bf%d" % chunk[0], [P, width, PACK], BF16)
             if chunk[0] == LAST_BLOCK:
                 for u, bank in enumerate(products[LAST_BLOCK]):
@@ -304,20 +305,19 @@ def tile_picked_hgrid_gelu_po_kernel(
                     nc.vector.tensor_tensor(
                         out=result[:, pair, :], in0=bank[:], in1=res_sb[:, pair, cols], op=ADD
                     )
+                    nc.sync.dma_start(out=out_rows[:, pair, HALF:], in_=results[1][:, pair, :])
                 round_and_interleave(nc.scalar.copy, o_bf, result, slice(0, OUT_SPLIT))
                 round_and_interleave(nc.vector.tensor_copy, o_bf, result, slice(OUT_SPLIT, BLOCK))
             else:
                 for n, b in enumerate(chunk):
                     piece = slice(n * BLOCK, (n + 1) * BLOCK)
+                    points = slice(b * BLOCK, (b + 1) * BLOCK)
                     nc.vector.tensor_tensor(
-                        out=result[:, :, piece], in0=products[b][0][:],
-                        in1=res_sb[:, :, b * BLOCK : (b + 1) * BLOCK], op=ADD,
+                        out=result[:, :, piece], in0=products[b][0][:], in1=res_sb[:, :, points], op=ADD
                     )
                     round_and_interleave(nc.scalar.copy, o_bf, result, piece)
-            for n, b in enumerate(chunk):
-                nc.sync.dma_start(
-                    out=out_rows[:, :, b * BLOCK : (b + 1) * BLOCK], in_=result[:, :, n * BLOCK : (n + 1) * BLOCK]
-                )
+                    if b in FIRST_BLOCKS:
+                        nc.sync.dma_start(out=out_rows[:, :, points], in_=result[:, :, piece])
             nc.vector.quantize_mx(
                 out=o_codes[:, cols].bitcast(FP8X4), scales=o_scales[:, cols],
                 in_=o_bf[:].rearrange("p v t -> p (v t)"),

@@ -13,6 +13,7 @@ FP8X4 = mybir.dt.float8_e4m3fn_x4
 FP4X4 = mybir.dt.float4_e2m1fn_x4
 MULT = mybir.AluOpType.mult
 ADD = mybir.AluOpType.add
+COPY = mybir.ActivationFunctionType.Copy
 GELU = mybir.ActivationFunctionType.Gelu_apprx_tanh
 
 P = 128
@@ -29,9 +30,12 @@ LAST_BLOCK = BLOCKS - 1
 EARLY_BLOCKS = (0, 1, 2)
 LATE_BLOCKS = (LAST_BLOCK,)
 FIRST_BLOCKS = (0, 1)
-RING = 3
+RING = 4
+PLAIN_RING = 3
+SECOND_SUMS = (4, 5, 0, 1)
 OUT_SPLIT = 48
-W1_SPLITS = (88, 56)
+RUN = 8
+W1_SPLITS = (10, 6, 6, 6)
 
 FLOPS = 3 * 2 * D * D * D
 BYTES = (
@@ -94,25 +98,31 @@ def tile_picked_hgrid_gelu_po_kernel(
         load_scale_rows(nc.sync, xs_table, x_scales)
         w1_raw = sb("w1_raw", [P, PACK, D], F32)
         nc.sync.dma_start(out=w1_raw[:], in_=w1.rearrange("(p j) c -> p j c", j=PACK))
-        w3_raw = sb("w3_raw", [P, 2 * D], U8, reuses="ring0")
+        w3_raw = sb("w3_raw", [P, 2 * D], U8)
         lists = [sb("list%d" % c, [P, D // GROUP], U16) for c in range(CORNERS)]
-        weights = [sb("weight%d" % c, [P, D], F32) for c in range(CORNERS)]
+        weight_pairs = [sb("weights%d" % u, [P, 2, D], F32) for u in range(2)]
+        weights = [weight_pairs[c // 2][:, c % 2, :] for c in range(CORNERS)]
 
-        def load_corner(c, entries, a):
+        def load_weights(c, a):
+            nc.sync.dma_start(out=weights[c], in_=a.rearrange("(p j) v -> p j v", j=PACK)[:, 0, :])
+
+        for c, entries in ((2, c3), (3, c4), (0, c1), (1, c2)):
             nc.sync.dma_start(out=lists[c][:], in_=entries)
-            nc.sync.dma_start(out=weights[c][:], in_=a.rearrange("(p j) v -> p j v", j=PACK)[:, 0, :])
-
+        load_weights(0, a1)
         nc.sync.dma_start(out=w3_raw[:].bitcast(I32), in_=w3_words[0].bitcast(I32))
-        for c, (entries, a) in enumerate(((c1, a1), (c2, a2), (c3, a3), (c4, a4))):
-            load_corner(c, entries, a)
+        for c, a in ((1, a2), (3, a4), (2, a3)):
+            load_weights(c, a)
         load_scale_rows(nc.sync, w3s_raw, w3_scales)
         w2_raw = sb("w2_raw", [P, PACK, D], F32)
-        nc.sync.dma_start(out=w2_raw[:], in_=w2.rearrange("(p j) c -> p j c", j=PACK))
+        for j in range(PACK):
+            nc.sync.dma_start(
+                out=w2_raw[:, j, :], in_=w2.rearrange("(q j r) c -> j q r c", j=PACK, r=RUN)[j]
+            )
         res_sb = sb("res_sb", [P, PACK, D], F32)
         nc.sync.dma_start(out=res_sb[:], in_=res.rearrange("(p t) v -> p t v", t=PACK))
 
-        y = [sb("y%d" % t, [P, 2 * D + 1], F32) for t in range(PACK)]
-        for plane in y:
+        y = [sb("y%d" % t, [P, 2 * D if t < 2 else D], F32) for t in range(PACK)]
+        for plane in y[:2]:
             nc.vector.memset(plane[:, D:], 0.0)
 
         ident = sb("ident", [P, P], F32)
@@ -124,27 +134,29 @@ def tile_picked_hgrid_gelu_po_kernel(
         nc.vector.tensor_copy(out=xw[:], in_=xw_table[:].indirect(picked[:]))
         xs = sb("xs", [P, D], U8)
         nc.vector.tensor_copy(out=xs[:], in_=xs_table[:].indirect(picked[:]))
-        w1_bf = [sb("w1_bf%d" % u, [P, 2, P, PACK], BF16) for u in range(2)]
-        w1_columns = w1_raw[:].rearrange("p j (m t) -> p m j t", t=PACK)
-        for u, split in enumerate(W1_SPLITS):
-            for m0, m1, copy in ((0, split, nc.vector.tensor_copy), (split, P, nc.scalar.copy)):
-                copy(
-                    out=w1_bf[u][:, :, m0:m1, :].rearrange("p t m j -> p m j t"),
-                    in_=w1_columns[:, m0:m1, :, 2 * u : 2 * u + 2],
-                )
+        w1_bf = [sb("w1_bf%d" % t, [P, P * PACK], BF16) for t in range(PACK)]
+        w1_columns = w1_raw[:].rearrange("p j (q t r) -> p t q j r", t=PACK, r=RUN)
         w1_codes = sb("w1_codes", [P, D], U32)
         w1_scales = sb("w1_scales", [P, D], U8)
 
-        def quantize_w1(t0, t1):
+        def round_w1(t):
+            grouped = w1_bf[t][:].rearrange("p (q r j) -> p q j r", r=RUN, j=PACK)
+            split = W1_SPLITS[t]
+            for q0, q1, copy in ((0, split, nc.vector.tensor_copy), (split, P // RUN, nc.scalar.copy)):
+                copy(out=grouped[:, q0:q1, :, :], in_=w1_columns[:, t, q0:q1, :, :])
+
+        def quantize_w1(t):
             nc.vector.quantize_mx(
-                out=w1_codes[:, P * t0 : P * t1].bitcast(FP8X4), scales=w1_scales[:, P * t0 : P * t1],
-                in_=w1_bf[t0 // 2][:, t0 % 2 : t0 % 2 + t1 - t0, :, :].rearrange("p t m j -> p (t m j)"),
+                out=w1_codes[:, P * t : P * (t + 1)].bitcast(FP8X4), scales=w1_scales[:, P * t : P * (t + 1)],
+                in_=w1_bf[t][:],
             )
 
-        for t0, t1 in ((0, 1), (1, 2), (2, PACK)):
-            quantize_w1(t0, t1)
-        pieces = [(0, n0, BLOCK) for n0 in range(0, D, BLOCK)] + [(t, 0, D) for t in range(1, PACK)]
-        for number, (t, n0, step) in enumerate(pieces):
+        round_w1(0)
+        for t in range(PACK):
+            if t + 1 < PACK:
+                round_w1(t + 1)
+            quantize_w1(t)
+        def make_plane(number, t, n0, step, copy):
             cols = slice(n0, n0 + step)
             bank = bank_tile(BLOCKS + number % BLOCKS, [P, step])
             nc.tensor.matmul_mx(
@@ -154,7 +166,11 @@ def tile_picked_hgrid_gelu_po_kernel(
                 rhs=xw[:, cols].bitcast(FP8X4), rhs_scale=xs[:, cols],
                 start=True, stop=True,
             )
-            nc.scalar.copy(out=y[t][:, cols], in_=bank[:])
+            copy(out=y[t][:, cols], in_=bank[:])
+
+        for n in range(BLOCKS):
+            make_plane(n, 0, n * BLOCK, BLOCK, nc.vector.tensor_copy if n % 2 else nc.scalar.copy)
+        make_plane(4, 1, 0, D, nc.scalar.copy)
 
         w3_codes = sb("w3_codes", [P, PACK, 2 * P], U8)
         nc.vector.tensor_copy(
@@ -162,95 +178,112 @@ def tile_picked_hgrid_gelu_po_kernel(
         )
 
 
-        def gather(out, t, c, v0=0, width=D):
+        def gather_weighted(t, c, v0, width, terms=None):
+            if terms is None:
+                terms = sb("terms%d_%d_%d" % (t, c, v0), [P, width], F32)[:]
             nc.vector.tensor_tensor(
-                out=out,
+                out=terms,
                 in0=y[t][:].indirect(lists[c][:, v0 // GROUP : (v0 + width) // GROUP]),
                 in1=weights[c][:, v0 : v0 + width], op=MULT,
             )
+            return terms
 
-        def add_turned(out, values, first, final):
-            nc.tensor.matmul(out=out, lhsT=values, rhs=ident[:], start=first, stop=final, is_transpose=True)
-
-        def quantize_block(name, grouped):
-            codes = sb(name + "_codes", [P, BLOCK], U32)
-            scales = sb(name + "_scales", [P, BLOCK], U8)
-            nc.vector.quantize_mx(
-                out=codes[:].bitcast(FP8X4), scales=scales[:],
-                in_=grouped,
+        def gather_corner(out, t, c, v0):
+            width = out.shape[1]
+            nc.scalar.activation(
+                out=out, in_=y[t][:].indirect(lists[c][:, v0 // GROUP : (v0 + width) // GROUP]), func=COPY
             )
+
+        def gather_plain(t, v0, width, reuses=None):
+            plain = sb("plain%d_%d" % (t, v0), [P, 2, width], F32, reuses=reuses)
+            for e in range(2):
+                gather_corner(plain[:, e, :], t, 2 + e, v0)
+            return plain
+
+        def weigh_one(plain, c, v0, terms):
+            nc.vector.tensor_tensor(
+                out=terms, in0=plain, in1=weights[c][:, v0 : v0 + plain.shape[1]], op=MULT
+            )
+            return terms
+
+        def weigh(plain, t, v0, width, pieces=1, terms=None, reuses=None):
+            if terms is None:
+                terms = sb("weighed%d_%d" % (t, v0), [P, 2, width], F32, reuses=reuses)
+            for n in range(pieces):
+                e = slice(2 * n // pieces, 2 * (n + 1) // pieces)
+                nc.vector.tensor_tensor(
+                    out=terms[:, e, :], in0=plain[:, e, :], in1=weight_pairs[1][:, e, v0 : v0 + width], op=MULT
+                )
+            return [terms[:, e, :] for e in range(2)]
+
+        sums = {}
+        backs = {}
+        paired = {}
+
+        added = {}
+
+        def add_turned(t, v0, terms):
+            for n in range(terms.shape[1] // BLOCK):
+                b = v0 // BLOCK + n
+                if (b, t // 2) not in sums:
+                    sums[b, t // 2] = bank_tile(b if t < 2 else SECOND_SUMS[b], [P, 2, P])
+                added[b, t] = added.get((b, t), 0) + 1
+                nc.tensor.matmul(
+                    out=sums[b, t // 2][:, t % 2, :], lhsT=terms[:, n * BLOCK : (n + 1) * BLOCK], rhs=ident[:],
+                    start=added[b, t] == 1, stop=added[b, t] == CORNERS - (b == LAST_BLOCK), is_transpose=True,
+                )
+
+        def round_sums(b, u, reuses=None):
+            pairs = sb("pairs%d_%d" % (b, u), [P, P, 2], BF16, reuses=reuses)
+            nc.scalar.copy(out=pairs[:], in_=sums[b, u][:].rearrange("v e p -> v p e"))
+            paired[b, u] = pairs
+
+        def turn_back(b):
+            backs[b] = bank_tile(SECOND_SUMS[b], [P, 2, BLOCK])
+            for u in range(2):
+                nc.tensor.transpose(
+                    backs[b][:, u, :], paired[b, u][:].rearrange("v p e -> v (p e)").bitcast(F32), ident[:]
+                )
+
+        def copy_part(u, reuses=None):
+            part = sb("part%d" % u, [P, 2, P], F32, reuses=reuses)
+            nc.scalar.copy(out=part[:], in_=sums[LAST_BLOCK, u][:])
+            paired[LAST_BLOCK, u] = part
+
+        def turn_back_part():
+            backs[LAST_BLOCK] = bank_tile(SECOND_SUMS[LAST_BLOCK], [P, PACK, BLOCK])
+            for t in range(PACK):
+                nc.tensor.transpose(backs[LAST_BLOCK][:, t, :], paired[LAST_BLOCK, t // 2][:, t % 2, :], ident[:])
+
+        def z_of(b, copy, words):
+            copy(out=words.rearrange("p (v u) -> p v u", u=2), in_=backs[b][:].rearrange("p u v -> p v u"))
+            return words.bitcast(BF16)
+
+        def quantize_block(name, grouped, reuses=None):
+            codes = sb(name + "_codes", [P, BLOCK], U32, reuses=reuses)
+            scales = sb(name + "_scales", [P, BLOCK], U8)
+            nc.vector.quantize_mx(out=codes[:].bitcast(FP8X4), scales=scales[:], in_=grouped)
             return codes, scales
 
-        three = CORNERS - 1
-        backs = [
-            bank_tile(BLOCKS + b, [P, 2 if b in EARLY_BLOCKS else PACK, BLOCK]) for b in range(BLOCKS)
-        ]
-        fourth = sb("fourth", [P, PACK * BLOCK], F32)
-        z_third = sb("z_third", [P, HALF], F32)
-        z_words = [fourth[:, :HALF], fourth[:, HALF:], z_third[:]]
-        sums = {}
-        gathers = 0
-        for t in range(PACK):
-            u, e = divmod(t, 2)
-            for b in range(BLOCKS):
-                if b in LATE_BLOCKS:
-                    sums[b] = bank_tile(b, [P, P])
-                elif e == 0:
-                    sums[b] = bank_tile(b, [P, 2, P])
-            steps = [(c, range(BLOCKS)) for c in range(three)]
-            if t < PACK - 1:
-                steps = steps + [(three, EARLY_BLOCKS)]
-            else:
-                steps = [(c, FIRST_BLOCKS) for c in range(CORNERS)]
-                steps = steps + [(c, (2, LAST_BLOCK)) for c in range(three)] + [(three, (2,))]
-            for c, blocks in steps:
-                terms = sb(
-                    "terms%d" % gathers, [P, len(blocks) * BLOCK], F32, reuses="ring%d" % (gathers % RING)
-                )
-                gathers = gathers + 1
-                gather(terms[:], t, c, blocks[0] * BLOCK, len(blocks) * BLOCK)
-                closed = []
-                for n, b in enumerate(blocks):
-                    corners = [corner for corner, served in steps if b in served]
-                    add_turned(
-                        sums[b][:, e, :] if b in EARLY_BLOCKS else sums[b][:],
-                        terms[:, n * BLOCK : (n + 1) * BLOCK], c == corners[0], c == corners[-1],
-                    )
-                    if c == corners[-1]:
-                        closed.append(b)
-                for b in closed:
-                    if b == LAST_BLOCK:
-                        part = sb("part%d_%d" % (b, t), [P, P], F32)
-                        nc.scalar.copy(out=part[:], in_=sums[b][:])
-                        nc.tensor.transpose(backs[b][:, t, :], part[:], ident[:])
-                    elif e == 1:
-                        pairs = sb("pairs%d_%d" % (b, u), [P, P, 2], BF16)
-                        nc.scalar.copy(out=pairs[:], in_=sums[b][:].rearrange("v e p -> v p e"))
-                        nc.tensor.transpose(
-                            backs[b][:, u, :], pairs[:].rearrange("v p e -> v (p e)").bitcast(F32), ident[:]
-                        )
-                for b in closed:
-                    if b != LAST_BLOCK and t == PACK - 1:
-                        nc.scalar.copy(
-                            out=z_words[b].rearrange("p (v u) -> p v u", u=2),
-                            in_=backs[b][:].rearrange("p u v -> p v u"),
-                        )
-        w2_bf = sb("w2_bf", [P, PACK, P, PACK], BF16, reuses="part%d_0" % LATE_BLOCKS[0])
-        for m0 in range(0, P, P // 4):
-            m1 = m0 + P // 4
-            round_and_deal(nc.scalar.copy, w2_bf[:, :, m0:m1, :], w2_raw[:, :, PACK * m0 : PACK * m1])
-        w3_sc = sb("w3_sc", [P, PACK, P], U8, reuses="ring%d" % ((gathers - 2) % RING))
-        nc.vector.tensor_copy(out=w3_sc[:], in_=w3s_raw[:].rearrange("p (m t) -> p t m", t=PACK))
-        w2_codes = sb("w2_codes", [P, D], U32, reuses="ring%d" % ((gathers - 3) % RING))
+        w2_bf = sb("w2_bf", [P, PACK, P, PACK], BF16)
+        w2_codes = sb("w2_codes", [P, D], U32)
         w2_scales = sb("w2_scales", [P, D], U8)
-        nc.vector.quantize_mx(
-            out=w2_codes[:].bitcast(FP8X4), scales=w2_scales[:],
-            in_=w2_bf[:].rearrange("p t m j -> p (t m j)"),
-        )
+
+        def round_w2(copy, m0, m1):
+            round_and_deal(copy, w2_bf[:, :, m0:m1, :], w2_raw[:, :, PACK * m0 : PACK * m1])
+
+        def quantize_w2():
+            nc.vector.quantize_mx(
+                out=w2_codes[:].bitcast(FP8X4), scales=w2_scales[:],
+                in_=w2_bf[:].rearrange("p t m j -> p (t m j)"),
+            )
+
+        def deal_w3_scales(w3_sc):
+            nc.vector.tensor_copy(out=w3_sc[:], in_=w3s_raw[:].rearrange("p (m t) -> p t m", t=PACK))
 
         def first_layer(b, z_bf):
             z_codes, z_scales = quantize_block("z%d" % b, z_bf)
-            pre = bank_tile(b, [P, PACK, BLOCK])
+            pre = bank_tile(6 + b % 2, [P, PACK, BLOCK])
             product_planes(
                 [pre[:, t, :] for t in range(PACK)], lambda t: w2_codes[:, P * t : P * (t + 1)].bitcast(FP8X4),
                 lambda t: w2_scales[:, P * t : P * (t + 1)], z_codes, z_scales,
@@ -259,10 +292,80 @@ def tile_picked_hgrid_gelu_po_kernel(
             nc.scalar.activation(out=h_bf[:], in_=pre[:].rearrange("p t v -> p v t"), func=GELU)
             return h_bf
 
-        hidden = [first_layer(b, z_words[b].bitcast(BF16)) for b in FIRST_BLOCKS]
+        products = {}
+
+        def second_layer(b, h_bf, w3_sc):
+            h_codes, h_scales = quantize_block("h%d" % b, h_bf[:].rearrange("p v t -> p (v t)"), "z_words2" if b == 1 else None)
+            numbers = (4, 5) if b == LAST_BLOCK else ((1, 0, 2)[b],)
+            share = PACK // len(numbers)
+            banks = [bank_tile(number, [P, share, BLOCK]) for number in numbers]
+            product_planes(
+                [banks[t // share][:, t % share, :] for t in range(PACK)],
+                lambda t: w3_codes[:, t, :].bitcast(FP4X4), lambda t: w3_sc[:, t, :], h_codes, h_scales,
+            )
+            products[b] = banks
+
+        def add_all(t, v0, terms):
+            for one in terms:
+                add_turned(t, v0, one)
+
+        def gather_half(t, v0, room):
+            return [gather_weighted(t, c, v0, HALF, room[:, c * HALF : (c + 1) * HALF]) for c in range(2)]
+
+        early = LAST_BLOCK * BLOCK
+        add_turned(0, 0, gather_weighted(0, 0, 0, early))
+        add_turned(0, 0, gather_weighted(0, 1, 0, D))
+        plain0 = gather_plain(0, 0, D)
+        make_plane(5, 2, 0, D, nc.scalar.copy)
+        make_plane(6, 3, 0, D, nc.scalar.copy)
+        ahead = gather_weighted(1, 1, 0, D)
+        w = weigh(plain0, 0, 0, D, 2)
+        add_all(0, 0, w)
+        add_turned(1, 0, ahead)
+        plain1 = gather_plain(1, 0, D)
+        add_turned(1, 0, gather_weighted(1, 0, 0, early, plain0[:, 0, :early]))
+        add_all(2, 0, gather_half(2, 0, plain0[:, 1, :]))
+        add_all(1, 0, weigh(plain1, 1, 0, D))
+        plains = {(t, v0): gather_plain(t, v0, HALF) for t, v0 in ((2, 0), (3, 0), (2, HALF))}
+        single = sb("single", [P, HALF], F32)
+        gather_corner(single[:], 2, 1, HALF)
+        for b in FIRST_BLOCKS:
+            round_sums(b, 0)
+        add_all(2, 0, weigh(plains[2, 0], 2, 0, HALF))
+        add_all(3, 0, weigh(plains[3, 0], 3, 0, HALF))
+        w = gather_half(3, 0, plain1[:, 0, :])
+        add_all(3, 0, w)
+        for b in FIRST_BLOCKS:
+            round_sums(b, 1)
+            turn_back(b)
+        z_words = [sb("z_words%d" % b, [P, HALF], F32) for b in EARLY_BLOCKS]
+        z_bf = [z_of(b, nc.scalar.copy, z_words[b][:]) for b in FIRST_BLOCKS]
+        plains[3, HALF] = gather_plain(3, HALF, HALF, reuses="pairs1_1")
+        round_sums(2, 0, reuses="pairs1_0")
+        copy_part(0, reuses="pairs0_0")
+        round_w2(nc.vector.tensor_copy, 0, P)
+        add_turned(2, HALF, weigh_one(single[:], 1, HALF, plain1[:, 1, :HALF]))
+        quantize_w2()
+        room = sb("room", [P, BLOCK], F32, reuses="w2_bf")
+        add_turned(2, HALF, gather_weighted(2, 0, HALF, BLOCK, room[:]))
+        hidden = [first_layer(b, z_bf[b]) for b in FIRST_BLOCKS]
+        last = sb("last", [P, 6, HALF], F32, reuses="z_words1")
+        add_all(2, HALF, weigh(plains[2, HALF], 2, HALF, HALF, terms=last[:, 0:2, :]))
+        add_turned(3, HALF, gather_weighted(3, 0, HALF, BLOCK, last[:, 4, :BLOCK]))
+        add_all(3, HALF, weigh(plains[3, HALF], 3, HALF, HALF, terms=last[:, 2:4, :]))
+        w = gather_weighted(3, 1, HALF, HALF, last[:, 5, :])
+        add_turned(3, HALF, w)
+        round_sums(2, 1)
+        turn_back(2)
+        copy_part(1)
+        turn_back_part()
+        z_bf.append(z_of(2, nc.scalar.copy, z_words[2][:]))
+        fourth = sb("fourth", [P, PACK * BLOCK], F32, reuses="pairs1_1")
         for t in range(PACK):
-            gather(fourth[:, t * BLOCK : (t + 1) * BLOCK], t, three, LAST_BLOCK * BLOCK, BLOCK)
-        hidden.append(first_layer(2, z_words[2].bitcast(BF16)))
+            w = gather_weighted(t, 0, early, BLOCK, fourth[:, t * BLOCK : (t + 1) * BLOCK])
+        w3_sc = sb("w3_sc", [P, PACK, P], U8, reuses="y2")
+        deal_w3_scales(w3_sc)
+        hidden.append(first_layer(2, z_bf[2]))
         z_last = sb("z_last", [P, BLOCK * PACK], BF16)
         nc.vector.tensor_tensor(
             out=z_last[:].rearrange("p (c i t) -> p c t i", i=2, t=PACK),
@@ -270,17 +373,8 @@ def tile_picked_hgrid_gelu_po_kernel(
             in1=fourth[:].rearrange("p (t c i) -> p c t i", t=PACK, i=2), op=ADD,
         )
         hidden.append(first_layer(LAST_BLOCK, z_last[:]))
-        products = []
         for b in range(BLOCKS):
-            h_codes, h_scales = quantize_block("h%d" % b, hidden[b][:].rearrange("p v t -> p (v t)"))
-            numbers = (0, BLOCKS + b) if b == LAST_BLOCK else (BLOCKS + b,)
-            share = PACK // len(numbers)
-            banks = [bank_tile(number, [P, share, BLOCK]) for number in numbers]
-            product_planes(
-                [banks[t // share][:, t % share, :] for t in range(PACK)],
-                lambda t: w3_codes[:, t, :].bitcast(FP4X4), lambda t: w3_sc[:, t, :], h_codes, h_scales,
-            )
-            products.append(banks)
+            second_layer(b, hidden[b], w3_sc)
 
         out_rows = out_0.rearrange("(p t) v -> p t v", t=PACK)
         out_words = out_1[0].rearrange("p n r -> p (n r)").bitcast(I32)

@@ -28,11 +28,7 @@ BLOCK = 128
 BLOCKS = D // BLOCK
 LAST_BLOCK = BLOCKS - 1
 EARLY_BLOCKS = (0, 1, 2)
-LATE_BLOCKS = (LAST_BLOCK,)
 FIRST_BLOCKS = (0, 1)
-RING = 4
-PLAIN_RING = 3
-SECOND_SUMS = (4, 5, 0, 1)
 OUT_SPLIT = 48
 RUN = 8
 W1_SPLITS = (10, 6, 6, 6)
@@ -89,6 +85,8 @@ def tile_picked_hgrid_gelu_po_kernel(
         nc.gpsimd.memset(warm_in[:], 0.0)
         w3s_raw = sb("w3s_raw", [P, D], U8)
         nc.gpsimd.memset(w3s_raw[:].bitcast(I32), 0)
+        w3_sc = sb("w3_sc", [P, PACK, P], U8)
+        nc.gpsimd.memset(w3_sc[:].rearrange("p t m -> p (t m)").bitcast(I32), 0)
         xw_table = sb("xw_table", [P, TABLE], U32)
         nc.sync.dma_start(
             out=xw_table[:].bitcast(I32), in_=x_words[0].rearrange("p n r -> p (n r)").bitcast(I32)
@@ -98,6 +96,7 @@ def tile_picked_hgrid_gelu_po_kernel(
         load_scale_rows(nc.sync, xs_table, x_scales)
         w1_raw = sb("w1_raw", [P, PACK, D], F32)
         nc.sync.dma_start(out=w1_raw[:], in_=w1.rearrange("(p j) c -> p j c", j=PACK))
+        nc.sync.dma_start(out=w3s_raw[:16, :].bitcast(I32), in_=w3_scales[0].bitcast(I32))
         w3_raw = sb("w3_raw", [P, 2 * D], U8)
         lists = [sb("list%d" % c, [P, D // GROUP], U16) for c in range(CORNERS)]
         weight_pairs = [sb("weights%d" % u, [P, 2, D], F32) for u in range(2)]
@@ -112,7 +111,6 @@ def tile_picked_hgrid_gelu_po_kernel(
         nc.sync.dma_start(out=w3_raw[:].bitcast(I32), in_=w3_words[0].bitcast(I32))
         for c, a in ((1, a2), (3, a4), (2, a3)):
             load_weights(c, a)
-        load_scale_rows(nc.sync, w3s_raw, w3_scales)
         w2_raw = sb("w2_raw", [P, PACK, D], F32)
         for j in range(PACK):
             nc.sync.dma_start(
@@ -121,8 +119,8 @@ def tile_picked_hgrid_gelu_po_kernel(
         res_sb = sb("res_sb", [P, PACK, D], F32)
         nc.sync.dma_start(out=res_sb[:], in_=res.rearrange("(p t) v -> p t v", t=PACK))
 
-        y = [sb("y%d" % t, [P, 2 * D if t < 2 else D], F32) for t in range(PACK)]
-        for plane in y[:2]:
+        y = [sb("y%d" % t, [P, 2 * D], F32) for t in range(PACK)]
+        for plane in y:
             nc.vector.memset(plane[:, D:], 0.0)
 
         ident = sb("ident", [P, P], F32)
@@ -176,11 +174,17 @@ def tile_picked_hgrid_gelu_po_kernel(
         nc.vector.tensor_copy(
             out=w3_codes[:].bitcast(U16), in_=w3_raw[:].bitcast(U16).rearrange("p (m t) -> p t m", t=PACK)
         )
+        w3s_dealt = sb("w3s_dealt", [P, PACK, P], U8)
+        nc.vector.tensor_copy(out=w3s_dealt[:], in_=w3s_raw[:].rearrange("p (m t) -> p t m", t=PACK))
+        for q in range(4):
+            nc.sync.dma_start(
+                out=w3_sc[32 * q : 32 * q + 4].rearrange("p t m -> p (t m)").bitcast(I32),
+                in_=w3s_dealt[4 * q : 4 * q + 4].rearrange("p t m -> p (t m)").bitcast(I32),
+            )
 
 
-        def gather_weighted(t, c, v0, width, terms=None):
-            if terms is None:
-                terms = sb("terms%d_%d_%d" % (t, c, v0), [P, width], F32)[:]
+        def gather_weighted(t, c, v0, terms):
+            width = terms.shape[1]
             nc.vector.tensor_tensor(
                 out=terms,
                 in0=y[t][:].indirect(lists[c][:, v0 // GROUP : (v0 + width) // GROUP]),
@@ -188,102 +192,68 @@ def tile_picked_hgrid_gelu_po_kernel(
             )
             return terms
 
-        def gather_corner(out, t, c, v0):
-            width = out.shape[1]
-            nc.scalar.activation(
-                out=out, in_=y[t][:].indirect(lists[c][:, v0 // GROUP : (v0 + width) // GROUP]), func=COPY
-            )
+        def gather_plain(t, c, out):
+            nc.scalar.activation(out=out, in_=y[t][:].indirect(lists[c][:]), func=COPY)
+            return out
 
-        def gather_plain(t, v0, width, reuses=None):
-            plain = sb("plain%d_%d" % (t, v0), [P, 2, width], F32, reuses=reuses)
-            for e in range(2):
-                gather_corner(plain[:, e, :], t, 2 + e, v0)
-            return plain
-
-        def weigh_one(plain, c, v0, terms):
-            nc.vector.tensor_tensor(
-                out=terms, in0=plain, in1=weights[c][:, v0 : v0 + plain.shape[1]], op=MULT
-            )
+        def weigh(plain, weight, terms):
+            nc.vector.tensor_tensor(out=terms, in0=plain, in1=weight, op=MULT)
             return terms
 
-        def weigh(plain, t, v0, width, pieces=1, terms=None, reuses=None):
-            if terms is None:
-                terms = sb("weighed%d_%d" % (t, v0), [P, 2, width], F32, reuses=reuses)
-            for n in range(pieces):
-                e = slice(2 * n // pieces, 2 * (n + 1) // pieces)
-                nc.vector.tensor_tensor(
-                    out=terms[:, e, :], in0=plain[:, e, :], in1=weight_pairs[1][:, e, v0 : v0 + width], op=MULT
-                )
-            return [terms[:, e, :] for e in range(2)]
-
         sums = {}
-        backs = {}
-        paired = {}
-
         added = {}
+        paired = {}
+        backs = {}
 
         def add_turned(t, v0, terms):
             for n in range(terms.shape[1] // BLOCK):
                 b = v0 // BLOCK + n
                 if (b, t // 2) not in sums:
-                    sums[b, t // 2] = bank_tile(b if t < 2 else SECOND_SUMS[b], [P, 2, P])
+                    sums[b, t // 2] = bank_tile(BLOCKS * (t // 2) + b, [P, 2, P])
                 added[b, t] = added.get((b, t), 0) + 1
                 nc.tensor.matmul(
                     out=sums[b, t // 2][:, t % 2, :], lhsT=terms[:, n * BLOCK : (n + 1) * BLOCK], rhs=ident[:],
                     start=added[b, t] == 1, stop=added[b, t] == CORNERS - (b == LAST_BLOCK), is_transpose=True,
                 )
 
-        def round_sums(b, u, reuses=None):
-            pairs = sb("pairs%d_%d" % (b, u), [P, P, 2], BF16, reuses=reuses)
+        def round_sums(b, u):
+            pairs = sb("pairs%d_%d" % (b, u), [P, P, 2], BF16)
             nc.scalar.copy(out=pairs[:], in_=sums[b, u][:].rearrange("v e p -> v p e"))
             paired[b, u] = pairs
 
         def turn_back(b):
-            backs[b] = bank_tile(SECOND_SUMS[b], [P, 2, BLOCK])
+            backs[b] = bank_tile(BLOCKS + b, [P, 2, BLOCK])
             for u in range(2):
                 nc.tensor.transpose(
                     backs[b][:, u, :], paired[b, u][:].rearrange("v p e -> v (p e)").bitcast(F32), ident[:]
                 )
 
-        def copy_part(u, reuses=None):
-            part = sb("part%d" % u, [P, 2, P], F32, reuses=reuses)
+        def copy_part(u):
+            part = sb("part%d" % u, [P, 2, P], F32)
             nc.scalar.copy(out=part[:], in_=sums[LAST_BLOCK, u][:])
             paired[LAST_BLOCK, u] = part
 
         def turn_back_part():
-            backs[LAST_BLOCK] = bank_tile(SECOND_SUMS[LAST_BLOCK], [P, PACK, BLOCK])
+            backs[LAST_BLOCK] = bank_tile(BLOCKS + LAST_BLOCK, [P, PACK, BLOCK])
             for t in range(PACK):
                 nc.tensor.transpose(backs[LAST_BLOCK][:, t, :], paired[LAST_BLOCK, t // 2][:, t % 2, :], ident[:])
 
-        def z_of(b, copy, words):
-            copy(out=words.rearrange("p (v u) -> p v u", u=2), in_=backs[b][:].rearrange("p u v -> p v u"))
+        def z_of(b, words):
+            nc.scalar.copy(out=words.rearrange("p (v u) -> p v u", u=2), in_=backs[b][:].rearrange("p u v -> p v u"))
             return words.bitcast(BF16)
 
-        def quantize_block(name, grouped, reuses=None):
-            codes = sb(name + "_codes", [P, BLOCK], U32, reuses=reuses)
+        def quantize_block(name, grouped):
+            codes = sb(name + "_codes", [P, BLOCK], U32)
             scales = sb(name + "_scales", [P, BLOCK], U8)
             nc.vector.quantize_mx(out=codes[:].bitcast(FP8X4), scales=scales[:], in_=grouped)
             return codes, scales
 
-        w2_bf = sb("w2_bf", [P, PACK, P, PACK], BF16)
         w2_codes = sb("w2_codes", [P, D], U32)
         w2_scales = sb("w2_scales", [P, D], U8)
 
-        def round_w2(copy, m0, m1):
-            round_and_deal(copy, w2_bf[:, :, m0:m1, :], w2_raw[:, :, PACK * m0 : PACK * m1])
-
-        def quantize_w2():
-            nc.vector.quantize_mx(
-                out=w2_codes[:].bitcast(FP8X4), scales=w2_scales[:],
-                in_=w2_bf[:].rearrange("p t m j -> p (t m j)"),
-            )
-
-        def deal_w3_scales(w3_sc):
-            nc.vector.tensor_copy(out=w3_sc[:], in_=w3s_raw[:].rearrange("p (m t) -> p t m", t=PACK))
-
         def first_layer(b, z_bf):
             z_codes, z_scales = quantize_block("z%d" % b, z_bf)
-            pre = bank_tile(6 + b % 2, [P, PACK, BLOCK])
+            pre = bank_tile(b, [P, PACK, BLOCK])
             product_planes(
                 [pre[:, t, :] for t in range(PACK)], lambda t: w2_codes[:, P * t : P * (t + 1)].bitcast(FP8X4),
                 lambda t: w2_scales[:, P * t : P * (t + 1)], z_codes, z_scales,
@@ -294,9 +264,9 @@ def tile_picked_hgrid_gelu_po_kernel(
 
         products = {}
 
-        def second_layer(b, h_bf, w3_sc):
-            h_codes, h_scales = quantize_block("h%d" % b, h_bf[:].rearrange("p v t -> p (v t)"), "z_words2" if b == 1 else None)
-            numbers = (4, 5) if b == LAST_BLOCK else ((1, 0, 2)[b],)
+        def second_layer(b, h_bf):
+            h_codes, h_scales = quantize_block("h%d" % b, h_bf[:].rearrange("p v t -> p (v t)"))
+            numbers = (BLOCKS + b, 0) if b == LAST_BLOCK else (BLOCKS + b,)
             share = PACK // len(numbers)
             banks = [bank_tile(number, [P, share, BLOCK]) for number in numbers]
             product_planes(
@@ -305,76 +275,83 @@ def tile_picked_hgrid_gelu_po_kernel(
             )
             products[b] = banks
 
-        def add_all(t, v0, terms):
-            for one in terms:
-                add_turned(t, v0, one)
-
-        def gather_half(t, v0, room):
-            return [gather_weighted(t, c, v0, HALF, room[:, c * HALF : (c + 1) * HALF]) for c in range(2)]
+        def row(name, width=D):
+            return sb(name, [P, width], F32)[:]
 
         early = LAST_BLOCK * BLOCK
-        add_turned(0, 0, gather_weighted(0, 0, 0, early))
-        add_turned(0, 0, gather_weighted(0, 1, 0, D))
-        plain0 = gather_plain(0, 0, D)
+        add_turned(0, 0, gather_weighted(0, 0, 0, row("terms00", early)))
+        add_turned(0, 0, gather_weighted(0, 1, 0, row("terms01")))
+        plain0 = [gather_plain(0, c, row("plain0%d" % c)) for c in (2, 3)]
         make_plane(5, 2, 0, D, nc.scalar.copy)
-        make_plane(6, 3, 0, D, nc.scalar.copy)
-        ahead = gather_weighted(1, 1, 0, D)
-        w = weigh(plain0, 0, 0, D, 2)
-        add_all(0, 0, w)
+        ahead = gather_weighted(1, 1, 0, row("terms11"))
+        for c in (2, 3):
+            add_turned(0, 0, weigh(plain0[c - 2], weights[c], row("terms0%d" % c)))
         add_turned(1, 0, ahead)
-        plain1 = gather_plain(1, 0, D)
-        add_turned(1, 0, gather_weighted(1, 0, 0, early, plain0[:, 0, :early]))
-        add_all(2, 0, gather_half(2, 0, plain0[:, 1, :]))
-        add_all(1, 0, weigh(plain1, 1, 0, D))
-        plains = {(t, v0): gather_plain(t, v0, HALF) for t, v0 in ((2, 0), (3, 0), (2, HALF))}
-        single = sb("single", [P, HALF], F32)
-        gather_corner(single[:], 2, 1, HALF)
-        for b in FIRST_BLOCKS:
+        plain1 = [gather_plain(1, c, row("plain1%d" % c)) for c in (2, 3)]
+        make_plane(6, 3, 0, D, nc.scalar.copy)
+        add_turned(1, 0, gather_weighted(1, 0, 0, plain0[0][:, :early]))
+        ahead = gather_weighted(2, 0, 0, plain0[1][:, :early])
+        for c in (2, 3):
+            add_turned(1, 0, weigh(plain1[c - 2], weights[c], row("terms1%d" % c)))
+        add_turned(2, 0, ahead)
+        plain21 = gather_plain(2, 1, row("plain21"))
+        plain2 = sb("plain2", [P, 2, D], F32)
+        plain3 = sb("plain3", [P, 2 * D], F32)
+        for c in (2, 3):
+            gather_plain(2, c, plain2[:, c - 2, :])
+        for c in (2, 3):
+            gather_plain(3, c, plain3[:, (c - 2) * D : (c - 1) * D])
+        for b in EARLY_BLOCKS:
             round_sums(b, 0)
-        add_all(2, 0, weigh(plains[2, 0], 2, 0, HALF))
-        add_all(3, 0, weigh(plains[3, 0], 3, 0, HALF))
-        w = gather_half(3, 0, plain1[:, 0, :])
-        add_all(3, 0, w)
+        copy_part(0)
+        w2_bf = sb("w2_bf", [P, PACK, P, PACK], BF16, reuses="plain12")
+        round_and_deal(nc.vector.tensor_copy, w2_bf[:], w2_raw[:])
+        ahead = gather_weighted(3, 1, 0, plain1[1][:, :HALF])
+        nc.vector.quantize_mx(
+            out=w2_codes[:].bitcast(FP8X4), scales=w2_scales[:], in_=w2_bf[:].rearrange("p t m j -> p (t m j)")
+        )
+        add_turned(2, 0, weigh(plain21, weights[1], w2_raw[:, 0, :]))
+        weigh(plain2[:], weight_pairs[1][:], w2_raw[:, 1:3, :])
+        for e in range(2):
+            add_turned(2, 0, w2_raw[:, 1 + e, :])
+        add_turned(3, 0, ahead)
+        add_turned(3, 0, gather_weighted(3, 0, 0, plain21[:, :early]))
+        pair3 = plain3[:].rearrange("p (e v) -> p e v", e=2)
+        for v0 in (0, HALF):
+            cols = slice(v0, v0 + HALF)
+            weigh(pair3[:, :, cols], weight_pairs[1][:, :, cols], plain2[:, :, cols])
+            for e in range(2):
+                add_turned(3, v0, plain2[:, e, cols])
+        add_turned(3, HALF, gather_weighted(3, 1, HALF, plain3[:, :HALF]))
+        fourth = plain3[:, HALF : HALF + D]
+        z_words = [plain3[:, HALF + early : D + early]] + [row("z_words%d" % b, HALF) for b in (1, 2)]
+        z_bf = []
         for b in FIRST_BLOCKS:
             round_sums(b, 1)
             turn_back(b)
-        z_words = [sb("z_words%d" % b, [P, HALF], F32) for b in EARLY_BLOCKS]
-        z_bf = [z_of(b, nc.scalar.copy, z_words[b][:]) for b in FIRST_BLOCKS]
-        plains[3, HALF] = gather_plain(3, HALF, HALF, reuses="pairs1_1")
-        round_sums(2, 0, reuses="pairs1_0")
-        copy_part(0, reuses="pairs0_0")
-        round_w2(nc.vector.tensor_copy, 0, P)
-        add_turned(2, HALF, weigh_one(single[:], 1, HALF, plain1[:, 1, :HALF]))
-        quantize_w2()
-        room = sb("room", [P, BLOCK], F32, reuses="w2_bf")
-        add_turned(2, HALF, gather_weighted(2, 0, HALF, BLOCK, room[:]))
-        hidden = [first_layer(b, z_bf[b]) for b in FIRST_BLOCKS]
-        last = sb("last", [P, 6, HALF], F32, reuses="z_words1")
-        add_all(2, HALF, weigh(plains[2, HALF], 2, HALF, HALF, terms=last[:, 0:2, :]))
-        add_turned(3, HALF, gather_weighted(3, 0, HALF, BLOCK, last[:, 4, :BLOCK]))
-        add_all(3, HALF, weigh(plains[3, HALF], 3, HALF, HALF, terms=last[:, 2:4, :]))
-        w = gather_weighted(3, 1, HALF, HALF, last[:, 5, :])
-        add_turned(3, HALF, w)
+        for b in FIRST_BLOCKS:
+            z_bf.append(z_of(b, z_words[b]))
         round_sums(2, 1)
         turn_back(2)
         copy_part(1)
         turn_back_part()
-        z_bf.append(z_of(2, nc.scalar.copy, z_words[2][:]))
-        fourth = sb("fourth", [P, PACK * BLOCK], F32, reuses="pairs1_1")
+        z_bf.append(z_of(2, z_words[2]))
+        hidden = []
         for t in range(PACK):
-            w = gather_weighted(t, 0, early, BLOCK, fourth[:, t * BLOCK : (t + 1) * BLOCK])
-        w3_sc = sb("w3_sc", [P, PACK, P], U8, reuses="y2")
-        deal_w3_scales(w3_sc)
-        hidden.append(first_layer(2, z_bf[2]))
+            gather_weighted(t, 0, early, fourth[:, t * BLOCK : (t + 1) * BLOCK])
+            if t % 2:
+                hidden.append(first_layer(t // 2, z_bf[t // 2]))
         z_last = sb("z_last", [P, BLOCK * PACK], BF16)
         nc.vector.tensor_tensor(
             out=z_last[:].rearrange("p (c i t) -> p c t i", i=2, t=PACK),
             in0=backs[LAST_BLOCK][:].rearrange("p t (c i) -> p c t i", i=2),
-            in1=fourth[:].rearrange("p (t c i) -> p c t i", t=PACK, i=2), op=ADD,
+            in1=fourth.rearrange("p (t c i) -> p c t i", t=PACK, i=2), op=ADD,
         )
+        hidden.append(first_layer(2, z_bf[2]))
+        second_layer(0, hidden[0])
         hidden.append(first_layer(LAST_BLOCK, z_last[:]))
-        for b in range(BLOCKS):
-            second_layer(b, hidden[b], w3_sc)
+        for b in range(1, BLOCKS):
+            second_layer(b, hidden[b])
 
         out_rows = out_0.rearrange("(p t) v -> p t v", t=PACK)
         out_words = out_1[0].rearrange("p n r -> p (n r)").bitcast(I32)

@@ -66,12 +66,6 @@ def tile_picked_hgrid_gelu_po_kernel(
                     in_=rows[0, 4 * q : 4 * q + 4, :].bitcast(I32),
                 )
 
-        def round_and_deal(copy, grouped, raw):
-            copy(
-                out=grouped.rearrange("p t m j -> p m j t"),
-                in_=raw.rearrange("p j (m t) -> p m j t", t=PACK),
-            )
-
         def product_planes(planes, codes, scales, rhs_codes, rhs_scales):
             for t in range(PACK):
                 nc.tensor.matmul_mx(
@@ -99,8 +93,8 @@ def tile_picked_hgrid_gelu_po_kernel(
         nc.sync.dma_start(out=w3s_raw[:16, :].bitcast(I32), in_=w3_scales[0].bitcast(I32))
         w3_raw = sb("w3_raw", [P, 2 * D], U8)
         lists = [sb("list%d" % c, [P, D // GROUP], U16) for c in range(CORNERS)]
-        weight_pairs = [sb("weights%d" % u, [P, 2, D], F32) for u in range(2)]
-        weights = [weight_pairs[c // 2][:, c % 2, :] for c in range(CORNERS)]
+        weight_pair = sb("weight_pair", [P, 2, D], F32)
+        weights = [sb("weights%d" % c, [P, D], F32)[:] for c in range(2)] + [weight_pair[:, e, :] for e in range(2)]
 
         def load_weights(c, a):
             nc.sync.dma_start(out=weights[c], in_=a.rearrange("(p j) v -> p j v", j=PACK)[:, 0, :])
@@ -192,8 +186,9 @@ def tile_picked_hgrid_gelu_po_kernel(
             )
             return terms
 
-        def gather_plain(t, c, out):
-            nc.scalar.activation(out=out, in_=y[t][:].indirect(lists[c][:]), func=COPY)
+        def gather_plain(t, c, out, v0=0):
+            entries = lists[c][:, v0 // GROUP : (v0 + out.shape[1]) // GROUP]
+            nc.scalar.activation(out=out, in_=y[t][:].indirect(entries), func=COPY)
             return out
 
         def weigh(plain, weight, terms):
@@ -210,10 +205,11 @@ def tile_picked_hgrid_gelu_po_kernel(
                 b = v0 // BLOCK + n
                 if (b, t // 2) not in sums:
                     sums[b, t // 2] = bank_tile(BLOCKS * (t // 2) + b, [P, 2, P])
-                added[b, t] = added.get((b, t), 0) + 1
+                added[b, t // 2] = added.get((b, t // 2), 0) + 1
                 nc.tensor.matmul(
                     out=sums[b, t // 2][:, t % 2, :], lhsT=terms[:, n * BLOCK : (n + 1) * BLOCK], rhs=ident[:],
-                    start=added[b, t] == 1, stop=added[b, t] == CORNERS - (b == LAST_BLOCK), is_transpose=True,
+                    start=added[b, t // 2] == 1, stop=added[b, t // 2] == 2 * (CORNERS - (b == LAST_BLOCK)),
+                    is_transpose=True,
                 )
 
         def round_sums(b, u):
@@ -248,7 +244,6 @@ def tile_picked_hgrid_gelu_po_kernel(
             nc.vector.quantize_mx(out=codes[:].bitcast(FP8X4), scales=scales[:], in_=grouped)
             return codes, scales
 
-        w2_codes = sb("w2_codes", [P, D], U32)
         w2_scales = sb("w2_scales", [P, D], U8)
 
         def first_layer(b, z_bf):
@@ -299,55 +294,56 @@ def tile_picked_hgrid_gelu_po_kernel(
         plain3 = sb("plain3", [P, 2 * D], F32)
         for c in (2, 3):
             gather_plain(2, c, plain2[:, c - 2, :])
-        for c in (2, 3):
-            gather_plain(3, c, plain3[:, (c - 2) * D : (c - 1) * D])
+        for v0 in (0, HALF):
+            for c in (2, 3):
+                at = (c - 2) * D + v0
+                gather_plain(3, c, plain3[:, at : at + HALF], v0)
         for b in EARLY_BLOCKS:
             round_sums(b, 0)
         copy_part(0)
-        w2_bf = sb("w2_bf", [P, PACK, P, PACK], BF16, reuses="plain12")
-        round_and_deal(nc.vector.tensor_copy, w2_bf[:], w2_raw[:])
-        ahead = gather_weighted(3, 1, 0, plain1[1][:, :HALF])
-        nc.vector.quantize_mx(
-            out=w2_codes[:].bitcast(FP8X4), scales=w2_scales[:], in_=w2_bf[:].rearrange("p t m j -> p (t m j)")
-        )
-        add_turned(2, 0, weigh(plain21, weights[1], w2_raw[:, 0, :]))
-        weigh(plain2[:], weight_pairs[1][:], w2_raw[:, 1:3, :])
-        for e in range(2):
-            add_turned(2, 0, w2_raw[:, 1 + e, :])
-        add_turned(3, 0, ahead)
-        add_turned(3, 0, gather_weighted(3, 0, 0, plain21[:, :early]))
+        add_turned(3, 0, gather_weighted(3, 1, 0, plain1[0]))
+        add_turned(3, 0, gather_weighted(3, 0, 0, plain1[1][:, :early]))
+        add_turned(2, 0, weigh(plain21, weights[1], row("terms21")))
+        for c in (2, 3):
+            add_turned(2, 0, weigh(plain2[:, c - 2, :], weights[c], row("terms2%d" % c)))
+        w2_bf = [sb("w2_bf%d" % u, [P, 2, P, PACK], BF16, reuses=("plain21", "terms21")[u]) for u in range(2)]
         pair3 = plain3[:].rearrange("p (e v) -> p e v", e=2)
-        for v0 in (0, HALF):
+        for u, v0 in enumerate((0, HALF)):
+            nc.vector.tensor_copy(
+                out=w2_bf[u][:].rearrange("p t m j -> p m j t"),
+                in_=w2_raw[:].rearrange("p j (m t) -> p m j t", t=PACK)[:, :, :, 2 * u : 2 * u + 2],
+            )
             cols = slice(v0, v0 + HALF)
-            weigh(pair3[:, :, cols], weight_pairs[1][:, :, cols], plain2[:, :, cols])
+            weigh(pair3[:, :, cols], weight_pair[:, :, cols], plain2[:, :, cols])
             for e in range(2):
                 add_turned(3, v0, plain2[:, e, cols])
-        add_turned(3, HALF, gather_weighted(3, 1, HALF, plain3[:, :HALF]))
+        w2_codes = sb("w2_codes", [P, D], U32, reuses="terms23")
+        for u in range(2):
+            nc.vector.quantize_mx(
+                out=w2_codes[:, u * HALF : (u + 1) * HALF].bitcast(FP8X4),
+                scales=w2_scales[:, u * HALF : (u + 1) * HALF],
+                in_=w2_bf[u][:].rearrange("p t m j -> p (t m j)"),
+            )
         fourth = plain3[:, HALF : HALF + D]
-        z_words = [plain3[:, HALF + early : D + early]] + [row("z_words%d" % b, HALF) for b in (1, 2)]
         z_bf = []
-        for b in FIRST_BLOCKS:
+        for b in EARLY_BLOCKS:
             round_sums(b, 1)
             turn_back(b)
-        for b in FIRST_BLOCKS:
-            z_bf.append(z_of(b, z_words[b]))
-        round_sums(2, 1)
-        turn_back(2)
         copy_part(1)
         turn_back_part()
-        z_bf.append(z_of(2, z_words[2]))
+        for b in EARLY_BLOCKS:
+            z_bf.append(z_of(b, row("z_words%d" % b, HALF)))
         hidden = []
         for t in range(PACK):
             gather_weighted(t, 0, early, fourth[:, t * BLOCK : (t + 1) * BLOCK])
-            if t % 2:
-                hidden.append(first_layer(t // 2, z_bf[t // 2]))
+            if t in EARLY_BLOCKS:
+                hidden.append(first_layer(t, z_bf[t]))
         z_last = sb("z_last", [P, BLOCK * PACK], BF16)
         nc.vector.tensor_tensor(
             out=z_last[:].rearrange("p (c i t) -> p c t i", i=2, t=PACK),
             in0=backs[LAST_BLOCK][:].rearrange("p t (c i) -> p c t i", i=2),
             in1=fourth.rearrange("p (t c i) -> p c t i", t=PACK, i=2), op=ADD,
         )
-        hidden.append(first_layer(2, z_bf[2]))
         second_layer(0, hidden[0])
         hidden.append(first_layer(LAST_BLOCK, z_last[:]))
         for b in range(1, BLOCKS):

@@ -372,7 +372,7 @@ def tile_picked_hgrid_gelu_po_kernel(
                     nc.vector.tensor_tensor(
                         out=result[:, pair, :], in0=bank[:], in1=res_sb[:, pair, cols], op=ADD
                     )
-                    nc.sync.dma_start(out=out_rows[:, pair, HALF:], in_=results[1][:, pair, :])
+                    nc.sync.dma_start(out=out_rows[:, pair, cols], in_=result[:, pair, :])
                 round_and_interleave(nc.scalar.copy, o_bf, result, slice(0, OUT_SPLIT))
                 round_and_interleave(nc.vector.tensor_copy, o_bf, result, slice(OUT_SPLIT, BLOCK))
             else:
@@ -383,8 +383,7 @@ def tile_picked_hgrid_gelu_po_kernel(
                         out=result[:, :, piece], in0=products[b][0][:], in1=res_sb[:, :, points], op=ADD
                     )
                     round_and_interleave(nc.scalar.copy, o_bf, result, piece)
-                    if b in FIRST_BLOCKS:
-                        nc.sync.dma_start(out=out_rows[:, :, points], in_=result[:, :, piece])
+                    nc.sync.dma_start(out=out_rows[:, :, points], in_=result[:, :, piece])
             nc.vector.quantize_mx(
                 out=o_codes[:, cols].bitcast(FP8X4), scales=o_scales[:, cols],
                 in_=o_bf[:].rearrange("p v t -> p (v t)"),

from contextlib import ExitStack

import concourse.mybir as mybir
from concourse.masks import make_identity

F32 = mybir.dt.float32
BF16 = mybir.dt.bfloat16
I32 = mybir.dt.int32
U32 = mybir.dt.uint32
U16 = mybir.dt.uint16
U8 = mybir.dt.uint8
FP8X4 = mybir.dt.float8_e4m3fn_x4
FP4X4 = mybir.dt.float4_e2m1fn_x4
MULT = mybir.AluOpType.mult
ADD = mybir.AluOpType.add
COPY = mybir.ActivationFunctionType.Copy
GELU = mybir.ActivationFunctionType.Gelu_apprx_tanh

P = 128
PACK = 4
D = 512
HALF = D // 2
TABLE = 2048
GROUP = 16
CORNERS = 4
LEVELS = 8
BLOCK = 128
BLOCKS = D // BLOCK
LAST_BLOCK = BLOCKS - 1
EARLY_BLOCKS = (0, 1, 2)
FIRST_BLOCKS = (0, 1)
OUT_SPLIT = 48
RUN = 8
W1_SPLITS = (10, 6, 6, 6)

FLOPS = 3 * 2 * D * D * D
BYTES = (
    P * TABLE * PACK + 16 * TABLE
    + 3 * D * D * 4
    + CORNERS * LEVELS * D * 4
    + P * 2 * D + 16 * D
    + 5 * P * (D // GROUP) * 2
    + D * D * 4 + P * D * PACK + 16 * D
)


def tile_picked_hgrid_gelu_po_kernel(
    tc, x_words, x_scales, w1, a1, a2, a3, a4, w2, res, w3_words, w3_scales, offs, c1, c2, c3, c4,
    out_0, out_1, out_2,
):
    nc = tc.nc
    with ExitStack() as ctx:
        keep = ctx.enter_context(tc.tile_pool(name="keep", bufs=1))
        psum = ctx.enter_context(tc.psum_pool(name="psum", bufs=1))

        def bank_tile(number, shape):
            return psum.tile(shape, F32, name="bank%d" % number)

        def sb(name, shape, dtype, reuses=None):
            return keep.tile(shape, dtype, name=name, tag=reuses or name, align_bytes=64)

        def load_scale_rows(queue, plane, rows):
            for q in range(4):
                queue.dma_start(
                    out=plane[32 * q : 32 * q + 4, :].bitcast(I32),
                    in_=rows[0, 4 * q : 4 * q + 4, :].bitcast(I32),
                )

        def product_planes(planes, codes, scales, rhs_codes, rhs_scales):
            for t in range(PACK):
                nc.tensor.matmul_mx(
                    out=planes[t], lhsT=codes(t), lhsT_scale=scales(t),
                    rhs=rhs_codes[:].bitcast(FP8X4), rhs_scale=rhs_scales[:], start=True, stop=True,
                )

        xs_table = sb("xs_table", [P, TABLE], U8)
        nc.gpsimd.memset(xs_table[:].bitcast(I32), 0)
        warm_in = sb("warm_in", [P, 1], F32)
        nc.gpsimd.memset(warm_in[:], 0.0)
        w3s_raw = sb("w3s_raw", [P, D], U8)
        nc.gpsimd.memset(w3s_raw[:].bitcast(I32), 0)
        w3_sc = sb("w3_sc", [P, PACK, P], U8)
        nc.gpsimd.memset(w3_sc[:].rearrange("p t m -> p (t m)").bitcast(I32), 0)
        xw_table = sb("xw_table", [P, TABLE], U32)
        nc.sync.dma_start(
            out=xw_table[:].bitcast(I32), in_=x_words[0].rearrange("p n r -> p (n r)").bitcast(I32)
        )
        picked = sb("picked", [P, D // GROUP], U16)
        nc.sync.dma_start(out=picked[:], in_=offs)
        load_scale_rows(nc.sync, xs_table, x_scales)
        w1_raw = sb("w1_raw", [P, PACK, D], F32)
        nc.sync.dma_start(out=w1_raw[:], in_=w1.rearrange("(p j) c -> p j c", j=PACK))
        nc.sync.dma_start(out=w3s_raw[:16, :].bitcast(I32), in_=w3_scales[0].bitcast(I32))
        w3_raw = sb("w3_raw", [P, 2 * D], U8)
        lists = [sb("list%d" % c, [P, D // GROUP], U16) for c in range(CORNERS)]
        weight_pair = sb("weight_pair", [P, 2, D], F32)
        weights = [sb("weights%d" % c, [P, D], F32)[:] for c in range(2)] + [weight_pair[:, e, :] for e in range(2)]

        def load_weights(c, a):
            nc.sync.dma_start(out=weights[c], in_=a.rearrange("(p j) v -> p j v", j=PACK)[:, 0, :])

        for c, entries in ((2, c3), (3, c4), (0, c1), (1, c2)):
            nc.sync.dma_start(out=lists[c][:], in_=entries)
        load_weights(0, a1)
        nc.sync.dma_start(out=w3_raw[:].bitcast(I32), in_=w3_words[0].bitcast(I32))
        for c, a in ((1, a2), (3, a4), (2, a3)):
            load_weights(c, a)
        w2_raw = sb("w2_raw", [P, PACK, D], F32)
        for j in range(PACK):
            nc.sync.dma_start(
                out=w2_raw[:, j, :], in_=w2.rearrange("(q j r) c -> j q r c", j=PACK, r=RUN)[j]
            )
        res_sb = sb("res_sb", [P, PACK, D], F32)
        nc.sync.dma_start(out=res_sb[:], in_=res.rearrange("(p t) v -> p t v", t=PACK))

        y = [sb("y%d" % t, [P, 2 * D], F32) for t in range(PACK)]
        for plane in y:
            nc.vector.memset(plane[:, D:], 0.0)

        ident = sb("ident", [P, P], F32)
        make_identity(nc, ident[:])
        warm_out = sb("warm_out", [P, 1], F32)
        nc.scalar.activation(out=warm_out[:], in_=warm_in[:], func=GELU)

        xw = sb("xw", [P, D], U32)
        nc.vector.tensor_copy(out=xw[:], in_=xw_table[:].indirect(picked[:]))
        xs = sb("xs", [P, D], U8)
        nc.vector.tensor_copy(out=xs[:], in_=xs_table[:].indirect(picked[:]))
        w1_bf = [sb("w1_bf%d" % t, [P, P * PACK], BF16) for t in range(PACK)]
        w1_columns = w1_raw[:].rearrange("p j (q t r) -> p t q j r", t=PACK, r=RUN)
        w1_codes = sb("w1_codes", [P, D], U32)
        w1_scales = sb("w1_scales", [P, D], U8)

        def round_w1(t):
            grouped = w1_bf[t][:].rearrange("p (q r j) -> p q j r", r=RUN, j=PACK)
            split = W1_SPLITS[t]
            for q0, q1, copy in ((0, split, nc.vector.tensor_copy), (split, P // RUN, nc.scalar.copy)):
                copy(out=grouped[:, q0:q1, :, :], in_=w1_columns[:, t, q0:q1, :, :])

        def quantize_w1(t):
            nc.vector.quantize_mx(
                out=w1_codes[:, P * t : P * (t + 1)].bitcast(FP8X4), scales=w1_scales[:, P * t : P * (t + 1)],
                in_=w1_bf[t][:],
            )

        round_w1(0)
        for t in range(PACK):
            if t + 1 < PACK:
                round_w1(t + 1)
            quantize_w1(t)
        def make_plane(number, t, n0, step, copy):
            cols = slice(n0, n0 + step)
            bank = bank_tile(BLOCKS + number % BLOCKS, [P, step])
            nc.tensor.matmul_mx(
                out=bank[:],
                lhsT=w1_codes[:, P * t : P * (t + 1)].bitcast(FP8X4),
                lhsT_scale=w1_scales[:, P * t : P * (t + 1)],
                rhs=xw[:, cols].bitcast(FP8X4), rhs_scale=xs[:, cols],
                start=True, stop=True,
            )
            copy(out=y[t][:, cols], in_=bank[:])

        for n in range(BLOCKS):
            make_plane(n, 0, n * BLOCK, BLOCK, nc.vector.tensor_copy if n % 2 else nc.scalar.copy)
        make_plane(4, 1, 0, D, nc.scalar.copy)

        w3_codes = sb("w3_codes", [P, PACK, 2 * P], U8)
        nc.vector.tensor_copy(
            out=w3_codes[:].bitcast(U16), in_=w3_raw[:].bitcast(U16).rearrange("p (m t) -> p t m", t=PACK)
        )
        w3s_dealt = sb("w3s_dealt", [P, PACK, P], U8)
        nc.vector.tensor_copy(out=w3s_dealt[:], in_=w3s_raw[:].rearrange("p (m t) -> p t m", t=PACK))
        for q in range(4):
            nc.sync.dma_start(
                out=w3_sc[32 * q : 32 * q + 4].rearrange("p t m -> p (t m)").bitcast(I32),
                in_=w3s_dealt[4 * q : 4 * q + 4].rearrange("p t m -> p (t m)").bitcast(I32),
            )


        def gather_weighted(t, c, v0, terms):
            width = terms.shape[1]
            nc.vector.tensor_tensor(
                out=terms,
                in0=y[t][:].indirect(lists[c][:, v0 // GROUP : (v0 + width) // GROUP]),
                in1=weights[c][:, v0 : v0 + width], op=MULT,
            )
            return terms

        def gather_plain(t, c, out, v0=0):
            entries = lists[c][:, v0 // GROUP : (v0 + out.shape[1]) // GROUP]
            nc.scalar.activation(out=out, in_=y[t][:].indirect(entries), func=COPY)
            return out

        def weigh(plain, weight, terms):
            nc.vector.tensor_tensor(out=terms, in0=plain, in1=weight, op=MULT)
            return terms

        sums = {}
        added = {}
        paired = {}
        backs = {}

        def add_turned(t, v0, terms):
            for n in range(terms.shape[1] // BLOCK):
                b = v0 // BLOCK + n
                if (b, t // 2) not in sums:
                    sums[b, t // 2] = bank_tile(BLOCKS * (t // 2) + b, [P, 2, P])
                added[b, t // 2] = added.get((b, t // 2), 0) + 1
                nc.tensor.matmul(
                    out=sums[b, t // 2][:, t % 2, :], lhsT=terms[:, n * BLOCK : (n + 1) * BLOCK], rhs=ident[:],
                    start=added[b, t // 2] == 1, stop=added[b, t // 2] == 2 * (CORNERS - (b == LAST_BLOCK)),
                    is_transpose=True,
                )

        def round_sums(b, u):
            pairs = sb("pairs%d_%d" % (b, u), [P, P, 2], BF16)
            nc.scalar.copy(out=pairs[:], in_=sums[b, u][:].rearrange("v e p -> v p e"))
            paired[b, u] = pairs

        def turn_back(b):
            backs[b] = bank_tile(BLOCKS + b, [P, 2, BLOCK])
            for u in range(2):
                nc.tensor.transpose(
                    backs[b][:, u, :], paired[b, u][:].rearrange("v p e -> v (p e)").bitcast(F32), ident[:]
                )

        def copy_part(u):
            part = sb("part%d" % u, [P, 2, P], F32)
            nc.scalar.copy(out=part[:], in_=sums[LAST_BLOCK, u][:])
            paired[LAST_BLOCK, u] = part

        def turn_back_part():
            backs[LAST_BLOCK] = bank_tile(BLOCKS + LAST_BLOCK, [P, PACK, BLOCK])
            for t in range(PACK):
                nc.tensor.transpose(backs[LAST_BLOCK][:, t, :], paired[LAST_BLOCK, t // 2][:, t % 2, :], ident[:])

        def z_of(b, words):
            nc.scalar.copy(out=words.rearrange("p (v u) -> p v u", u=2), in_=backs[b][:].rearrange("p u v -> p v u"))
            return words.bitcast(BF16)

        def quantize_block(name, grouped):
            codes = sb(name + "_codes", [P, BLOCK], U32)
            scales = sb(name + "_scales", [P, BLOCK], U8)
            nc.vector.quantize_mx(out=codes[:].bitcast(FP8X4), scales=scales[:], in_=grouped)
            return codes, scales

        w2_scales = sb("w2_scales", [P, D], U8)

        def first_layer(b, z_bf):
            z_codes, z_scales = quantize_block("z%d" % b, z_bf)
            pre = bank_tile(b, [P, PACK, BLOCK])
            product_planes(
                [pre[:, t, :] for t in range(PACK)], lambda t: w2_codes[:, P * t : P * (t + 1)].bitcast(FP8X4),
                lambda t: w2_scales[:, P * t : P * (t + 1)], z_codes, z_scales,
            )
            h_bf = sb("h_bf%d" % b, [P, BLOCK, PACK], BF16)
            nc.scalar.activation(out=h_bf[:], in_=pre[:].rearrange("p t v -> p v t"), func=GELU)
            return h_bf

        products = {}

        def second_layer(b, h_bf):
            h_codes, h_scales = quantize_block("h%d" % b, h_bf[:].rearrange("p v t -> p (v t)"))
            numbers = (BLOCKS + b, 0) if b == LAST_BLOCK else (BLOCKS + b,)
            share = PACK // len(numbers)
            banks = [bank_tile(number, [P, share, BLOCK]) for number in numbers]
            product_planes(
                [banks[t // share][:, t % share, :] for t in range(PACK)],
                lambda t: w3_codes[:, t, :].bitcast(FP4X4), lambda t: w3_sc[:, t, :], h_codes, h_scales,
            )
            products[b] = banks

        def row(name, width=D):
            return sb(name, [P, width], F32)[:]

        early = LAST_BLOCK * BLOCK
        add_turned(0, 0, gather_weighted(0, 0, 0, row("terms00", early)))
        add_turned(0, 0, gather_weighted(0, 1, 0, row("terms01")))
        plain0 = [gather_plain(0, c, row("plain0%d" % c)) for c in (2, 3)]
        make_plane(5, 2, 0, D, nc.scalar.copy)
        ahead = gather_weighted(1, 1, 0, row("terms11"))
        for c in (2, 3):
            add_turned(0, 0, weigh(plain0[c - 2], weights[c], row("terms0%d" % c)))
        add_turned(1, 0, ahead)
        plain1 = [gather_plain(1, c, row("plain1%d" % c)) for c in (2, 3)]
        make_plane(6, 3, 0, D, nc.scalar.copy)
        add_turned(1, 0, gather_weighted(1, 0, 0, plain0[0][:, :early]))
        ahead = gather_weighted(2, 0, 0, plain0[1][:, :early])
        for c in (2, 3):
            add_turned(1, 0, weigh(plain1[c - 2], weights[c], row("terms1%d" % c)))
        add_turned(2, 0, ahead)
        plain21 = gather_plain(2, 1, row("plain21"))
        plain2 = sb("plain2", [P, 2, D], F32)
        plain3 = sb("plain3", [P, 2 * D], F32)
        for c in (2, 3):
            gather_plain(2, c, plain2[:, c - 2, :])
        for v0 in (0, HALF):
            for c in (2, 3):
                at = (c - 2) * D + v0
                gather_plain(3, c, plain3[:, at : at + HALF], v0)
        for b in EARLY_BLOCKS:
            round_sums(b, 0)
        copy_part(0)
        add_turned(3, 0, gather_weighted(3, 1, 0, plain1[0]))
        add_turned(3, 0, gather_weighted(3, 0, 0, plain1[1][:, :early]))
        add_turned(2, 0, weigh(plain21, weights[1], row("terms21")))
        for c in (2, 3):
            add_turned(2, 0, weigh(plain2[:, c - 2, :], weights[c], row("terms2%d" % c)))
        w2_bf = [sb("w2_bf%d" % u, [P, 2, P, PACK], BF16, reuses=("plain21", "terms21")[u]) for u in range(2)]
        pair3 = plain3[:].rearrange("p (e v) -> p e v", e=2)
        for u, v0 in enumerate((0, HALF)):
            nc.vector.tensor_copy(
                out=w2_bf[u][:].rearrange("p t m j -> p m j t"),
                in_=w2_raw[:].rearrange("p j (m t) -> p m j t", t=PACK)[:, :, :, 2 * u : 2 * u + 2],
            )
            cols = slice(v0, v0 + HALF)
            weigh(pair3[:, :, cols], weight_pair[:, :, cols], plain2[:, :, cols])
            for e in range(2):
                add_turned(3, v0, plain2[:, e, cols])
        w2_codes = sb("w2_codes", [P, D], U32, reuses="terms23")
        for u in range(2):
            nc.vector.quantize_mx(
                out=w2_codes[:, u * HALF : (u + 1) * HALF].bitcast(FP8X4),
                scales=w2_scales[:, u * HALF : (u + 1) * HALF],
                in_=w2_bf[u][:].rearrange("p t m j -> p (t m j)"),
            )
        fourth = plain3[:, HALF : HALF + D]
        z_bf = []
        for b in EARLY_BLOCKS:
            round_sums(b, 1)
            turn_back(b)
        copy_part(1)
        turn_back_part()
        for b in EARLY_BLOCKS:
            z_bf.append(z_of(b, row("z_words%d" % b, HALF)))
        hidden = []
        for t in range(PACK):
            gather_weighted(t, 0, early, fourth[:, t * BLOCK : (t + 1) * BLOCK])
            if t in EARLY_BLOCKS:
                hidden.append(first_layer(t, z_bf[t]))
        z_last = sb("z_last", [P, BLOCK * PACK], BF16)
        nc.vector.tensor_tensor(
            out=z_last[:].rearrange("p (c i t) -> p c t i", i=2, t=PACK),
            in0=backs[LAST_BLOCK][:].rearrange("p t (c i) -> p c t i", i=2),
            in1=fourth.rearrange("p (t c i) -> p c t i", t=PACK, i=2), op=ADD,
        )
        second_layer(0, hidden[0])
        hidden.append(first_layer(LAST_BLOCK, z_last[:]))
        for b in range(1, BLOCKS):
            second_layer(b, hidden[b])

        out_rows = out_0.rearrange("(p t) v -> p t v", t=PACK)
        out_words = out_1[0].rearrange("p n r -> p (n r)").bitcast(I32)
        o_codes = sb("o_codes", [P, D], U32)
        o_scales = sb("o_scales", [P, D], U8)

        def round_and_interleave(copy, o_bf, result, piece):
            copy(
                out=o_bf[:, piece, :].rearrange("p (c i) t -> p c t i", i=4),
                in_=result[:, :, piece].rearrange("p t (c i) -> p c t i", i=4),
            )

        results = [sb("result%d" % h, [P, PACK, HALF], F32) for h in range(2)]
        for chunk in (FIRST_BLOCKS, (2,), (LAST_BLOCK,)):
            v0, width = chunk[0] * BLOCK, len(chunk) * BLOCK
            cols = slice(v0, v0 + width)
            result = results[v0 // HALF][:, :, v0 % HALF : v0 % HALF + width]
            o_bf = sb("o_bf%d" % chunk[0], [P, width, PACK], BF16)
            if chunk[0] == LAST_BLOCK:
                for u, bank in enumerate(products[LAST_BLOCK]):
                    pair = slice(2 * u, 2 * u + 2)
                    nc.vector.tensor_tensor(
                        out=result[:, pair, :], in0=bank[:], in1=res_sb[:, pair, cols], op=ADD
                    )
                    nc.sync.dma_start(out=out_rows[:, pair, cols], in_=result[:, pair, :])
                round_and_interleave(nc.scalar.copy, o_bf, result, slice(0, OUT_SPLIT))
                round_and_interleave(nc.vector.tensor_copy, o_bf, result, slice(OUT_SPLIT, BLOCK))
            else:
                for n, b in enumerate(chunk):
                    piece = slice(n * BLOCK, (n + 1) * BLOCK)
                    points = slice(b * BLOCK, (b + 1) * BLOCK)
                    nc.vector.tensor_tensor(
                        out=result[:, :, piece], in0=products[b][0][:], in1=res_sb[:, :, points], op=ADD
                    )
                    round_and_interleave(nc.scalar.copy, o_bf, result, piece)
                    nc.sync.dma_start(out=out_rows[:, :, points], in_=result[:, :, piece])
            nc.vector.quantize_mx(
                out=o_codes[:, cols].bitcast(FP8X4), scales=o_scales[:, cols],
                in_=o_bf[:].rearrange("p v t -> p (v t)"),
            )
        for cols in (slice(0, LAST_BLOCK * BLOCK), slice(LAST_BLOCK * BLOCK, D)):
            nc.sync.dma_start(out=out_words[:, cols], in_=o_codes[:, cols].bitcast(I32))
        for q in range(4):
            queue = nc.scalar if q % 2 else nc.sync
            queue.dma_start(
                out=out_2[0, 4 * q : 4 * q + 4, :].bitcast(I32),
                in_=o_scales[32 * q : 32 * q + 4, :].bitcast(I32),
            )
